import numpy as np
import ml_dtypes


def mxq(x, axis, fmt="e4m3"):
    dtype, down = {"e4m3": (ml_dtypes.float8_e4m3fn, 7), "e5m2": (ml_dtypes.float8_e5m2, 14)}[fmt]
    v = np.moveaxis(np.asarray(x, np.float32).astype(ml_dtypes.bfloat16).astype(np.float64), axis, -1)
    blocks = v.reshape(v.shape[:-1] + (-1, 32))
    amax = np.abs(blocks).max(-1, keepdims=True)
    byte = np.maximum(np.where(amax > 0, np.frexp(amax)[1] - 1 + 127, 0) - down, 1)
    scale = np.exp2(byte - 127.0)
    codes = (blocks / scale).astype(np.float32).astype(dtype).astype(np.float64)
    return np.moveaxis((codes * scale).reshape(v.shape), -1, axis)


WIDE = False


def mx_kscale(k):
    if not WIDE:
        return np.ones(k)
    levels = np.array([10, -10, 5, -5, 0])
    if k % 512:
        return np.exp2(np.random.permutation(np.resize(levels, k // 32))).repeat(32)
    a = np.empty((k // 512, 16))
    for p in range(k // 512):
        a[p, :8] = np.random.permutation(np.resize(levels, 8))
        for g in range(8):
            far = levels[np.abs(levels - a[p, g]) >= 10]
            a[p, g + 8] = far[np.random.randint(len(far))]
    return np.exp2(a.ravel()).repeat(32)


def f64(x):
    return np.asarray(x).astype(np.float64)


def striped(idx):
    return np.tile(idx.reshape(-1, 16).T, (8, 1)).astype(np.uint16)


def unstriped(offs):
    return offs[:16].T.reshape(-1).astype(np.int64)


E2M1 = np.array([0.0, 0.5, 1.0, 1.5, 2.0, 3.0, 4.0, 6.0, -0.0, -0.5, -1.0, -1.5, -2.0, -3.0, -4.0, -6.0])


def pack_weight(w, fmt):
    k, n = w.shape
    w = f64(np.asarray(w, np.float32).astype(ml_dtypes.bfloat16)).reshape(k // 32, 32, n)
    amax = np.abs(w).max(1)
    if fmt == "e4m3":
        byte = np.frexp(amax)[1] - 1 + 127 - 7
    else:
        mant, ex = np.frexp(amax / 6.0)
        byte = np.where(mant > 0.5, ex, ex - 1) + 127
    byte = np.clip(np.where(amax > 0, byte, 1), 1, 254)
    scaled = (w * np.exp2(127.0 - byte)[:, None, :]).reshape(k, n).astype(np.float32)
    by_word = np.ascontiguousarray(scaled.reshape(k // 512, 128, 4, n).transpose(0, 1, 3, 2))
    if fmt == "e4m3":
        words = by_word.astype(ml_dtypes.float8_e4m3fn).view(np.uint8)
    else:
        c = by_word.astype(ml_dtypes.float4_e2m1fn).view(np.uint8) & 0xF
        words = (c[..., 0::2] | (c[..., 1::2] << 4)).reshape(k // 512, 128, 2 * n)
    return np.ascontiguousarray(words), np.ascontiguousarray(byte.astype(np.uint8).reshape(k // 512, 16, n))


def unpack_weight(words, scales, fmt):
    g, _, n = scales.shape
    words = np.ascontiguousarray(words).reshape(g, 128, n, -1)
    if fmt == "e4m3":
        vals = words.view(ml_dtypes.float8_e4m3fn).astype(np.float64)
    else:
        nib = np.empty((g, 128, n, 4), np.uint8)
        nib[..., 0::2] = words & 0xF
        nib[..., 1::2] = words >> 4
        vals = E2M1[nib]
    vals = vals * np.repeat(np.exp2(scales.astype(np.float64) - 127.0), 8, axis=1)[..., None]
    return vals.transpose(0, 1, 3, 2).reshape(g * 512, n)


def gelu(v):
    return 0.5 * v * (1.0 + np.tanh(np.sqrt(2.0 / np.pi) * (v + 0.044715 * v**3)))


K, T, S, P, H, N = 1024, 4096, 1024, 512, 1024, 1024

def setup_inputs():
    n = np.random.standard_normal
    s = mx_kscale(K)[:, None]
    u = mx_kscale(H)[:, None]
    w = mx_kscale(N)[:, None]
    tab_words, tab_scales = pack_weight(n((K, T)) * s, "e4m3")
    w1_words, w1_scales = pack_weight(n((K, H)) / np.sqrt(K) / s * u.T, "e2m1")
    w2 = (n((H, N)) / np.sqrt(H) / u).astype(np.float32)
    w3_words, w3_scales = pack_weight(n((N, N)) / np.sqrt(N) / w, "e4m3")
    gain = (np.exp(0.3 * n(N)) * w[:, 0]).astype(np.float32)
    return {
        "tab_words": tab_words, "tab_scales": tab_scales,
        "offs": striped(np.random.permutation(T)[:S]),
        "pos1": striped(np.random.permutation(S)[:P]),
        "pos2": striped(np.random.permutation(S)[:P]),
        "pos3": striped(np.random.permutation(S)[:P]),
        "w1_words": w1_words, "w1_scales": w1_scales,
        "w2": w2,
        "w3_words": w3_words, "w3_scales": w3_scales,
        "gain": gain,
    }

def reference(tab_words, tab_scales, offs, pos1, pos2, pos3, w1_words, w1_scales, w2, w3_words, w3_scales, gain):
    v = unpack_weight(tab_words, tab_scales, "e4m3")[:, unstriped(offs)]
    h = unpack_weight(w1_words, w1_scales, "e2m1").T @ v
    belly = h[:, unstriped(pos1)]
    short = h[:, unstriped(pos2)]
    long = h[:, unstriped(pos3)]
    z = np.abs(belly) - 0.5 * (short + long)
    y = mxq(f64(w2), 0, "e4m3").T @ mxq(z, 0, "e4m3")
    act = f64(gain)[:, None] * np.tanh(y)
    return unpack_weight(w3_words, w3_scales, "e4m3").T @ mxq(act, 0, "e4m3") + y

@@ -1,0 +1,289 @@
+from contextlib import ExitStack
+
+import concourse.mybir as mybir
+
+K, T, S, M, H, N = 1024, 4096, 1024, 512, 1024, 1024
+FLOPS = 2 * K * H * S + 2 * H * N * M + 2 * N * N * M
+
+F32 = mybir.dt.float32
+BF16 = mybir.dt.bfloat16
+I32 = mybir.dt.int32
+U32 = mybir.dt.uint32
+U16 = mybir.dt.uint16
+U8 = mybir.dt.uint8
+FP8X4 = mybir.dt.float8_e4m3fn_x4
+FP4X4 = mybir.dt.float4_e2m1fn_x4
+ALU = mybir.AluOpType
+ACT = mybir.ActivationFunctionType
+
+P = 128
+BANK = 512
+SUB = 128
+CHUNKS = [(0, 256), (256, 128), (384, 128)]
+
+
+def tile_list_muni_butterfly_residual_kernel(
+    tc, tab_words, tab_scales, offs, pos1, pos2, pos3, w1_words, w1_scales, w2, w3_words, w3_scales, gain, out
+):
+    nc = tc.nc
+    with ExitStack() as ctx:
+        keep = ctx.enter_context(tc.tile_pool(name="keep", bufs=1))
+        ring = ctx.enter_context(tc.tile_pool(name="ring", bufs=2))
+        psum = ctx.enter_context(tc.psum_pool(name="psum", bufs=8))
+
+        def kept(name, shape, dtype):
+            return keep.tile(shape, dtype, name=name, align_bytes=64)
+
+        offs_sb = kept("offs_sb", [P, S // 16], U16)
+        pos_sb = [kept("pos_sb%d" % i, [P, M // 16], U16) for i in range(3)]
+        tab_sb = [kept("big%d" % a, [P, T], I32) for a in range(2)]
+        tab_sc = kept("tab_sc", [P, T], U8)
+        w1_raw = kept("w1_raw", [P, 2, H // 2], I32)
+        w_sc_raw = kept("w_sc_raw", [P, 2, N], U8)
+        gain_sb = kept("gain_sb", [P, 2, 4], F32)
+        planes = [kept("planes%d" % a, [P, 3, 1024], U8) for a in range(2)]
+
+        for rows in (slice(32, 64), slice(64, P)):
+            nc.vector.memset(tab_sc[rows].bitcast(I32), 0)
+            nc.gpsimd.memset(w_sc_raw[rows].bitcast(I32), 0)
+        nc.gpsimd.memset(planes[1][:].bitcast(I32), 0)
+
+        nc.sync.dma_start(offs_sb[:], offs)
+        nc.sync.dma_start(tab_sc[0:32].bitcast(I32), tab_scales.rearrange("a q t -> (a q) t").bitcast(I32))
+        nc.sync.dma_start(w_sc_raw[0:32, 0].bitcast(I32), w1_scales.rearrange("a q c -> (a q) c").bitcast(I32))
+        nc.sync.dma_start(w_sc_raw[0:32, 1].bitcast(I32), w3_scales.rearrange("a q c -> (a q) c").bitcast(I32))
+        nc.sync.dma_start(w1_raw[:], w1_words.rearrange("a p c -> p a c").bitcast(I32))
+        nc.sync.dma_start(tab_sb[0][:], tab_words[0].rearrange("p t i -> p (t i)").bitcast(I32))
+        for tile, lst in zip(pos_sb, (pos1, pos2, pos3)):
+            nc.sync.dma_start(tile[:], lst)
+        nc.sync.dma_start(gain_sb[:], gain.rearrange("(b p t) -> p b t", b=2, t=4))
+        nc.sync.dma_start(tab_sb[1][:], tab_words[1].rearrange("p t i -> p (t i)").bitcast(I32))
+
+        v_sc = kept("v_sc", [P, S], U8)
+        v_codes = [kept("v_codes%d" % a, [P, S], U32) for a in range(2)]
+        nc.vector.tensor_copy(v_sc[:], tab_sc[:].indirect(offs_sb[:]))
+        nc.vector.tensor_copy(
+            planes[0][:, 1].bitcast(I32).rearrange("p (b t q w) -> p b q t w", b=2, t=4, w=2),
+            w_sc_raw[:, 0].bitcast(I32).rearrange("p (b q t w) -> p b q t w", b=2, t=4, w=2),
+        )
+        nc.vector.tensor_copy(
+            planes[0][:, 2].rearrange("p (b t g m) -> p b g t m", b=2, t=4, m=16),
+            w_sc_raw[:, 1].rearrange("p (b g m t) -> p b g t m", b=2, t=4, m=16),
+        )
+        nc.vector.tensor_copy(planes[0][:, 0].bitcast(I32), v_sc[:].bitcast(I32))
+        for a in range(2):
+            for q in range(4):
+                row = 16 * a + 4 * q
+                if row:
+                    nc.scalar.dma_start(
+                        planes[a][32 * q : 32 * q + 4].bitcast(I32), planes[0][row : row + 4].bitcast(I32)
+                    )
+        w1_codes = kept("w1_codes", [P, 2, H // 2], I32)
+        nc.vector.tensor_copy(
+            w1_codes[:].rearrange("p a (b t q w) -> p (a b) q t w", b=2, t=4, w=4),
+            w1_raw[:].rearrange("p a (b q t w) -> p (a b) q t w", b=2, t=4, w=4),
+        )
+        w3_raw = kept("w1_raw", [P, 2, N], I32)
+        nc.sync.dma_start(w3_raw[:], w3_words.rearrange("a p c i -> p a (c i)").bitcast(I32))
+
+        nc.vector.tensor_copy(v_codes[0][:], tab_sb[0][:].bitcast(U32).indirect(offs_sb[:]))
+        for half in range(2):
+            nc.vector.tensor_copy(
+                v_codes[1][:, BANK * half : BANK * (half + 1)],
+                tab_sb[1][:].bitcast(U32).indirect(offs_sb[:, 32 * half : 32 * (half + 1)]),
+            )
+
+        w2_raw = [kept("big%d" % a, [P, 4, N], F32) for a in range(2)]
+        for a in range(2):
+            rows = w2[512 * a : 512 * a + 512, :].rearrange("(q j i) n -> j q i n", j=4, i=8)
+            for j in range(4):
+                nc.sync.dma_start(w2_raw[a][:, j, :], rows[j])
+
+        w3_codes = []
+
+        def order_w3():
+            w3_codes.append(kept("w1_codes", [P, 2, N], I32))
+            nc.vector.tensor_copy(
+                w3_codes[0][:].rearrange("p a (b t g m) -> p (a b) g t m", b=2, t=4, m=4),
+                w3_raw[:].rearrange("p a (b g m t) -> p (a b) g t m", b=2, t=4, m=4),
+            )
+
+        h_sb = [kept("h_sb%d" % i, [P, S], F32) for i in range(8)]
+
+        def first_product(i):
+            cols = slice(P * i, P * (i + 1))
+            for half in range(2):
+                quotes = slice(BANK * half, BANK * (half + 1))
+                bank = psum.tile([P, BANK], F32, name="bank")
+                for a in range(2):
+                    nc.tensor.matmul_mx(
+                        out=bank[:],
+                        lhsT=w1_codes[:, a, cols.start // 2 : cols.stop // 2].bitcast(U8).bitcast(FP4X4),
+                        lhsT_scale=planes[a][:, 1, cols],
+                        rhs=v_codes[a][:, quotes].bitcast(FP8X4),
+                        rhs_scale=planes[a][:, 0, quotes],
+                        start=(a == 0),
+                        stop=(a == 1),
+                    )
+                nc.scalar.copy(h_sb[i][:, quotes], bank[:])
+
+        w2_codes = [kept("w2_codes%d" % a, [P, N], U32) for a in range(2)]
+        w2_sc = [kept("w2_sc%d" % a, [P, N], U8) for a in range(2)]
+        w2_grouped = {}
+
+        def round_w2(piece):
+            a, b, part = piece // 4, piece // 2 % 2, piece % 2
+            if part == 0:
+                w2_grouped[a, b] = ring.tile([P, 2048], BF16, name="w2_grouped", align_bytes=64)
+            dst = w2_grouped[a, b][:].rearrange("p (t m j) -> p m t j", t=4, j=4)
+            src = w2_raw[a][:, :, 512 * b : 512 * (b + 1)].rearrange("p j (m t) -> p m t j", t=4)
+            ms = slice(64 * part, 64 * (part + 1))
+            nc.scalar.copy(dst[:, ms], src[:, ms])
+            if part == 1:
+                cols = slice(512 * b, 512 * (b + 1))
+                nc.vector.quantize_mx(
+                    out=w2_codes[a][:, cols].bitcast(FP8X4), scales=w2_sc[a][:, cols], in_=w2_grouped[a, b][:]
+                )
+
+        z_codes = [kept("z_codes%d" % a, [P, M], U32) for a in range(2)]
+        z_sc = [kept("z_sc%d" % a, [P, M], U8) for a in range(2)]
+
+        steps = [(c, i) for c in range(len(CHUNKS)) for i in range(8)]
+        belly = {}
+        short = {}
+        wings = {}
+        z_bf = {}
+
+        def picks(c, k):
+            m0, width = CHUNKS[c]
+            return pos_sb[k][:, m0 // 16 : (m0 + width) // 16]
+
+        def gather_belly(c, i):
+            width = CHUNKS[c][1]
+            raw = ring.tile([P, width], F32, name="belly_raw", bufs=3)
+            nc.vector.tensor_copy(raw[:], h_sb[i][:].indirect(picks(c, 0)))
+            belly[c, i] = ring.tile([P, width], F32, name="belly_abs", bufs=3)
+            nc.scalar.activation(belly[c, i][:], raw[:], ACT.Abs, scale=2.0)
+
+        def gather_short(c, i):
+            width = CHUNKS[c][1]
+            short[c, i] = ring.tile([P, width], F32, name="short", bufs=3)
+            nc.vector.tensor_tensor(short[c, i][:], h_sb[i][:].indirect(picks(c, 1)), belly[c, i][:], ALU.subtract)
+
+        def gather_long(c, i):
+            width = CHUNKS[c][1]
+            a, t = divmod(i, 4)
+            if t == 0:
+                wings[c, a] = ring.tile([P, 4, width], F32, name="wings")
+            nc.vector.tensor_tensor(wings[c, a][:, t, :], h_sb[i][:].indirect(picks(c, 2)), short[c, i][:], ALU.add)
+            if t == 3:
+                z_bf[c, a] = ring.tile([P, width, 4], BF16, name="z_bf", align_bytes=64)
+                nc.scalar.activation(z_bf[c, a][:], wings[c, a][:].rearrange("p t m -> p m t"), ACT.Copy, scale=-0.5)
+
+        def quantise_z(c, a):
+            m0, width = CHUNKS[c]
+            cols = slice(m0, m0 + width)
+            nc.vector.quantize_mx(
+                out=z_codes[a][:, cols].bitcast(FP8X4),
+                scales=z_sc[a][:, cols],
+                in_=z_bf[c, a][:].rearrange("p m t -> p (m t)"),
+            )
+
+        def product(bank, w_codes, w_sc, b, x_codes, x_sc):
+            for t in range(4):
+                cols = slice(512 * b + P * t, 512 * b + P * (t + 1))
+                for a in range(2):
+                    nc.tensor.matmul_mx(
+                        out=bank[:, t, :],
+                        lhsT=w_codes(a, cols).bitcast(FP8X4),
+                        lhsT_scale=w_sc(a, cols),
+                        rhs=x_codes[a].bitcast(FP8X4),
+                        rhs_scale=x_sc[a],
+                        start=(a == 0),
+                        stop=(a == 1),
+                    )
+
+        y_sb = {}
+        th = {}
+        act_codes = {}
+        act_sc = {}
+
+        def second_product(u):
+            trades = slice(SUB * u, SUB * (u + 1))
+            for b in range(2):
+                bank = psum.tile([P, 4, SUB], F32, name="bank")
+                product(
+                    bank,
+                    lambda a, cols: w2_codes[a][:, cols],
+                    lambda a, cols: w2_sc[a][:, cols],
+                    b,
+                    [z_codes[a][:, trades] for a in range(2)],
+                    [z_sc[a][:, trades] for a in range(2)],
+                )
+                th[u, b] = ring.tile([P, SUB, 4], F32, name="th")
+                nc.scalar.activation(th[u, b][:], bank[:].rearrange("p t m -> p m t"), ACT.Tanh)
+                y_sb[u, b] = ring.tile([P, 4, SUB], F32, name="y_b", bufs=4)
+                nc.scalar.copy(y_sb[u, b][:], bank[:])
+
+        def quantise_act(u):
+            act_bf = []
+            for b in range(2):
+                act_bf.append(ring.tile([P, SUB, 4], BF16, name="act_bf", align_bytes=64))
+                nc.vector.tensor_tensor(
+                    act_bf[b][:], th[u, b][:], gain_sb[:, b, :].unsqueeze(1).to_broadcast([P, SUB, 4]), ALU.mult
+                )
+            for b in range(2):
+                act_codes[u, b] = ring.tile([P, SUB], U32, name="act_codes", bufs=4, align_bytes=64)
+                act_sc[u, b] = ring.tile([P, SUB], U8, name="act_sc", bufs=4, align_bytes=64)
+                nc.vector.quantize_mx(
+                    out=act_codes[u, b][:].bitcast(FP8X4),
+                    scales=act_sc[u, b][:],
+                    in_=act_bf[b][:].rearrange("p m t -> p (m t)"),
+                )
+
+        def third_product(u):
+            for b in range(2):
+                bank = psum.tile([P, 4, SUB], F32, name="bank")
+                product(
+                    bank,
+                    lambda a, cols: w3_codes[0][:, a, cols],
+                    lambda a, cols: planes[a][:, 2, cols],
+                    b,
+                    [act_codes[u, a][:] for a in range(2)],
+                    [act_sc[u, a][:] for a in range(2)],
+                )
+                result = ring.tile([P, 4, SUB], F32, name="result", bufs=4)
+                nc.vector.tensor_tensor(result[:], bank[:], y_sb[u, b][:], ALU.add)
+                nc.sync.dma_start(
+                    out[512 * b : 512 * (b + 1), SUB * u : SUB * (u + 1)].rearrange("(p t) m -> p t m", t=4), result[:]
+                )
+
+        extra = {}
+
+        def at(n, work):
+            extra.setdefault(n, []).append(work)
+
+        for piece, n in enumerate((2, 3, 5, 6, 8, 9, 10, 11)):
+            at(n, lambda piece=piece: round_w2(piece))
+        at(8, order_w3)
+        for c in range(len(CHUNKS)):
+            for a in range(2):
+                at(8 * c + 4 * a + 6, lambda c=c, a=a: quantise_z(c, a))
+        for u, n in enumerate((13, 16, 19, 26)):
+            at(n, lambda u=u: second_product(u))
+            at(n + 1, lambda u=u: quantise_act(u))
+            at(n + 2, lambda u=u: third_product(u))
+
+        first_product(0)
+
+        for n in range(len(steps) + 5):
+            if n + 1 < 8:
+                first_product(n + 1)
+            if n < len(steps):
+                gather_belly(*steps[n])
+            if 1 <= n <= len(steps):
+                gather_short(*steps[n - 1])
+            if 2 <= n <= len(steps) + 1:
+                gather_long(*steps[n - 2])
+            for work in extra.get(n, []):
+                work()

@@ -29,7 +29,7 @@ def tile_list_muni_butterfly_residual_kernel(
     with ExitStack() as ctx:
         keep = ctx.enter_context(tc.tile_pool(name="keep", bufs=1))
         ring = ctx.enter_context(tc.tile_pool(name="ring", bufs=2))
-        psum = ctx.enter_context(tc.psum_pool(name="psum", bufs=8))
+        psum = ctx.enter_context(tc.psum_pool(name="psum", bufs=4))
 
         def kept(name, shape, dtype):
             return keep.tile(shape, dtype, name=name, align_bytes=64)
@@ -54,10 +54,10 @@ def tile_list_muni_butterfly_residual_kernel(
         nc.sync.dma_start(w_sc_raw[0:32, 1].bitcast(I32), w3_scales.rearrange("a q c -> (a q) c").bitcast(I32))
         nc.sync.dma_start(w1_raw[:], w1_words.rearrange("a p c -> p a c").bitcast(I32))
         nc.sync.dma_start(tab_sb[0][:], tab_words[0].rearrange("p t i -> p (t i)").bitcast(I32))
+        nc.sync.dma_start(tab_sb[1][:], tab_words[1].rearrange("p t i -> p (t i)").bitcast(I32))
         for tile, lst in zip(pos_sb, (pos1, pos2, pos3)):
             nc.sync.dma_start(tile[:], lst)
         nc.sync.dma_start(gain_sb[:], gain.rearrange("(b p t) -> p b t", b=2, t=4))
-        nc.sync.dma_start(tab_sb[1][:], tab_words[1].rearrange("p t i -> p (t i)").bitcast(I32))
 
         v_sc = kept("v_sc", [P, S], U8)
         v_codes = [kept("v_codes%d" % a, [P, S], U32) for a in range(2)]
@@ -75,7 +75,8 @@ def tile_list_muni_butterfly_residual_kernel(
             for q in range(4):
                 row = 16 * a + 4 * q
                 if row:
-                    nc.scalar.dma_start(
+                    queue = nc.gpsimd if row == 28 else nc.scalar
+                    queue.dma_start(
                         planes[a][32 * q : 32 * q + 4].bitcast(I32), planes[0][row : row + 4].bitcast(I32)
                     )
         w1_codes = kept("w1_codes", [P, 2, H // 2], I32)
@@ -99,12 +100,11 @@ def tile_list_muni_butterfly_residual_kernel(
             for j in range(4):
                 nc.sync.dma_start(w2_raw[a][:, j, :], rows[j])
 
-        w3_codes = []
+        w3_codes = kept("w3_codes", [P, 2, N], I32)
 
         def order_w3():
-            w3_codes.append(kept("w1_codes", [P, 2, N], I32))
             nc.vector.tensor_copy(
-                w3_codes[0][:].rearrange("p a (b t g m) -> p (a b) g t m", b=2, t=4, m=4),
+                w3_codes[:].rearrange("p a (b t g m) -> p (a b) g t m", b=2, t=4, m=4),
                 w3_raw[:].rearrange("p a (b g m t) -> p (a b) g t m", b=2, t=4, m=4),
             )
 
@@ -114,7 +114,7 @@ def tile_list_muni_butterfly_residual_kernel(
             cols = slice(P * i, P * (i + 1))
             for half in range(2):
                 quotes = slice(BANK * half, BANK * (half + 1))
-                bank = psum.tile([P, BANK], F32, name="bank")
+                bank = psum.tile([P, BANK], F32, name="bank_a")
                 for a in range(2):
                     nc.tensor.matmul_mx(
                         out=bank[:],
@@ -125,7 +125,10 @@ def tile_list_muni_butterfly_residual_kernel(
                         start=(a == 0),
                         stop=(a == 1),
                     )
-                nc.scalar.copy(h_sb[i][:, quotes], bank[:])
+                if i < 2 and half == 1:
+                    nc.vector.tensor_copy(h_sb[i][:, quotes], bank[:])
+                else:
+                    nc.scalar.copy(h_sb[i][:, quotes], bank[:])
 
         w2_codes = [kept("w2_codes%d" % a, [P, N], U32) for a in range(2)]
         w2_sc = [kept("w2_sc%d" % a, [P, N], U8) for a in range(2)]
@@ -135,8 +138,8 @@ def tile_list_muni_butterfly_residual_kernel(
             a, b, part = piece // 4, piece // 2 % 2, piece % 2
             if part == 0:
                 w2_grouped[a, b] = ring.tile([P, 2048], BF16, name="w2_grouped", align_bytes=64)
-            dst = w2_grouped[a, b][:].rearrange("p (t m j) -> p m t j", t=4, j=4)
-            src = w2_raw[a][:, :, 512 * b : 512 * (b + 1)].rearrange("p j (m t) -> p m t j", t=4)
+            dst = w2_grouped[a, b][:].rearrange("p (t m j) -> p m j t", t=4, j=4)
+            src = w2_raw[a][:, :, 512 * b : 512 * (b + 1)].rearrange("p j (m t) -> p m j t", t=4)
             ms = slice(64 * part, 64 * (part + 1))
             nc.scalar.copy(dst[:, ms], src[:, ms])
             if part == 1:
@@ -148,9 +151,8 @@ def tile_list_muni_butterfly_residual_kernel(
         z_codes = [kept("z_codes%d" % a, [P, M], U32) for a in range(2)]
         z_sc = [kept("z_sc%d" % a, [P, M], U8) for a in range(2)]
 
-        steps = [(c, i) for c in range(len(CHUNKS)) for i in range(8)]
+        steps = [(c, pair) for c in range(len(CHUNKS)) for pair in range(4)]
         belly = {}
-        short = {}
         wings = {}
         z_bf = {}
 
@@ -158,27 +160,36 @@ def tile_list_muni_butterfly_residual_kernel(
             m0, width = CHUNKS[c]
             return pos_sb[k][:, m0 // 16 : (m0 + width) // 16]
 
-        def gather_belly(c, i):
+        def gather_belly(c, pair):
             width = CHUNKS[c][1]
-            raw = ring.tile([P, width], F32, name="belly_raw", bufs=3)
-            nc.vector.tensor_copy(raw[:], h_sb[i][:].indirect(picks(c, 0)))
-            belly[c, i] = ring.tile([P, width], F32, name="belly_abs", bufs=3)
-            nc.scalar.activation(belly[c, i][:], raw[:], ACT.Abs, scale=2.0)
+            belly[c, pair] = ring.tile([P, 2, width], F32, name="belly")
+            for e in range(2):
+                nc.vector.tensor_copy(belly[c, pair][:, e, :], h_sb[2 * pair + e][:].indirect(picks(c, 0)))
 
-        def gather_short(c, i):
+        def gather_wings(c, pair):
             width = CHUNKS[c][1]
-            short[c, i] = ring.tile([P, width], F32, name="short", bufs=3)
-            nc.vector.tensor_tensor(short[c, i][:], h_sb[i][:].indirect(picks(c, 1)), belly[c, i][:], ALU.subtract)
-
-        def gather_long(c, i):
-            width = CHUNKS[c][1]
-            a, t = divmod(i, 4)
-            if t == 0:
+            a, half = divmod(pair, 2)
+            twice_abs = ring.tile([P, 2, width], F32, name="twice_abs")
+            nc.scalar.activation(twice_abs[:], belly[c, pair][:], ACT.Abs, scale=2.0)
+            short = ring.tile([P, 2, width], F32, name="short")
+            for e in range(2):
+                nc.vector.tensor_tensor(
+                    short[:, e, :], h_sb[2 * pair + e][:].indirect(picks(c, 1)), twice_abs[:, e, :], ALU.subtract
+                )
+            if half == 0:
                 wings[c, a] = ring.tile([P, 4, width], F32, name="wings")
-            nc.vector.tensor_tensor(wings[c, a][:, t, :], h_sb[i][:].indirect(picks(c, 2)), short[c, i][:], ALU.add)
-            if t == 3:
+            for e in range(2):
+                nc.vector.tensor_tensor(
+                    wings[c, a][:, 2 * half + e, :], h_sb[2 * pair + e][:].indirect(picks(c, 2)), short[:, e, :], ALU.add
+                )
+            if half == 1:
                 z_bf[c, a] = ring.tile([P, width, 4], BF16, name="z_bf", align_bytes=64)
-                nc.scalar.activation(z_bf[c, a][:], wings[c, a][:].rearrange("p t m -> p m t"), ACT.Copy, scale=-0.5)
+                nc.scalar.activation(
+                    z_bf[c, a][:].rearrange("p (g m) t -> p g t m", m=4),
+                    wings[c, a][:].rearrange("p t (g m) -> p g t m", m=4),
+                    ACT.Copy,
+                    scale=-0.5,
+                )
 
         def quantise_z(c, a):
             m0, width = CHUNKS[c]
@@ -190,17 +201,17 @@ def tile_list_muni_butterfly_residual_kernel(
             )
 
         def product(bank, w_codes, w_sc, b, x_codes, x_sc):
-            for t in range(4):
-                cols = slice(512 * b + P * t, 512 * b + P * (t + 1))
-                for a in range(2):
+            for a in range(2):
+                for t in range(4):
+                    cols = slice(512 * b + P * t, 512 * b + P * (t + 1))
                     nc.tensor.matmul_mx(
                         out=bank[:, t, :],
                         lhsT=w_codes(a, cols).bitcast(FP8X4),
                         lhsT_scale=w_sc(a, cols),
                         rhs=x_codes[a].bitcast(FP8X4),
                         rhs_scale=x_sc[a],
-                        start=(a == 0),
-                        stop=(a == 1),
+                        start=(a == 0 and t == 0),
+                        stop=(a == 1 and t == 3),
                     )
 
         y_sb = {}
@@ -210,8 +221,10 @@ def tile_list_muni_butterfly_residual_kernel(
 
         def second_product(u):
             trades = slice(SUB * u, SUB * (u + 1))
+            banks = []
             for b in range(2):
-                bank = psum.tile([P, 4, SUB], F32, name="bank")
+                bank = psum.tile([P, 4, SUB], F32, name="bank_b")
+                banks.append(bank)
                 product(
                     bank,
                     lambda a, cols: w2_codes[a][:, cols],
@@ -222,8 +235,9 @@ def tile_list_muni_butterfly_residual_kernel(
                 )
                 th[u, b] = ring.tile([P, SUB, 4], F32, name="th")
                 nc.scalar.activation(th[u, b][:], bank[:].rearrange("p t m -> p m t"), ACT.Tanh)
+            for b in range(2):
                 y_sb[u, b] = ring.tile([P, 4, SUB], F32, name="y_b", bufs=4)
-                nc.scalar.copy(y_sb[u, b][:], bank[:])
+                nc.scalar.copy(y_sb[u, b][:], banks[b][:])
 
         def quantise_act(u):
             act_bf = []
@@ -243,10 +257,10 @@ def tile_list_muni_butterfly_residual_kernel(
 
         def third_product(u):
             for b in range(2):
-                bank = psum.tile([P, 4, SUB], F32, name="bank")
+                bank = psum.tile([P, 4, SUB], F32, name="bank_a")
                 product(
                     bank,
-                    lambda a, cols: w3_codes[0][:, a, cols],
+                    lambda a, cols: w3_codes[:, a, cols],
                     lambda a, cols: planes[a][:, 2, cols],
                     b,
                     [act_codes[u, a][:] for a in range(2)],
@@ -263,27 +277,28 @@ def tile_list_muni_butterfly_residual_kernel(
         def at(n, work):
             extra.setdefault(n, []).append(work)
 
-        for piece, n in enumerate((2, 3, 5, 6, 8, 9, 10, 11)):
+        for piece, n in enumerate((1, 1, 2, 2, 3, 3, 4, 4)):
             at(n, lambda piece=piece: round_w2(piece))
-        at(8, order_w3)
         for c in range(len(CHUNKS)):
             for a in range(2):
-                at(8 * c + 4 * a + 6, lambda c=c, a=a: quantise_z(c, a))
-        for u, n in enumerate((13, 16, 19, 26)):
+                at(4 * c + 2 * a + 2, lambda c=c, a=a: quantise_z(c, a))
+        for u, n in enumerate((5, 8, 11, 12)):
             at(n, lambda u=u: second_product(u))
             at(n + 1, lambda u=u: quantise_act(u))
             at(n + 2, lambda u=u: third_product(u))
 
         first_product(0)
+        first_product(1)
 
-        for n in range(len(steps) + 5):
-            if n + 1 < 8:
-                first_product(n + 1)
+        gather_belly(*steps[0])
+        order_w3()
+        for n in range(len(steps) + 3):
+            if n < 3:
+                first_product(2 * n + 2)
+                first_product(2 * n + 3)
+            if n + 1 < len(steps):
+                gather_belly(*steps[n + 1])
             if n < len(steps):
-                gather_belly(*steps[n])
-            if 1 <= n <= len(steps):
-                gather_short(*steps[n - 1])
-            if 2 <= n <= len(steps) + 1:
-                gather_long(*steps[n - 2])
+                gather_wings(*steps[n])
             for work in extra.get(n, []):
                 work()

@@ -1,6 +1,7 @@
 from contextlib import ExitStack
 
 import concourse.mybir as mybir
+from concourse.masks import make_identity
 
 K, T, S, M, H, N = 1024, 4096, 1024, 512, 1024, 1024
 FLOPS = 2 * K * H * S + 2 * H * N * M + 2 * N * N * M
@@ -29,7 +30,7 @@ def tile_list_muni_butterfly_residual_kernel(
     with ExitStack() as ctx:
         keep = ctx.enter_context(tc.tile_pool(name="keep", bufs=1))
         ring = ctx.enter_context(tc.tile_pool(name="ring", bufs=2))
-        psum = ctx.enter_context(tc.psum_pool(name="psum", bufs=4))
+        psum = ctx.enter_context(tc.psum_pool(name="psum", bufs=2))
 
         def kept(name, shape, dtype):
             return keep.tile(shape, dtype, name=name, align_bytes=64)
@@ -38,23 +39,26 @@ def tile_list_muni_butterfly_residual_kernel(
         pos_sb = [kept("pos_sb%d" % i, [P, M // 16], U16) for i in range(3)]
         tab_sb = [kept("big%d" % a, [P, T], I32) for a in range(2)]
         tab_sc = kept("tab_sc", [P, T], U8)
-        w1_raw = kept("w1_raw", [P, 2, H // 2], I32)
-        w_sc_raw = kept("w_sc_raw", [P, 2, N], U8)
+        w1_codes = kept("w1_codes", [P, 2, H // 2], I32)
+        w3_sc_raw = kept("w3_sc_raw", [P, N], U8)
         gain_sb = kept("gain_sb", [P, 2, 4], F32)
         planes = [kept("planes%d" % a, [P, 3, 1024], U8) for a in range(2)]
+        ident = kept("ident", [P, P], F32)
 
         for rows in (slice(32, 64), slice(64, P)):
             nc.vector.memset(tab_sc[rows].bitcast(I32), 0)
-            nc.gpsimd.memset(w_sc_raw[rows].bitcast(I32), 0)
+            nc.gpsimd.memset(w3_sc_raw[rows].bitcast(I32), 0)
+            nc.gpsimd.memset(planes[0][rows, 1].bitcast(I32), 0)
         nc.gpsimd.memset(planes[1][:].bitcast(I32), 0)
+        make_identity(nc, ident[:])
 
         nc.sync.dma_start(offs_sb[:], offs)
         nc.sync.dma_start(tab_sc[0:32].bitcast(I32), tab_scales.rearrange("a q t -> (a q) t").bitcast(I32))
-        nc.sync.dma_start(w_sc_raw[0:32, 0].bitcast(I32), w1_scales.rearrange("a q c -> (a q) c").bitcast(I32))
-        nc.sync.dma_start(w_sc_raw[0:32, 1].bitcast(I32), w3_scales.rearrange("a q c -> (a q) c").bitcast(I32))
-        nc.sync.dma_start(w1_raw[:], w1_words.rearrange("a p c -> p a c").bitcast(I32))
-        nc.sync.dma_start(tab_sb[0][:], tab_words[0].rearrange("p t i -> p (t i)").bitcast(I32))
-        nc.sync.dma_start(tab_sb[1][:], tab_words[1].rearrange("p t i -> p (t i)").bitcast(I32))
+        nc.sync.dma_start(w3_sc_raw[0:32].bitcast(I32), w3_scales.rearrange("a q c -> (a q) c").bitcast(I32))
+        nc.sync.dma_start(planes[0][0:32, 1].bitcast(I32), w1_scales.rearrange("a q c -> (a q) c").bitcast(I32))
+        nc.sync.dma_start(w1_codes[:], w1_words.rearrange("a p c -> p a c").bitcast(I32))
+        for a in range(2):
+            nc.sync.dma_start(tab_sb[a][:], tab_words[a].rearrange("p t i -> p (t i)").bitcast(I32))
         for tile, lst in zip(pos_sb, (pos1, pos2, pos3)):
             nc.sync.dma_start(tile[:], lst)
         nc.sync.dma_start(gain_sb[:], gain.rearrange("(b p t) -> p b t", b=2, t=4))
@@ -63,12 +67,8 @@ def tile_list_muni_butterfly_residual_kernel(
         v_codes = [kept("v_codes%d" % a, [P, S], U32) for a in range(2)]
         nc.vector.tensor_copy(v_sc[:], tab_sc[:].indirect(offs_sb[:]))
         nc.vector.tensor_copy(
-            planes[0][:, 1].bitcast(I32).rearrange("p (b t q w) -> p b q t w", b=2, t=4, w=2),
-            w_sc_raw[:, 0].bitcast(I32).rearrange("p (b q t w) -> p b q t w", b=2, t=4, w=2),
-        )
-        nc.vector.tensor_copy(
             planes[0][:, 2].rearrange("p (b t g m) -> p b g t m", b=2, t=4, m=16),
-            w_sc_raw[:, 1].rearrange("p (b g m t) -> p b g t m", b=2, t=4, m=16),
+            w3_sc_raw[:].rearrange("p (b g m t) -> p b g t m", b=2, t=4, m=16),
         )
         nc.vector.tensor_copy(planes[0][:, 0].bitcast(I32), v_sc[:].bitcast(I32))
         for a in range(2):
@@ -79,12 +79,7 @@ def tile_list_muni_butterfly_residual_kernel(
                     queue.dma_start(
                         planes[a][32 * q : 32 * q + 4].bitcast(I32), planes[0][row : row + 4].bitcast(I32)
                     )
-        w1_codes = kept("w1_codes", [P, 2, H // 2], I32)
-        nc.vector.tensor_copy(
-            w1_codes[:].rearrange("p a (b t q w) -> p (a b) q t w", b=2, t=4, w=4),
-            w1_raw[:].rearrange("p a (b q t w) -> p (a b) q t w", b=2, t=4, w=4),
-        )
-        w3_raw = kept("w1_raw", [P, 2, N], I32)
+        w3_raw = kept("v_sc", [P, 2, N], I32)
         nc.sync.dma_start(w3_raw[:], w3_words.rearrange("a p c i -> p a (c i)").bitcast(I32))
 
         nc.vector.tensor_copy(v_codes[0][:], tab_sb[0][:].bitcast(U32).indirect(offs_sb[:]))
@@ -94,11 +89,13 @@ def tile_list_muni_butterfly_residual_kernel(
                 tab_sb[1][:].bitcast(U32).indirect(offs_sb[:, 32 * half : 32 * (half + 1)]),
             )
 
-        w2_raw = [kept("big%d" % a, [P, 4, N], F32) for a in range(2)]
+        w2_raw = [kept("big%d" % a, [P, 2, 4, 512], F32) for a in range(2)]
         for a in range(2):
-            rows = w2[512 * a : 512 * a + 512, :].rearrange("(q j i) n -> j q i n", j=4, i=8)
-            for j in range(4):
-                nc.sync.dma_start(w2_raw[a][:, j, :], rows[j])
+            for b in range(2):
+                nc.sync.dma_start(
+                    w2_raw[a][:, b],
+                    w2[512 * a : 512 * (a + 1), 512 * b : 512 * (b + 1)].rearrange("(p j) n -> p j n", j=4),
+                )
 
         w3_codes = kept("w3_codes", [P, 2, N], I32)
 
@@ -111,21 +108,20 @@ def tile_list_muni_butterfly_residual_kernel(
         h_sb = [kept("h_sb%d" % i, [P, S], F32) for i in range(8)]
 
         def first_product(i):
-            cols = slice(P * i, P * (i + 1))
             for half in range(2):
                 quotes = slice(BANK * half, BANK * (half + 1))
-                bank = psum.tile([P, BANK], F32, name="bank_a")
+                bank = psum.tile([P, BANK], F32, name="bank_a", bufs=3)
                 for a in range(2):
                     nc.tensor.matmul_mx(
                         out=bank[:],
-                        lhsT=w1_codes[:, a, cols.start // 2 : cols.stop // 2].bitcast(U8).bitcast(FP4X4),
-                        lhsT_scale=planes[a][:, 1, cols],
+                        lhsT=w1_codes[:, a, 64 * i : 64 * (i + 1)].bitcast(U8).bitcast(FP4X4),
+                        lhsT_scale=planes[a][:, 1, P * i : P * (i + 1)],
                         rhs=v_codes[a][:, quotes].bitcast(FP8X4),
                         rhs_scale=planes[a][:, 0, quotes],
                         start=(a == 0),
                         stop=(a == 1),
                     )
-                if i < 2 and half == 1:
+                if i == 0 and half == 1:
                     nc.vector.tensor_copy(h_sb[i][:, quotes], bank[:])
                 else:
                     nc.scalar.copy(h_sb[i][:, quotes], bank[:])
@@ -139,7 +135,7 @@ def tile_list_muni_butterfly_residual_kernel(
             if part == 0:
                 w2_grouped[a, b] = ring.tile([P, 2048], BF16, name="w2_grouped", align_bytes=64)
             dst = w2_grouped[a, b][:].rearrange("p (t m j) -> p m j t", t=4, j=4)
-            src = w2_raw[a][:, :, 512 * b : 512 * (b + 1)].rearrange("p j (m t) -> p m j t", t=4)
+            src = w2_raw[a][:, b].rearrange("p j (m t) -> p m j t", t=4)
             ms = slice(64 * part, 64 * (part + 1))
             nc.scalar.copy(dst[:, ms], src[:, ms])
             if part == 1:
@@ -150,58 +146,69 @@ def tile_list_muni_butterfly_residual_kernel(
 
         z_codes = [kept("z_codes%d" % a, [P, M], U32) for a in range(2)]
         z_sc = [kept("z_sc%d" % a, [P, M], U8) for a in range(2)]
-
-        steps = [(c, pair) for c in range(len(CHUNKS)) for pair in range(4)]
-        belly = {}
-        wings = {}
+        legs = {}
+        sums = {}
         z_bf = {}
 
-        def picks(c, k):
+        def gather(g):
+            c, a = divmod(g, 2)
             m0, width = CHUNKS[c]
-            return pos_sb[k][:, m0 // 16 : (m0 + width) // 16]
+            for k in range(3):
+                legs[g, k] = ring.tile([P, 4, width], F32, name="leg%d" % k)
+                for t in range(4):
+                    nc.vector.tensor_copy(
+                        legs[g, k][:, t, :],
+                        h_sb[4 * a + t][:].indirect(pos_sb[k][:, m0 // 16 : (m0 + width) // 16]),
+                    )
 
-        def gather_belly(c, pair):
-            width = CHUNKS[c][1]
-            belly[c, pair] = ring.tile([P, 2, width], F32, name="belly")
-            for e in range(2):
-                nc.vector.tensor_copy(belly[c, pair][:, e, :], h_sb[2 * pair + e][:].indirect(picks(c, 0)))
+        def add_legs(g):
+            width = CHUNKS[g // 2][1]
+            magnitude = ring.tile([P, 4, width], F32, name="magnitude")
+            nc.scalar.activation(magnitude[:], legs[g, 0][:], ACT.Abs)
+            belly = ring.tile([P, 4, width], F32, name="belly")
+            nc.vector.tensor_scalar(belly[:], magnitude[:], -2.0, None, ALU.mult)
+            terms = (belly, legs[g, 1], legs[g, 2])
+            for block in range(width // SUB):
+                sums[g, block] = psum.tile([P, 4, P], F32, name="bank_sum")
+                for k in range(3):
+                    for t in range(4):
+                        nc.tensor.matmul(
+                            sums[g, block][:, t, :],
+                            lhsT=terms[k][:, t, SUB * block : SUB * (block + 1)],
+                            rhs=ident[:],
+                            is_transpose=True,
+                            start=(k == 0 and t == 0),
+                            stop=(k == 2 and t == 3),
+                        )
 
-        def gather_wings(c, pair):
-            width = CHUNKS[c][1]
-            a, half = divmod(pair, 2)
-            twice_abs = ring.tile([P, 2, width], F32, name="twice_abs")
-            nc.scalar.activation(twice_abs[:], belly[c, pair][:], ACT.Abs, scale=2.0)
-            short = ring.tile([P, 2, width], F32, name="short")
-            for e in range(2):
-                nc.vector.tensor_tensor(
-                    short[:, e, :], h_sb[2 * pair + e][:].indirect(picks(c, 1)), twice_abs[:, e, :], ALU.subtract
-                )
-            if half == 0:
-                wings[c, a] = ring.tile([P, 4, width], F32, name="wings")
-            for e in range(2):
-                nc.vector.tensor_tensor(
-                    wings[c, a][:, 2 * half + e, :], h_sb[2 * pair + e][:].indirect(picks(c, 2)), short[:, e, :], ALU.add
-                )
-            if half == 1:
-                z_bf[c, a] = ring.tile([P, width, 4], BF16, name="z_bf", align_bytes=64)
+        def round_z(g):
+            blocks = CHUNKS[g // 2][1] // SUB
+            back = psum.tile([P, blocks, 2, SUB], F32, name="bank_back", bufs=1)
+            for block in range(blocks):
+                z_t = ring.tile([P, 2, P, 2], BF16, name="z_t")
                 nc.scalar.activation(
-                    z_bf[c, a][:].rearrange("p (g m) t -> p g t m", m=4),
-                    wings[c, a][:].rearrange("p t (g m) -> p g t m", m=4),
+                    z_t[:],
+                    sums[g, block][:].rearrange("m t r -> m (t r)").rearrange("m (p u e) -> m u p e", u=2, e=2),
                     ACT.Copy,
                     scale=-0.5,
                 )
-
-        def quantise_z(c, a):
-            m0, width = CHUNKS[c]
-            cols = slice(m0, m0 + width)
-            nc.vector.quantize_mx(
-                out=z_codes[a][:, cols].bitcast(FP8X4),
-                scales=z_sc[a][:, cols],
-                in_=z_bf[c, a][:].rearrange("p m t -> p (m t)"),
+                pairs = z_t[:].rearrange("m u p e -> m u (p e)").bitcast(F32)
+                for u in range(2):
+                    nc.tensor.transpose(back[:, block, u, :], pairs[:, u, :], ident[:])
+            z_bf[g] = ring.tile([P, blocks * SUB * 4], BF16, name="z_bf", align_bytes=64)
+            nc.scalar.copy(
+                z_bf[g][:].bitcast(F32).rearrange("p (k m u) -> p k m u", m=SUB, u=2),
+                back[:].rearrange("p k u m -> p k m u"),
             )
 
-        def product(bank, w_codes, w_sc, b, x_codes, x_sc):
-            for a in range(2):
+        def quantise_z(g):
+            c, a = divmod(g, 2)
+            m0, width = CHUNKS[c]
+            cols = slice(m0, m0 + width)
+            nc.vector.quantize_mx(out=z_codes[a][:, cols].bitcast(FP8X4), scales=z_sc[a][:, cols], in_=z_bf[g][:])
+
+        def product(bank, w_codes, w_sc, b, x_codes, x_sc, passes):
+            for a in passes:
                 for t in range(4):
                     cols = slice(512 * b + P * t, 512 * b + P * (t + 1))
                     nc.tensor.matmul_mx(
@@ -210,21 +217,21 @@ def tile_list_muni_butterfly_residual_kernel(
                         lhsT_scale=w_sc(a, cols),
                         rhs=x_codes[a].bitcast(FP8X4),
                         rhs_scale=x_sc[a],
-                        start=(a == 0 and t == 0),
-                        stop=(a == 1 and t == 3),
+                        start=(a == passes[0] and t == 0),
+                        stop=(a == passes[1] and t == 3),
                     )
 
         y_sb = {}
+        y_banks = {}
         th = {}
         act_codes = {}
         act_sc = {}
 
         def second_product(u):
             trades = slice(SUB * u, SUB * (u + 1))
-            banks = []
             for b in range(2):
-                bank = psum.tile([P, 4, SUB], F32, name="bank_b")
-                banks.append(bank)
+                bank = psum.tile([P, 4, SUB], F32, name="bank_y")
+                y_banks[u, b] = bank
                 product(
                     bank,
                     lambda a, cols: w2_codes[a][:, cols],
@@ -232,12 +239,15 @@ def tile_list_muni_butterfly_residual_kernel(
                     b,
                     [z_codes[a][:, trades] for a in range(2)],
                     [z_sc[a][:, trades] for a in range(2)],
+                    (0, 1) if u == 3 else (1, 0),
                 )
-                th[u, b] = ring.tile([P, SUB, 4], F32, name="th")
+                th[u, b] = ring.tile([P, SUB, 4], F32, name="th", bufs=4)
                 nc.scalar.activation(th[u, b][:], bank[:].rearrange("p t m -> p m t"), ACT.Tanh)
+
+        def keep_y(u):
             for b in range(2):
                 y_sb[u, b] = ring.tile([P, 4, SUB], F32, name="y_b", bufs=4)
-                nc.scalar.copy(y_sb[u, b][:], banks[b][:])
+                nc.scalar.copy(y_sb[u, b][:], y_banks[u, b][:])
 
         def quantise_act(u):
             act_bf = []
@@ -257,7 +267,7 @@ def tile_list_muni_butterfly_residual_kernel(
 
         def third_product(u):
             for b in range(2):
-                bank = psum.tile([P, 4, SUB], F32, name="bank_a")
+                bank = psum.tile([P, 4, SUB], F32, name="bank_a", bufs=3)
                 product(
                     bank,
                     lambda a, cols: w3_codes[:, a, cols],
@@ -265,6 +275,7 @@ def tile_list_muni_butterfly_residual_kernel(
                     b,
                     [act_codes[u, a][:] for a in range(2)],
                     [act_sc[u, a][:] for a in range(2)],
+                    (0, 1),
                 )
                 result = ring.tile([P, 4, SUB], F32, name="result", bufs=4)
                 nc.vector.tensor_tensor(result[:], bank[:], y_sb[u, b][:], ALU.add)
@@ -272,33 +283,60 @@ def tile_list_muni_butterfly_residual_kernel(
                     out[512 * b : 512 * (b + 1), SUB * u : SUB * (u + 1)].rearrange("(p t) m -> p t m", t=4), result[:]
                 )
 
-        extra = {}
-
-        def at(n, work):
-            extra.setdefault(n, []).append(work)
-
-        for piece, n in enumerate((1, 1, 2, 2, 3, 3, 4, 4)):
-            at(n, lambda piece=piece: round_w2(piece))
-        for c in range(len(CHUNKS)):
-            for a in range(2):
-                at(4 * c + 2 * a + 2, lambda c=c, a=a: quantise_z(c, a))
-        for u, n in enumerate((5, 8, 11, 12)):
-            at(n, lambda u=u: second_product(u))
-            at(n + 1, lambda u=u: quantise_act(u))
-            at(n + 2, lambda u=u: third_product(u))
-
         first_product(0)
         first_product(1)
-
-        gather_belly(*steps[0])
+        first_product(2)
+        first_product(3)
+        gather(0)
         order_w3()
-        for n in range(len(steps) + 3):
-            if n < 3:
-                first_product(2 * n + 2)
-                first_product(2 * n + 3)
-            if n + 1 < len(steps):
-                gather_belly(*steps[n + 1])
-            if n < len(steps):
-                gather_wings(*steps[n])
-            for work in extra.get(n, []):
-                work()
+        first_product(4)
+        first_product(5)
+        first_product(6)
+        first_product(7)
+        gather(1)
+        add_legs(0)
+        round_w2(0)
+        round_z(0)
+        gather(2)
+        quantise_z(0)
+        add_legs(1)
+        round_w2(1)
+        round_w2(2)
+        round_z(1)
+        gather(3)
+        quantise_z(1)
+        add_legs(2)
+        round_w2(3)
+        round_w2(4)
+        round_z(2)
+        gather(4)
+        quantise_z(2)
+        add_legs(3)
+        round_w2(5)
+        round_w2(6)
+        round_w2(7)
+        round_z(3)
+        gather(5)
+        quantise_z(3)
+        second_product(0)
+        keep_y(0)
+        add_legs(4)
+        quantise_act(0)
+        round_z(4)
+        second_product(1)
+        keep_y(1)
+        third_product(0)
+        quantise_z(4)
+        add_legs(5)
+        quantise_act(1)
+        second_product(2)
+        keep_y(2)
+        third_product(1)
+        round_z(5)
+        quantise_z(5)
+        quantise_act(2)
+        second_product(3)
+        keep_y(3)
+        third_product(2)
+        quantise_act(3)
+        third_product(3)

@@ -1,7 +1,6 @@
 from contextlib import ExitStack
 
 import concourse.mybir as mybir
-from concourse.masks import make_identity
 
 K, T, S, M, H, N = 1024, 4096, 1024, 512, 1024, 1024
 FLOPS = 2 * K * H * S + 2 * H * N * M + 2 * N * N * M
@@ -18,9 +17,12 @@ ALU = mybir.AluOpType
 ACT = mybir.ActivationFunctionType
 
 P = 128
+PASS = 512
 BANK = 512
-SUB = 128
-CHUNKS = [(0, 256), (256, 128), (384, 128)]
+BLOCK = 128
+BLOCKS = M // BLOCK
+PER_COLUMN = 16
+SPANS = [(0, 0, M), (1, 0, M - BLOCK), (1, M - BLOCK, BLOCK)]
 
 
 def tile_list_muni_butterfly_residual_kernel(
@@ -30,58 +32,62 @@ def tile_list_muni_butterfly_residual_kernel(
     with ExitStack() as ctx:
         keep = ctx.enter_context(tc.tile_pool(name="keep", bufs=1))
         ring = ctx.enter_context(tc.tile_pool(name="ring", bufs=2))
-        psum = ctx.enter_context(tc.psum_pool(name="psum", bufs=2))
+        psum = ctx.enter_context(tc.psum_pool(name="psum", bufs=4))
 
-        def kept(name, shape, dtype):
-            return keep.tile(shape, dtype, name=name, align_bytes=64)
+        def kept(tag, shape, dtype):
+            return keep.tile(shape, dtype, name=tag, align_bytes=64)
 
-        offs_sb = kept("offs_sb", [P, S // 16], U16)
-        pos_sb = [kept("pos_sb%d" % i, [P, M // 16], U16) for i in range(3)]
+        offs_sb = kept("offs_sb", [P, S // PER_COLUMN], U16)
+        pos_sb = [kept("pos_sb%d" % leg, [P, M // PER_COLUMN], U16) for leg in range(3)]
         tab_sb = [kept("big%d" % a, [P, T], I32) for a in range(2)]
-        tab_sc = kept("tab_sc", [P, T], U8)
-        w1_codes = kept("w1_codes", [P, 2, H // 2], I32)
-        w3_sc_raw = kept("w3_sc_raw", [P, N], U8)
+        w1_raw = kept("w_raw", [P, 2, H // 2], I32)
         gain_sb = kept("gain_sb", [P, 2, 4], F32)
-        planes = [kept("planes%d" % a, [P, 3, 1024], U8) for a in range(2)]
-        ident = kept("ident", [P, P], F32)
 
+        tab_sc = kept("tab_sc", [P, T], U8)
+        w_sc_raw = kept("w_sc_raw", [P, 2, N], U8)
+        scale_sb = [kept("scale_sb%d" % a, [P, 3, 1024], U8) for a in range(2)]
         for rows in (slice(32, 64), slice(64, P)):
             nc.vector.memset(tab_sc[rows].bitcast(I32), 0)
-            nc.gpsimd.memset(w3_sc_raw[rows].bitcast(I32), 0)
-            nc.gpsimd.memset(planes[0][rows, 1].bitcast(I32), 0)
-        nc.gpsimd.memset(planes[1][:].bitcast(I32), 0)
-        make_identity(nc, ident[:])
+            nc.gpsimd.memset(w_sc_raw[rows].bitcast(I32), 0)
+        nc.gpsimd.memset(scale_sb[1][:].bitcast(I32), 0)
 
         nc.sync.dma_start(offs_sb[:], offs)
         nc.sync.dma_start(tab_sc[0:32].bitcast(I32), tab_scales.rearrange("a q t -> (a q) t").bitcast(I32))
-        nc.sync.dma_start(w3_sc_raw[0:32].bitcast(I32), w3_scales.rearrange("a q c -> (a q) c").bitcast(I32))
-        nc.sync.dma_start(planes[0][0:32, 1].bitcast(I32), w1_scales.rearrange("a q c -> (a q) c").bitcast(I32))
-        nc.sync.dma_start(w1_codes[:], w1_words.rearrange("a p c -> p a c").bitcast(I32))
+        nc.sync.dma_start(w_sc_raw[0:32, 0].bitcast(I32), w1_scales.rearrange("a q c -> (a q) c").bitcast(I32))
+        nc.sync.dma_start(w_sc_raw[0:32, 1].bitcast(I32), w3_scales.rearrange("a q c -> (a q) c").bitcast(I32))
+        nc.sync.dma_start(w1_raw[:], w1_words.rearrange("a p c -> p a c").bitcast(I32))
         for a in range(2):
             nc.sync.dma_start(tab_sb[a][:], tab_words[a].rearrange("p t i -> p (t i)").bitcast(I32))
-        for tile, lst in zip(pos_sb, (pos1, pos2, pos3)):
-            nc.sync.dma_start(tile[:], lst)
+        for leg, positions in enumerate((pos1, pos2, pos3)):
+            nc.sync.dma_start(pos_sb[leg][:], positions)
         nc.sync.dma_start(gain_sb[:], gain.rearrange("(b p t) -> p b t", b=2, t=4))
 
         v_sc = kept("v_sc", [P, S], U8)
-        v_codes = [kept("v_codes%d" % a, [P, S], U32) for a in range(2)]
         nc.vector.tensor_copy(v_sc[:], tab_sc[:].indirect(offs_sb[:]))
         nc.vector.tensor_copy(
-            planes[0][:, 2].rearrange("p (b t g m) -> p b g t m", b=2, t=4, m=16),
-            w3_sc_raw[:].rearrange("p (b g m t) -> p b g t m", b=2, t=4, m=16),
+            scale_sb[0][:, 1].bitcast(I32).rearrange("p (b t g w) -> p b g t w", b=2, t=4, w=2),
+            w_sc_raw[:, 0].bitcast(I32).rearrange("p (b g t w) -> p b g t w", b=2, t=4, w=2),
         )
-        nc.vector.tensor_copy(planes[0][:, 0].bitcast(I32), v_sc[:].bitcast(I32))
-        for a in range(2):
-            for q in range(4):
-                row = 16 * a + 4 * q
-                if row:
-                    queue = nc.gpsimd if row == 28 else nc.scalar
-                    queue.dma_start(
-                        planes[a][32 * q : 32 * q + 4].bitcast(I32), planes[0][row : row + 4].bitcast(I32)
-                    )
-        w3_raw = kept("v_sc", [P, 2, N], I32)
+        nc.vector.tensor_copy(
+            scale_sb[0][:, 2].rearrange("p (b t g m) -> p b g t m", b=2, t=4, m=16),
+            w_sc_raw[:, 1].rearrange("p (b g m t) -> p b g t m", b=2, t=4, m=16),
+        )
+        nc.vector.tensor_copy(scale_sb[0][:, 0].bitcast(I32), v_sc[:].bitcast(I32))
+        moves = [(a, q) for a in range(2) for q in range(4)][1:]
+        for a, q in moves:
+            queue = nc.gpsimd if (a, q) == moves[-1] else nc.scalar
+            row = 16 * a + 4 * q
+            queue.dma_start(scale_sb[a][32 * q : 32 * q + 4].bitcast(I32), scale_sb[0][row : row + 4].bitcast(I32))
+
+        w1_codes = kept("w1_codes", [P, 2, H // 2], I32)
+        nc.vector.tensor_copy(
+            w1_codes[:].rearrange("p a (b t g w) -> p (a b) g t w", b=2, t=4, w=4),
+            w1_raw[:].rearrange("p a (b g t w) -> p (a b) g t w", b=2, t=4, w=4),
+        )
+        w3_raw = kept("w_raw", [P, 2, N], I32)
         nc.sync.dma_start(w3_raw[:], w3_words.rearrange("a p c i -> p a (c i)").bitcast(I32))
 
+        v_codes = [kept("v_codes%d" % a, [P, S], U32) for a in range(2)]
         nc.vector.tensor_copy(v_codes[0][:], tab_sb[0][:].bitcast(U32).indirect(offs_sb[:]))
         for half in range(2):
             nc.vector.tensor_copy(
@@ -89,15 +95,19 @@ def tile_list_muni_butterfly_residual_kernel(
                 tab_sb[1][:].bitcast(U32).indirect(offs_sb[:, 32 * half : 32 * (half + 1)]),
             )
 
-        w2_raw = [kept("big%d" % a, [P, 2, 4, 512], F32) for a in range(2)]
+        w2_raw = [kept("big%d" % a, [P, 4, N], F32) for a in range(2)]
         for a in range(2):
-            for b in range(2):
-                nc.sync.dma_start(
-                    w2_raw[a][:, b],
-                    w2[512 * a : 512 * (a + 1), 512 * b : 512 * (b + 1)].rearrange("(p j) n -> p j n", j=4),
-                )
+            w2_rows = w2[PASS * a : PASS * (a + 1), :].rearrange("(g t i) n -> t g i n", t=4, i=8)
+            for t in range(4):
+                nc.sync.dma_start(w2_raw[a][:, t, :], w2_rows[t])
 
         w3_codes = kept("w3_codes", [P, 2, N], I32)
+        h_sb = [kept("h_sb%d" % i, [P, S], F32) for i in range(8)]
+        w2_codes = [kept("w2_codes%d" % a, [P, N], U32) for a in range(2)]
+        w2_sc = [kept("w2_sc%d" % a, [P, N], U8) for a in range(2)]
+        z_codes = [kept("z_codes%d" % a, [P, M], U32) for a in range(2)]
+        z_sc = [kept("z_sc%d" % a, [P, M], U8) for a in range(2)]
+        belly, wings, y_bank, y_sb, tanh_y, act_codes, act_sc = {}, {}, {}, {}, {}, {}, {}
 
         def order_w3():
             nc.vector.tensor_copy(
@@ -105,160 +115,118 @@ def tile_list_muni_butterfly_residual_kernel(
                 w3_raw[:].rearrange("p a (b g m t) -> p (a b) g t m", b=2, t=4, m=4),
             )
 
-        h_sb = [kept("h_sb%d" % i, [P, S], F32) for i in range(8)]
-
-        def first_product(i):
-            for half in range(2):
-                quotes = slice(BANK * half, BANK * (half + 1))
-                bank = psum.tile([P, BANK], F32, name="bank_a", bufs=3)
-                for a in range(2):
-                    nc.tensor.matmul_mx(
-                        out=bank[:],
-                        lhsT=w1_codes[:, a, 64 * i : 64 * (i + 1)].bitcast(U8).bitcast(FP4X4),
-                        lhsT_scale=planes[a][:, 1, P * i : P * (i + 1)],
-                        rhs=v_codes[a][:, quotes].bitcast(FP8X4),
-                        rhs_scale=planes[a][:, 0, quotes],
-                        start=(a == 0),
-                        stop=(a == 1),
-                    )
-                if i == 0 and half == 1:
-                    nc.vector.tensor_copy(h_sb[i][:, quotes], bank[:])
-                else:
-                    nc.scalar.copy(h_sb[i][:, quotes], bank[:])
-
-        w2_codes = [kept("w2_codes%d" % a, [P, N], U32) for a in range(2)]
-        w2_sc = [kept("w2_sc%d" % a, [P, N], U8) for a in range(2)]
-        w2_grouped = {}
-
-        def round_w2(piece):
-            a, b, part = piece // 4, piece // 2 % 2, piece % 2
-            if part == 0:
-                w2_grouped[a, b] = ring.tile([P, 2048], BF16, name="w2_grouped", align_bytes=64)
-            dst = w2_grouped[a, b][:].rearrange("p (t m j) -> p m j t", t=4, j=4)
-            src = w2_raw[a][:, b].rearrange("p j (m t) -> p m j t", t=4)
-            ms = slice(64 * part, 64 * (part + 1))
-            nc.scalar.copy(dst[:, ms], src[:, ms])
-            if part == 1:
-                cols = slice(512 * b, 512 * (b + 1))
-                nc.vector.quantize_mx(
-                    out=w2_codes[a][:, cols].bitcast(FP8X4), scales=w2_sc[a][:, cols], in_=w2_grouped[a, b][:]
-                )
-
-        z_codes = [kept("z_codes%d" % a, [P, M], U32) for a in range(2)]
-        z_sc = [kept("z_sc%d" % a, [P, M], U8) for a in range(2)]
-        legs = {}
-        sums = {}
-        z_bf = {}
-
-        def gather(g):
-            c, a = divmod(g, 2)
-            m0, width = CHUNKS[c]
-            for k in range(3):
-                legs[g, k] = ring.tile([P, 4, width], F32, name="leg%d" % k)
-                for t in range(4):
-                    nc.vector.tensor_copy(
-                        legs[g, k][:, t, :],
-                        h_sb[4 * a + t][:].indirect(pos_sb[k][:, m0 // 16 : (m0 + width) // 16]),
-                    )
-
-        def add_legs(g):
-            width = CHUNKS[g // 2][1]
-            magnitude = ring.tile([P, 4, width], F32, name="magnitude")
-            nc.scalar.activation(magnitude[:], legs[g, 0][:], ACT.Abs)
-            belly = ring.tile([P, 4, width], F32, name="belly")
-            nc.vector.tensor_scalar(belly[:], magnitude[:], -2.0, None, ALU.mult)
-            terms = (belly, legs[g, 1], legs[g, 2])
-            for block in range(width // SUB):
-                sums[g, block] = psum.tile([P, 4, P], F32, name="bank_sum")
-                for k in range(3):
-                    for t in range(4):
-                        nc.tensor.matmul(
-                            sums[g, block][:, t, :],
-                            lhsT=terms[k][:, t, SUB * block : SUB * (block + 1)],
-                            rhs=ident[:],
-                            is_transpose=True,
-                            start=(k == 0 and t == 0),
-                            stop=(k == 2 and t == 3),
+        def first_product(pair):
+            for i in (2 * pair, 2 * pair + 1):
+                for half in range(2):
+                    quotes = slice(BANK * half, BANK * (half + 1))
+                    bank = psum.tile([P, BANK], F32, name="bank_h_out")
+                    for a in range(2):
+                        nc.tensor.matmul_mx(
+                            out=bank[:],
+                            lhsT=w1_codes[:, a, 64 * i : 64 * (i + 1)].bitcast(U8).bitcast(FP4X4),
+                            lhsT_scale=scale_sb[a][:, 1, P * i : P * (i + 1)],
+                            rhs=v_codes[a][:, quotes].bitcast(FP8X4),
+                            rhs_scale=scale_sb[a][:, 0, quotes],
+                            start=(a == 0),
+                            stop=(a == 1),
                         )
+                    if pair == 0 and half == 1:
+                        nc.vector.tensor_copy(h_sb[i][:, quotes], bank[:])
+                    else:
+                        nc.scalar.copy(h_sb[i][:, quotes], bank[:])
 
-        def round_z(g):
-            blocks = CHUNKS[g // 2][1] // SUB
-            back = psum.tile([P, blocks, 2, SUB], F32, name="bank_back", bufs=1)
-            for block in range(blocks):
-                z_t = ring.tile([P, 2, P, 2], BF16, name="z_t")
-                nc.scalar.activation(
-                    z_t[:],
-                    sums[g, block][:].rearrange("m t r -> m (t r)").rearrange("m (p u e) -> m u p e", u=2, e=2),
-                    ACT.Copy,
-                    scale=-0.5,
-                )
-                pairs = z_t[:].rearrange("m u p e -> m u (p e)").bitcast(F32)
-                for u in range(2):
-                    nc.tensor.transpose(back[:, block, u, :], pairs[:, u, :], ident[:])
-            z_bf[g] = ring.tile([P, blocks * SUB * 4], BF16, name="z_bf", align_bytes=64)
-            nc.scalar.copy(
-                z_bf[g][:].bitcast(F32).rearrange("p (k m u) -> p k m u", m=SUB, u=2),
-                back[:].rearrange("p k u m -> p k m u"),
+        def quantise_w2(a):
+            for b in range(2):
+                cols = slice(PASS * b, PASS * (b + 1))
+                grouped = ring.tile([P, 4 * PASS], BF16, name="w2_grouped", align_bytes=64)
+                dst = grouped[:].rearrange("p (t m j) -> p m j t", t=4, j=4)
+                src = w2_raw[a][:, :, cols].rearrange("p j (m t) -> p m j t", t=4)
+                for part in (slice(0, 64), slice(64, P)):
+                    nc.scalar.copy(dst[:, part], src[:, part])
+                nc.vector.quantize_mx(out=w2_codes[a][:, cols].bitcast(FP8X4), scales=w2_sc[a][:, cols], in_=grouped[:])
+
+        def picked(span, t, leg):
+            a, first, count = SPANS[span]
+            entries = pos_sb[leg][:, first // PER_COLUMN : (first + count) // PER_COLUMN]
+            return h_sb[4 * a + t][:].indirect(entries)
+
+        def gather_belly(span, half):
+            belly[span, half] = ring.tile([P, 2, SPANS[span][2]], F32, name="belly")
+            for e in range(2):
+                nc.vector.tensor_copy(belly[span, half][:, e, :], picked(span, 2 * half + e, 0))
+
+        def gather_wings(span, half):
+            count = SPANS[span][2]
+            twice_abs = ring.tile([P, 2, count], F32, name="twice_abs")
+            nc.scalar.activation(twice_abs[:], belly[span, half][:], ACT.Abs, scale=2.0)
+            short = ring.tile([P, 2, count], F32, name="short")
+            for e in range(2):
+                nc.vector.tensor_tensor(short[:, e, :], picked(span, 2 * half + e, 1), twice_abs[:, e, :], ALU.subtract)
+            if half == 0:
+                wings[span] = ring.tile([P, 4, count], F32, name="wings")
+            for e in range(2):
+                t = 2 * half + e
+                nc.vector.tensor_tensor(wings[span][:, t, :], picked(span, t, 2), short[:, e, :], ALU.add)
+
+        def quantise_z(span, start, count):
+            a, first = SPANS[span][:2]
+            z_bf = ring.tile([P, count, 4], BF16, name="z_bf", bufs=3, align_bytes=64)
+            nc.scalar.activation(
+                z_bf[:].rearrange("p (g m) t -> p g t m", m=4),
+                wings[span][:, :, start : start + count].rearrange("p t (g m) -> p g t m", m=4),
+                ACT.Copy,
+                scale=-0.5,
+            )
+            trades = slice(first + start, first + start + count)
+            nc.vector.quantize_mx(
+                out=z_codes[a][:, trades].bitcast(FP8X4),
+                scales=z_sc[a][:, trades],
+                in_=z_bf[:].rearrange("p m t -> p (m t)"),
             )
 
-        def quantise_z(g):
-            c, a = divmod(g, 2)
-            m0, width = CHUNKS[c]
-            cols = slice(m0, m0 + width)
-            nc.vector.quantize_mx(out=z_codes[a][:, cols].bitcast(FP8X4), scales=z_sc[a][:, cols], in_=z_bf[g][:])
-
-        def product(bank, w_codes, w_sc, b, x_codes, x_sc, passes):
-            for a in passes:
+        def product(bank, b, w_codes, w_sc, x_codes, x_sc):
+            for a in range(2):
                 for t in range(4):
-                    cols = slice(512 * b + P * t, 512 * b + P * (t + 1))
+                    cols = slice(PASS * b + P * t, PASS * b + P * (t + 1))
                     nc.tensor.matmul_mx(
                         out=bank[:, t, :],
-                        lhsT=w_codes(a, cols).bitcast(FP8X4),
-                        lhsT_scale=w_sc(a, cols),
+                        lhsT=w_codes[a][:, cols].bitcast(FP8X4),
+                        lhsT_scale=w_sc[a][:, cols],
                         rhs=x_codes[a].bitcast(FP8X4),
                         rhs_scale=x_sc[a],
-                        start=(a == passes[0] and t == 0),
-                        stop=(a == passes[1] and t == 3),
+                        start=(a == 0 and t == 0),
+                        stop=(a == 1 and t == 3),
                     )
 
-        y_sb = {}
-        y_banks = {}
-        th = {}
-        act_codes = {}
-        act_sc = {}
-
         def second_product(u):
-            trades = slice(SUB * u, SUB * (u + 1))
+            trades = slice(BLOCK * u, BLOCK * (u + 1))
             for b in range(2):
-                bank = psum.tile([P, 4, SUB], F32, name="bank_y")
-                y_banks[u, b] = bank
+                y_bank[u, b] = psum.tile([P, 4, BLOCK], F32, name="bank_y")
                 product(
-                    bank,
-                    lambda a, cols: w2_codes[a][:, cols],
-                    lambda a, cols: w2_sc[a][:, cols],
+                    y_bank[u, b],
                     b,
+                    w2_codes,
+                    w2_sc,
                     [z_codes[a][:, trades] for a in range(2)],
                     [z_sc[a][:, trades] for a in range(2)],
-                    (0, 1) if u == 3 else (1, 0),
                 )
-                th[u, b] = ring.tile([P, SUB, 4], F32, name="th", bufs=4)
-                nc.scalar.activation(th[u, b][:], bank[:].rearrange("p t m -> p m t"), ACT.Tanh)
+                tanh_y[u, b] = ring.tile([P, BLOCK, 4], F32, name="tanh_y", bufs=4)
+                nc.scalar.activation(tanh_y[u, b][:], y_bank[u, b][:].rearrange("p t m -> p m t"), ACT.Tanh)
 
         def keep_y(u):
             for b in range(2):
-                y_sb[u, b] = ring.tile([P, 4, SUB], F32, name="y_b", bufs=4)
-                nc.scalar.copy(y_sb[u, b][:], y_banks[u, b][:])
+                y_sb[u, b] = ring.tile([P, 4, BLOCK], F32, name="y_sb", bufs=6)
+                nc.scalar.copy(y_sb[u, b][:], y_bank[u, b][:])
 
         def quantise_act(u):
-            act_bf = []
+            act_bf = [ring.tile([P, BLOCK, 4], BF16, name="act_bf", align_bytes=64) for b in range(2)]
             for b in range(2):
-                act_bf.append(ring.tile([P, SUB, 4], BF16, name="act_bf", align_bytes=64))
                 nc.vector.tensor_tensor(
-                    act_bf[b][:], th[u, b][:], gain_sb[:, b, :].unsqueeze(1).to_broadcast([P, SUB, 4]), ALU.mult
+                    act_bf[b][:], tanh_y[u, b][:], gain_sb[:, b, :].unsqueeze(1).to_broadcast([P, BLOCK, 4]), ALU.mult
                 )
             for b in range(2):
-                act_codes[u, b] = ring.tile([P, SUB], U32, name="act_codes", bufs=4, align_bytes=64)
-                act_sc[u, b] = ring.tile([P, SUB], U8, name="act_sc", bufs=4, align_bytes=64)
+                act_codes[u, b] = ring.tile([P, BLOCK], U32, name="act_codes", bufs=4, align_bytes=64)
+                act_sc[u, b] = ring.tile([P, BLOCK], U8, name="act_sc", bufs=4, align_bytes=64)
                 nc.vector.quantize_mx(
                     out=act_codes[u, b][:].bitcast(FP8X4),
                     scales=act_sc[u, b][:],
@@ -267,76 +235,49 @@ def tile_list_muni_butterfly_residual_kernel(
 
         def third_product(u):
             for b in range(2):
-                bank = psum.tile([P, 4, SUB], F32, name="bank_a", bufs=3)
+                bank = psum.tile([P, 4, BLOCK], F32, name="bank_h_out")
                 product(
                     bank,
-                    lambda a, cols: w3_codes[:, a, cols],
-                    lambda a, cols: planes[a][:, 2, cols],
                     b,
+                    [w3_codes[:, a] for a in range(2)],
+                    [scale_sb[a][:, 2] for a in range(2)],
                     [act_codes[u, a][:] for a in range(2)],
                     [act_sc[u, a][:] for a in range(2)],
-                    (0, 1),
                 )
-                result = ring.tile([P, 4, SUB], F32, name="result", bufs=4)
+                result = ring.tile([P, 4, BLOCK], F32, name="result", bufs=4)
                 nc.vector.tensor_tensor(result[:], bank[:], y_sb[u, b][:], ALU.add)
-                nc.sync.dma_start(
-                    out[512 * b : 512 * (b + 1), SUB * u : SUB * (u + 1)].rearrange("(p t) m -> p t m", t=4), result[:]
-                )
+                rows = out[PASS * b : PASS * (b + 1), BLOCK * u : BLOCK * (u + 1)]
+                nc.sync.dma_start(rows.rearrange("(p t) m -> p t m", t=4), result[:])
 
         first_product(0)
+        gather_belly(0, 0)
+        order_w3()
         first_product(1)
+        gather_belly(0, 1)
+        gather_wings(0, 0)
         first_product(2)
         first_product(3)
-        gather(0)
-        order_w3()
-        first_product(4)
-        first_product(5)
-        first_product(6)
-        first_product(7)
-        gather(1)
-        add_legs(0)
-        round_w2(0)
-        round_z(0)
-        gather(2)
-        quantise_z(0)
-        add_legs(1)
-        round_w2(1)
-        round_w2(2)
-        round_z(1)
-        gather(3)
-        quantise_z(1)
-        add_legs(2)
-        round_w2(3)
-        round_w2(4)
-        round_z(2)
-        gather(4)
-        quantise_z(2)
-        add_legs(3)
-        round_w2(5)
-        round_w2(6)
-        round_w2(7)
-        round_z(3)
-        gather(5)
-        quantise_z(3)
+        gather_belly(1, 0)
+        gather_wings(0, 1)
+        quantise_w2(0)
+        for start in (0, M // 2):
+            quantise_z(0, start, M // 2)
+        gather_belly(1, 1)
+        gather_wings(1, 0)
+        quantise_w2(1)
+        gather_belly(2, 0)
+        gather_wings(1, 1)
+        gather_belly(2, 1)
+        gather_wings(2, 0)
+        quantise_z(1, 0, BLOCK)
+        gather_wings(2, 1)
+        for u in range(1, BLOCKS - 1):
+            quantise_z(1, BLOCK * u, BLOCK)
         second_product(0)
-        keep_y(0)
-        add_legs(4)
-        quantise_act(0)
-        round_z(4)
-        second_product(1)
-        keep_y(1)
-        third_product(0)
-        quantise_z(4)
-        add_legs(5)
-        quantise_act(1)
-        second_product(2)
-        keep_y(2)
-        third_product(1)
-        round_z(5)
-        quantise_z(5)
-        quantise_act(2)
-        second_product(3)
-        keep_y(3)
-        third_product(2)
-        quantise_act(3)
-        third_product(3)
+        quantise_z(2, 0, BLOCK)
+        for u in range(BLOCKS):
+            keep_y(u)
+            if u + 1 < BLOCKS:
+                second_product(u + 1)
+            quantise_act(u)
+            third_product(u)

@@ -23,6 +23,15 @@ BLOCK = 128
 BLOCKS = M // BLOCK
 PER_COLUMN = 16
 SPANS = [(0, 0, M), (1, 0, M - BLOCK), (1, M - BLOCK, BLOCK)]
+TAB_AT = (0, 25664)
+W3_AT = 0
+GAIN_AT = 8192
+W3_SC_AT = 8256
+W2_AT = (9280, 25664)
+V_AT = (42048, 46144)
+W1_CODES_AT = 50240
+TAIL = [(BLOCK * u, BLOCK) for u in range(BLOCKS)]
+REPEATED = [(0, 0), (0, 1), (1, 0)]
 
 
 def tile_list_muni_butterfly_residual_kernel(
@@ -31,21 +40,20 @@ def tile_list_muni_butterfly_residual_kernel(
     nc = tc.nc
     with ExitStack() as ctx:
         keep = ctx.enter_context(tc.tile_pool(name="keep", bufs=1))
+        big = ctx.enter_context(tc.tile_pool(name="big", bufs=1))
         ring = ctx.enter_context(tc.tile_pool(name="ring", bufs=2))
-        psum = ctx.enter_context(tc.psum_pool(name="psum", bufs=4))
+        psum = ctx.enter_context(tc.psum_pool(name="psum", bufs=1))
 
         def kept(tag, shape, dtype):
             return keep.tile(shape, dtype, name=tag, align_bytes=64)
 
         offs_sb = kept("offs_sb", [P, S // PER_COLUMN], U16)
         pos_sb = [kept("pos_sb%d" % leg, [P, M // PER_COLUMN], U16) for leg in range(3)]
-        tab_sb = [kept("big%d" % a, [P, T], I32) for a in range(2)]
-        w1_raw = kept("w_raw", [P, 2, H // 2], I32)
-        gain_sb = kept("gain_sb", [P, 2, 4], F32)
+        w1_raw = kept("w1_raw", [P, 2, H // 2], I32)
 
         tab_sc = kept("tab_sc", [P, T], U8)
         w_sc_raw = kept("w_sc_raw", [P, 2, N], U8)
-        scale_sb = [kept("scale_sb%d" % a, [P, 3, 1024], U8) for a in range(2)]
+        scale_sb = [kept("scale_sb%d" % a, [P, 2, 1024], U8) for a in range(2)]
         for rows in (slice(32, 64), slice(64, P)):
             nc.vector.memset(tab_sc[rows].bitcast(I32), 0)
             nc.gpsimd.memset(w_sc_raw[rows].bitcast(I32), 0)
@@ -55,51 +63,72 @@ def tile_list_muni_butterfly_residual_kernel(
         nc.sync.dma_start(tab_sc[0:32].bitcast(I32), tab_scales.rearrange("a q t -> (a q) t").bitcast(I32))
         nc.sync.dma_start(w_sc_raw[0:32, 0].bitcast(I32), w1_scales.rearrange("a q c -> (a q) c").bitcast(I32))
         nc.sync.dma_start(w_sc_raw[0:32, 1].bitcast(I32), w3_scales.rearrange("a q c -> (a q) c").bitcast(I32))
-        nc.sync.dma_start(w1_raw[:], w1_words.rearrange("a p c -> p a c").bitcast(I32))
-        for a in range(2):
-            nc.sync.dma_start(tab_sb[a][:], tab_words[a].rearrange("p t i -> p (t i)").bitcast(I32))
         for leg, positions in enumerate((pos1, pos2, pos3)):
             nc.sync.dma_start(pos_sb[leg][:], positions)
-        nc.sync.dma_start(gain_sb[:], gain.rearrange("(b p t) -> p b t", b=2, t=4))
 
-        v_sc = kept("v_sc", [P, S], U8)
+        def load_table(a, first, last):
+            words = slice(T // 4 * first, T // 4 * last)
+            nc.sync.dma_start(tab_sb[a][:, words], tab_words[a].rearrange("p t i -> p (t i)").bitcast(I32)[:, words])
+
+        tab_sb = {0: big.tile([P, T], I32, name="tab_sb0", offset=TAB_AT[0])}
+        nc.sync.dma_start(tab_sb[0][:], tab_words[0].rearrange("p t i -> p (t i)").bitcast(I32))
+        nc.sync.dma_start(w1_raw[:], w1_words.rearrange("a p c -> p a c").bitcast(I32))
+
+        v_sc = big.tile([P, S], U8, name="v_sc", offset=TAB_AT[1])
         nc.vector.tensor_copy(v_sc[:], tab_sc[:].indirect(offs_sb[:]))
+        nc.vector.tensor_copy(scale_sb[0][:, 0].bitcast(I32), v_sc[:].bitcast(I32))
         nc.vector.tensor_copy(
             scale_sb[0][:, 1].bitcast(I32).rearrange("p (b t g w) -> p b g t w", b=2, t=4, w=2),
             w_sc_raw[:, 0].bitcast(I32).rearrange("p (b g t w) -> p b g t w", b=2, t=4, w=2),
         )
-        nc.vector.tensor_copy(
-            scale_sb[0][:, 2].rearrange("p (b t g m) -> p b g t m", b=2, t=4, m=16),
-            w_sc_raw[:, 1].rearrange("p (b g m t) -> p b g t m", b=2, t=4, m=16),
-        )
-        nc.vector.tensor_copy(scale_sb[0][:, 0].bitcast(I32), v_sc[:].bitcast(I32))
         moves = [(a, q) for a in range(2) for q in range(4)][1:]
+        tab_sb[1] = big.tile([P, T], I32, name="tab_sb1", offset=TAB_AT[1])
+        load_table(1, 0, 1)
         for a, q in moves:
-            queue = nc.gpsimd if (a, q) == moves[-1] else nc.scalar
+            if (a, q) == moves[4]:
+                load_table(1, 1, 3)
             row = 16 * a + 4 * q
-            queue.dma_start(scale_sb[a][32 * q : 32 * q + 4].bitcast(I32), scale_sb[0][row : row + 4].bitcast(I32))
+            nc.sync.dma_start(scale_sb[a][32 * q : 32 * q + 4].bitcast(I32), scale_sb[0][row : row + 4].bitcast(I32))
+        load_table(1, 3, 4)
 
-        w1_codes = kept("w1_codes", [P, 2, H // 2], I32)
+        w1_codes = big.tile([P, 2, H // 2], I32, name="w1_codes", offset=W1_CODES_AT, align_bytes=64)
         nc.vector.tensor_copy(
             w1_codes[:].rearrange("p a (b t g w) -> p (a b) g t w", b=2, t=4, w=4),
             w1_raw[:].rearrange("p a (b g t w) -> p (a b) g t w", b=2, t=4, w=4),
         )
-        w3_raw = kept("w_raw", [P, 2, N], I32)
-        nc.sync.dma_start(w3_raw[:], w3_words.rearrange("a p c i -> p a (c i)").bitcast(I32))
 
-        v_codes = [kept("v_codes%d" % a, [P, S], U32) for a in range(2)]
-        nc.vector.tensor_copy(v_codes[0][:], tab_sb[0][:].bitcast(U32).indirect(offs_sb[:]))
+        v_first = big.tile([P, S], U32, name="v_first", offset=V_AT[0], align_bytes=64)
+        nc.vector.tensor_copy(v_first[:], tab_sb[0][:].bitcast(U32).indirect(offs_sb[:]))
+        v_codes = {(0, half): v_first[:, BANK * half : BANK * (half + 1)] for half in range(2)}
         for half in range(2):
+            v_second = big.tile(
+                [P, BANK], U32, name="v_second%d" % half, offset=V_AT[1] + 4 * BANK * half, align_bytes=64
+            )
+            v_codes[1, half] = v_second[:]
             nc.vector.tensor_copy(
-                v_codes[1][:, BANK * half : BANK * (half + 1)],
+                v_second[:],
                 tab_sb[1][:].bitcast(U32).indirect(offs_sb[:, 32 * half : 32 * (half + 1)]),
             )
 
-        w2_raw = [kept("big%d" % a, [P, 4, N], F32) for a in range(2)]
+        w3_raw = big.tile([P, 2, N], I32, name="w3_raw", offset=W3_AT)
+        for a in range(2):
+            nc.sync.dma_start(w3_raw[:, a], w3_words[a].rearrange("p c i -> p (c i)").bitcast(I32))
+        gain_sb = big.tile([P, 2, 4], F32, name="gain_sb", offset=GAIN_AT)
+        nc.sync.dma_start(gain_sb[:], gain.rearrange("(b p t) -> p b t", b=2, t=4))
+        w2_raw = [big.tile([P, 4, N], F32, name="w2_raw%d" % a, offset=W2_AT[a]) for a in range(2)]
         for a in range(2):
             w2_rows = w2[PASS * a : PASS * (a + 1), :].rearrange("(g t i) n -> t g i n", t=4, i=8)
             for t in range(4):
                 nc.sync.dma_start(w2_raw[a][:, t, :], w2_rows[t])
+
+        w3_sc = big.tile([P, N], U8, name="w3_sc", offset=W3_SC_AT, align_bytes=64)
+        nc.vector.tensor_copy(
+            w3_sc[:].rearrange("p (b t g m) -> p b g t m", b=2, t=4, m=16),
+            w_sc_raw[:, 1].rearrange("p (b g m t) -> p b g t m", b=2, t=4, m=16),
+        )
+        for a, q in moves:
+            row, to = 16 * a + 4 * q, 32 * q + 4 * a
+            nc.sync.dma_start(w3_sc[to : to + 4].bitcast(I32), w3_sc[row : row + 4].bitcast(I32))
 
         w3_codes = kept("w3_codes", [P, 2, N], I32)
         h_sb = [kept("h_sb%d" % i, [P, S], F32) for i in range(8)]
@@ -108,69 +137,78 @@ def tile_list_muni_butterfly_residual_kernel(
         z_codes = [kept("z_codes%d" % a, [P, M], U32) for a in range(2)]
         z_sc = [kept("z_sc%d" % a, [P, M], U8) for a in range(2)]
         belly, wings, y_bank, y_sb, tanh_y, act_codes, act_sc = {}, {}, {}, {}, {}, {}, {}
+        act_bf, out_bank, twice_abs = {}, {}, {}
 
         def order_w3():
-            nc.vector.tensor_copy(
-                w3_codes[:].rearrange("p a (b t g m) -> p (a b) g t m", b=2, t=4, m=4),
-                w3_raw[:].rearrange("p a (b g m t) -> p (a b) g t m", b=2, t=4, m=4),
-            )
+            for a in range(2):
+                nc.vector.tensor_copy(
+                    w3_codes[:, a].rearrange("p (b t g m) -> p b g t m", b=2, t=4, m=4),
+                    w3_raw[:, a].rearrange("p (b g m t) -> p b g t m", b=2, t=4, m=4),
+                )
 
         def first_product(pair):
             for i in (2 * pair, 2 * pair + 1):
                 for half in range(2):
                     quotes = slice(BANK * half, BANK * (half + 1))
-                    bank = psum.tile([P, BANK], F32, name="bank_h_out")
+                    bank = psum.tile([P, BANK], F32, name="bank%d" % ((2 * i + half) % 8))
                     for a in range(2):
                         nc.tensor.matmul_mx(
                             out=bank[:],
                             lhsT=w1_codes[:, a, 64 * i : 64 * (i + 1)].bitcast(U8).bitcast(FP4X4),
                             lhsT_scale=scale_sb[a][:, 1, P * i : P * (i + 1)],
-                            rhs=v_codes[a][:, quotes].bitcast(FP8X4),
+                            rhs=v_codes[a, half].bitcast(FP8X4),
                             rhs_scale=scale_sb[a][:, 0, quotes],
                             start=(a == 0),
                             stop=(a == 1),
                         )
-                    if pair == 0 and half == 1:
-                        nc.vector.tensor_copy(h_sb[i][:, quotes], bank[:])
-                    else:
-                        nc.scalar.copy(h_sb[i][:, quotes], bank[:])
+                    nc.scalar.copy(h_sb[i][:, quotes], bank[:])
 
-        def quantise_w2(a):
-            for b in range(2):
-                cols = slice(PASS * b, PASS * (b + 1))
-                grouped = ring.tile([P, 4 * PASS], BF16, name="w2_grouped", align_bytes=64)
-                dst = grouped[:].rearrange("p (t m j) -> p m j t", t=4, j=4)
-                src = w2_raw[a][:, :, cols].rearrange("p j (m t) -> p m j t", t=4)
-                for part in (slice(0, 64), slice(64, P)):
-                    nc.scalar.copy(dst[:, part], src[:, part])
-                nc.vector.quantize_mx(out=w2_codes[a][:, cols].bitcast(FP8X4), scales=w2_sc[a][:, cols], in_=grouped[:])
+        def quantise_w2(a, b):
+            cols = slice(PASS * b, PASS * (b + 1))
+            grouped = ring.tile([P, 4 * PASS], BF16, name="w2_grouped", bufs=3, align_bytes=64)
+            dst = grouped[:].rearrange("p (t m j) -> p m j t", t=4, j=4)
+            src = w2_raw[a][:, :, cols].rearrange("p j (m t) -> p m j t", t=4)
+            for part in (slice(0, 64), slice(64, P)):
+                nc.scalar.copy(dst[:, part], src[:, part])
+            nc.vector.quantize_mx(out=w2_codes[a][:, cols].bitcast(FP8X4), scales=w2_sc[a][:, cols], in_=grouped[:])
 
-        def picked(span, t, leg):
-            a, first, count = SPANS[span]
+        def picked(i, leg, first, count):
             entries = pos_sb[leg][:, first // PER_COLUMN : (first + count) // PER_COLUMN]
-            return h_sb[4 * a + t][:].indirect(entries)
+            return h_sb[i][:].indirect(entries)
 
-        def gather_belly(span, half):
-            belly[span, half] = ring.tile([P, 2, SPANS[span][2]], F32, name="belly")
+        def gather_belly(pair):
+            belly[pair] = kept("belly%d" % pair, [P, 2, M], F32)
             for e in range(2):
-                nc.vector.tensor_copy(belly[span, half][:, e, :], picked(span, 2 * half + e, 0))
+                nc.vector.tensor_copy(belly[pair][:, e, :], picked(2 * pair + e, 0, 0, M))
+
+        def double_abs(pair):
+            twice_abs[pair] = big.tile([P, 2, M], F32, name="twice_abs%d" % pair, offset=V_AT[0] + 8 * M * pair)
+            nc.scalar.activation(twice_abs[pair][:], belly[pair][:], ACT.Abs, scale=2.0)
 
         def gather_wings(span, half):
-            count = SPANS[span][2]
-            twice_abs = ring.tile([P, 2, count], F32, name="twice_abs")
-            nc.scalar.activation(twice_abs[:], belly[span, half][:], ACT.Abs, scale=2.0)
-            short = ring.tile([P, 2, count], F32, name="short")
-            for e in range(2):
-                nc.vector.tensor_tensor(short[:, e, :], picked(span, 2 * half + e, 1), twice_abs[:, e, :], ALU.subtract)
+            a, first, count = SPANS[span]
             if half == 0:
-                wings[span] = ring.tile([P, 4, count], F32, name="wings")
+                wings[span] = kept("wings%d" % span, [P, 4, count], F32)
+            if (span, half) == (1, 1):
+                short = kept("wings0", [P, 2, count], F32)
+            elif (span, half) == (2, 0):
+                short = kept("z_first", [P, 2, count], F32)
+            else:
+                short = ring.tile([P, 2, count], F32, name="short")
+            for e in range(2):
+                i = 4 * a + 2 * half + e
+                doubled = twice_abs[i // 2][:, e, first : first + count]
+                nc.vector.tensor_tensor(short[:, e, :], picked(i, 1, first, count), doubled, ALU.subtract)
             for e in range(2):
                 t = 2 * half + e
-                nc.vector.tensor_tensor(wings[span][:, t, :], picked(span, t, 2), short[:, e, :], ALU.add)
+                nc.vector.tensor_tensor(wings[span][:, t, :], picked(4 * a + t, 2, first, count), short[:, e, :], ALU.add)
 
         def quantise_z(span, start, count):
             a, first = SPANS[span][:2]
-            z_bf = ring.tile([P, count, 4], BF16, name="z_bf", bufs=3, align_bytes=64)
+            if (span, start) == (1, 0):
+                z_bf = kept("z_first", [P, count, 4], BF16)
+            else:
+                z_bf = ring.tile([P, count, 4], BF16, name="z_bf", bufs=3, align_bytes=64)
             nc.scalar.activation(
                 z_bf[:].rearrange("p (g m) t -> p g t m", m=4),
                 wings[span][:, :, start : start + count].rearrange("p t (g m) -> p g t m", m=4),
@@ -184,100 +222,162 @@ def tile_list_muni_butterfly_residual_kernel(
                 in_=z_bf[:].rearrange("p m t -> p (m t)"),
             )
 
-        def product(bank, b, w_codes, w_sc, x_codes, x_sc):
+        def banks_of(u):
+            per_bank = BANK // TAIL[u][1]
+            return [(b, t0, per_bank) for b in range(2) for t0 in range(0, 4, per_bank)]
+
+        def product(bank, b, t0, w_codes, w_sc, x_codes, x_sc, start, stop):
+            count = bank.shape[1]
             for a in range(2):
-                for t in range(4):
-                    cols = slice(PASS * b + P * t, PASS * b + P * (t + 1))
+                for e in range(count):
+                    cols = slice(PASS * b + P * (t0 + e), PASS * b + P * (t0 + e + 1))
                     nc.tensor.matmul_mx(
-                        out=bank[:, t, :],
+                        out=bank[:, e, :],
                         lhsT=w_codes[a][:, cols].bitcast(FP8X4),
                         lhsT_scale=w_sc[a][:, cols],
                         rhs=x_codes[a].bitcast(FP8X4),
                         rhs_scale=x_sc[a],
-                        start=(a == 0 and t == 0),
-                        stop=(a == 1 and t == 3),
+                        start=(start and a == 0 and e == 0),
+                        stop=(stop and a == 1 and e == count - 1),
                     )
 
+        def z_product(bank, u, b, t0, stop):
+            trades = slice(TAIL[u][0], TAIL[u][0] + TAIL[u][1])
+            z_codes_u = [z_codes[a][:, trades] for a in range(2)]
+            product(bank, b, t0, w2_codes, w2_sc, z_codes_u, [z_sc[a][:, trades] for a in range(2)], True, stop)
+
         def second_product(u):
-            trades = slice(BLOCK * u, BLOCK * (u + 1))
-            for b in range(2):
-                y_bank[u, b] = psum.tile([P, 4, BLOCK], F32, name="bank_y")
-                product(
-                    y_bank[u, b],
-                    b,
-                    w2_codes,
-                    w2_sc,
-                    [z_codes[a][:, trades] for a in range(2)],
-                    [z_sc[a][:, trades] for a in range(2)],
-                )
-                tanh_y[u, b] = ring.tile([P, BLOCK, 4], F32, name="tanh_y", bufs=4)
-                nc.scalar.activation(tanh_y[u, b][:], y_bank[u, b][:].rearrange("p t m -> p m t"), ACT.Tanh)
+            width = TAIL[u][1]
+            for b, t0, count in banks_of(u):
+                y_bank[u, b, t0] = psum.tile([P, count, width], F32, name="bank%d" % (2 * u + b))
+                z_product(y_bank[u, b, t0], u, b, t0, True)
+                if width == BLOCK:
+                    tanh_y[u, b] = ring.tile([P, width, 4], F32, name="tanh_y", bufs=6)
+                    nc.scalar.activation(tanh_y[u, b][:], y_bank[u, b, t0][:].rearrange("p t m -> p m t"), ACT.Tanh)
+                else:
+                    tanh_y[u, b, t0] = ring.tile([P, count, width], F32, name="tanh_y", bufs=6)
+                    nc.scalar.activation(tanh_y[u, b, t0][:], y_bank[u, b, t0][:], ACT.Tanh)
+
+        def open_out(u):
+            for b, t0, count in banks_of(u):
+                if (u, b) in REPEATED:
+                    out_bank[u, b, t0] = psum.tile([P, count, TAIL[u][1]], F32, name="bank%d" % (2 * u + b))
+                    z_product(out_bank[u, b, t0], u, b, t0, False)
 
         def keep_y(u):
-            for b in range(2):
-                y_sb[u, b] = ring.tile([P, 4, BLOCK], F32, name="y_sb", bufs=6)
-                nc.scalar.copy(y_sb[u, b][:], y_bank[u, b][:])
+            for b, t0, count in banks_of(u):
+                if (u, b) not in REPEATED:
+                    y_sb[u, b, t0] = ring.tile([P, count, TAIL[u][1]], F32, name="y_sb", bufs=5)
+                    nc.scalar.copy(y_sb[u, b, t0][:], y_bank[u, b, t0][:])
 
-        def quantise_act(u):
-            act_bf = [ring.tile([P, BLOCK, 4], BF16, name="act_bf", align_bytes=64) for b in range(2)]
-            for b in range(2):
-                nc.vector.tensor_tensor(
-                    act_bf[b][:], tanh_y[u, b][:], gain_sb[:, b, :].unsqueeze(1).to_broadcast([P, BLOCK, 4]), ALU.mult
+        def gain_on_scalar(u, b):
+            width = TAIL[u][1]
+            planes = ring.tile([P, 4, width], BF16, name="act_planes")
+            for t in range(4):
+                nc.scalar.activation(
+                    planes[:, t, :], tanh_y[u, b, t - t % 2][:, t % 2, :], ACT.Copy, scale=gain_sb[:, b, t : t + 1]
                 )
-            for b in range(2):
-                act_codes[u, b] = ring.tile([P, BLOCK], U32, name="act_codes", bufs=4, align_bytes=64)
-                act_sc[u, b] = ring.tile([P, BLOCK], U8, name="act_sc", bufs=4, align_bytes=64)
-                nc.vector.quantize_mx(
-                    out=act_codes[u, b][:].bitcast(FP8X4),
-                    scales=act_sc[u, b][:],
-                    in_=act_bf[b][:].rearrange("p m t -> p (m t)"),
-                )
+            act_bf[u, b] = ring.tile([P, width, 4], BF16, name="act_bf", bufs=4, align_bytes=64)
+            nc.scalar.copy(
+                act_bf[u, b][:].rearrange("p (g m) t -> p g t m", m=4),
+                planes[:].rearrange("p t (g m) -> p g t m", m=4),
+            )
+
+        def gain_on_vector(u, b):
+            width = TAIL[u][1]
+            act_bf[u, b] = ring.tile([P, width, 4], BF16, name="act_bf", bufs=4, align_bytes=64)
+            nc.vector.tensor_tensor(
+                act_bf[u, b][:], tanh_y[u, b][:], gain_sb[:, b, :].unsqueeze(1).to_broadcast([P, width, 4]), ALU.mult
+            )
+
+        def quantise_act(u, b):
+            width = TAIL[u][1]
+            act_codes[u, b] = ring.tile([P, width], U32, name="act_codes", bufs=4, align_bytes=64)
+            act_sc[u, b] = ring.tile([P, width], U8, name="act_sc", bufs=4, align_bytes=64)
+            nc.vector.quantize_mx(
+                out=act_codes[u, b][:].bitcast(FP8X4),
+                scales=act_sc[u, b][:],
+                in_=act_bf[u, b][:].rearrange("p m t -> p (m t)"),
+            )
 
         def third_product(u):
-            for b in range(2):
-                bank = psum.tile([P, 4, BLOCK], F32, name="bank_h_out")
+            first, width = TAIL[u]
+            for b, t0, count in banks_of(u):
+                repeated = (u, b) in REPEATED
+                if not repeated:
+                    out_bank[u, b, t0] = psum.tile([P, count, width], F32, name="bank%d" % (2 * u + b))
+                bank = out_bank[u, b, t0]
                 product(
                     bank,
                     b,
+                    t0,
                     [w3_codes[:, a] for a in range(2)],
-                    [scale_sb[a][:, 2] for a in range(2)],
+                    [w3_sc[4 * a : P] for a in range(2)],
                     [act_codes[u, a][:] for a in range(2)],
                     [act_sc[u, a][:] for a in range(2)],
+                    not repeated,
+                    True,
                 )
-                result = ring.tile([P, 4, BLOCK], F32, name="result", bufs=4)
-                nc.vector.tensor_tensor(result[:], bank[:], y_sb[u, b][:], ALU.add)
-                rows = out[PASS * b : PASS * (b + 1), BLOCK * u : BLOCK * (u + 1)]
-                nc.sync.dma_start(rows.rearrange("(p t) m -> p t m", t=4), result[:])
 
-        first_product(0)
-        gather_belly(0, 0)
+        def finish(u, b):
+            first, width = TAIL[u]
+            result = ring.tile([P, 4, width], F32, name="result", bufs=8)
+            if (u, b) in REPEATED:
+                nc.scalar.copy(result[:], out_bank[u, b, 0][:])
+            else:
+                nc.vector.tensor_tensor(result[:], out_bank[u, b, 0][:], y_sb[u, b, 0][:], ALU.add)
+            rows = out[PASS * b : PASS * (b + 1), first : first + width].rearrange("(p t) m -> p t m", t=4)
+            nc.sync.dma_start(rows, result[:])
+
+        def act(u):
+            for b in range(2):
+                gain_on_vector(u, b)
+            for b in range(2):
+                quantise_act(u, b)
+
         order_w3()
-        first_product(1)
-        gather_belly(0, 1)
-        gather_wings(0, 0)
-        first_product(2)
-        first_product(3)
-        gather_belly(1, 0)
-        gather_wings(0, 1)
-        quantise_w2(0)
+        for pair in range(4):
+            first_product(pair)
+            gather_belly(pair)
+        for pair in range(4):
+            double_abs(pair)
+        for half in range(2):
+            gather_wings(0, half)
+        for b in range(2):
+            quantise_w2(0, b)
+        gather_wings(1, 0)
+        quantise_w2(1, 0)
         for start in (0, M // 2):
             quantise_z(0, start, M // 2)
-        gather_belly(1, 1)
-        gather_wings(1, 0)
-        quantise_w2(1)
-        gather_belly(2, 0)
         gather_wings(1, 1)
-        gather_belly(2, 1)
-        gather_wings(2, 0)
-        quantise_z(1, 0, BLOCK)
-        gather_wings(2, 1)
-        for u in range(1, BLOCKS - 1):
+        quantise_w2(1, 1)
+        for u in range(BLOCKS - 1):
             quantise_z(1, BLOCK * u, BLOCK)
+        for half in range(2):
+            gather_wings(2, half)
         second_product(0)
         quantise_z(2, 0, BLOCK)
-        for u in range(BLOCKS):
-            keep_y(u)
-            if u + 1 < BLOCKS:
-                second_product(u + 1)
-            quantise_act(u)
-            third_product(u)
+        second_product(1)
+        open_out(0)
+        act(0)
+        second_product(2)
+        open_out(1)
+        keep_y(1)
+        act(1)
+        third_product(0)
+        second_product(3)
+        finish(0, 0)
+        finish(0, 1)
+        act(2)
+        third_product(1)
+        keep_y(2)
+        finish(1, 1)
+        finish(1, 0)
+        third_product(2)
+        keep_y(3)
+        finish(2, 0)
+        act(3)
+        third_product(3)
+        finish(2, 1)
+        for b in range(2):
+            finish(3, b)

@@ -185,42 +185,40 @@ def tile_list_muni_butterfly_residual_kernel(
             twice_abs[pair] = big.tile([P, 2, M], F32, name="twice_abs%d" % pair, offset=V_AT[0] + 8 * M * pair)
             nc.scalar.activation(twice_abs[pair][:], belly[pair][:], ACT.Abs, scale=2.0)
 
-        def gather_wings(span, half):
-            a, first, count = SPANS[span]
-            if half == 0:
-                wings[span] = kept("wings%d" % span, [P, 4, count], F32)
-            if (span, half) == (1, 1):
-                short = kept("wings0", [P, 2, count], F32)
-            elif (span, half) == (2, 0):
-                short = kept("z_first", [P, 2, count], F32)
-            else:
-                short = ring.tile([P, 2, count], F32, name="short")
+        def gather_wings(a, half, first, count, short):
+            trades = slice(first, first + count)
             for e in range(2):
                 i = 4 * a + 2 * half + e
-                doubled = twice_abs[i // 2][:, e, first : first + count]
-                nc.vector.tensor_tensor(short[:, e, :], picked(i, 1, first, count), doubled, ALU.subtract)
+                nc.vector.tensor_tensor(
+                    short[:, e, :], picked(i, 1, first, count), twice_abs[i // 2][:, e, trades], ALU.subtract
+                )
             for e in range(2):
                 t = 2 * half + e
-                nc.vector.tensor_tensor(wings[span][:, t, :], picked(4 * a + t, 2, first, count), short[:, e, :], ALU.add)
+                nc.vector.tensor_tensor(
+                    wings[a][:, t, trades], picked(4 * a + t, 2, first, count), short[:, e, :], ALU.add
+                )
 
-        def quantise_z(span, start, count):
-            a, first = SPANS[span][:2]
-            if (span, start) == (1, 0):
-                z_bf = kept("z_first", [P, count, 4], BF16)
-            else:
-                z_bf = ring.tile([P, count, 4], BF16, name="z_bf", bufs=3, align_bytes=64)
+        def gather_all_trades(a, half):
+            if half == 0:
+                wings[a] = kept("wings%d" % a, [P, 4, M], F32)
+            gather_wings(a, half, 0, M, ring.tile([P, 2, M], F32, name="short"))
+
+        def quantise_z(a, first, count, z_bf):
+            trades = slice(first, first + count)
             nc.scalar.activation(
                 z_bf[:].rearrange("p (g m) t -> p g t m", m=4),
-                wings[span][:, :, start : start + count].rearrange("p t (g m) -> p g t m", m=4),
+                wings[a][:, :, trades].rearrange("p t (g m) -> p g t m", m=4),
                 ACT.Copy,
                 scale=-0.5,
             )
-            trades = slice(first + start, first + start + count)
             nc.vector.quantize_mx(
                 out=z_codes[a][:, trades].bitcast(FP8X4),
                 scales=z_sc[a][:, trades],
                 in_=z_bf[:].rearrange("p m t -> p (m t)"),
             )
+
+        def z_tile(count):
+            return ring.tile([P, count, 4], BF16, name="z_bf", bufs=3, align_bytes=64)
 
         def banks_of(u):
             per_bank = BANK // TAIL[u][1]
@@ -342,21 +340,21 @@ def tile_list_muni_butterfly_residual_kernel(
         for pair in range(4):
             double_abs(pair)
         for half in range(2):
-            gather_wings(0, half)
+            gather_all_trades(0, half)
         for b in range(2):
             quantise_w2(0, b)
-        gather_wings(1, 0)
+        gather_all_trades(1, 0)
         quantise_w2(1, 0)
-        for start in (0, M // 2):
-            quantise_z(0, start, M // 2)
-        gather_wings(1, 1)
+        for first in (0, M // 2):
+            quantise_z(0, first, M // 2, z_tile(M // 2))
+        gather_wings(1, 1, 0, M - BLOCK, kept("wings0", [P, 2, M - BLOCK], F32))
         quantise_w2(1, 1)
-        for u in range(BLOCKS - 1):
-            quantise_z(1, BLOCK * u, BLOCK)
-        for half in range(2):
-            gather_wings(2, half)
+        quantise_z(1, 0, BLOCK, kept("z_first", [P, BLOCK, 4], BF16))
+        for u in (1, 2):
+            quantise_z(1, BLOCK * u, BLOCK, z_tile(BLOCK))
+        gather_wings(1, 1, M - BLOCK, BLOCK, kept("z_first", [P, 2, BLOCK], F32))
         second_product(0)
-        quantise_z(2, 0, BLOCK)
+        quantise_z(1, M - BLOCK, BLOCK, z_tile(BLOCK))
         second_product(1)
         open_out(0)
         act(0)

@@ -59,20 +59,19 @@ def tile_list_muni_butterfly_residual_kernel(
             nc.gpsimd.memset(w_sc_raw[rows].bitcast(I32), 0)
         nc.gpsimd.memset(scale_sb[1][:].bitcast(I32), 0)
 
-        nc.sync.dma_start(offs_sb[:], offs)
+        tab_sb = {0: big.tile([P, T], I32, name="tab_sb0", offset=TAB_AT[0])}
         nc.sync.dma_start(tab_sc[0:32].bitcast(I32), tab_scales.rearrange("a q t -> (a q) t").bitcast(I32))
+        nc.sync.dma_start(offs_sb[:], offs)
         nc.sync.dma_start(w_sc_raw[0:32, 0].bitcast(I32), w1_scales.rearrange("a q c -> (a q) c").bitcast(I32))
+        nc.sync.dma_start(tab_sb[0][:], tab_words[0].rearrange("p t i -> p (t i)").bitcast(I32))
         nc.sync.dma_start(w_sc_raw[0:32, 1].bitcast(I32), w3_scales.rearrange("a q c -> (a q) c").bitcast(I32))
         for leg, positions in enumerate((pos1, pos2, pos3)):
             nc.sync.dma_start(pos_sb[leg][:], positions)
+        nc.sync.dma_start(w1_raw[:], w1_words.rearrange("a p c -> p a c").bitcast(I32))
 
         def load_table(a, first, last):
             words = slice(T // 4 * first, T // 4 * last)
             nc.sync.dma_start(tab_sb[a][:, words], tab_words[a].rearrange("p t i -> p (t i)").bitcast(I32)[:, words])
-
-        tab_sb = {0: big.tile([P, T], I32, name="tab_sb0", offset=TAB_AT[0])}
-        nc.sync.dma_start(tab_sb[0][:], tab_words[0].rearrange("p t i -> p (t i)").bitcast(I32))
-        nc.sync.dma_start(w1_raw[:], w1_words.rearrange("a p c -> p a c").bitcast(I32))
 
         v_sc = big.tile([P, S], U8, name="v_sc", offset=TAB_AT[1])
         nc.vector.tensor_copy(v_sc[:], tab_sc[:].indirect(offs_sb[:]))

@@ -19,19 +19,21 @@ ACT = mybir.ActivationFunctionType
 P = 128
 PASS = 512
 BANK = 512
-BLOCK = 128
-BLOCKS = M // BLOCK
+BANKS = 8
+BATCH = 128
+BATCHES = M // BATCH
+LAST = BATCHES - 1
 PER_COLUMN = 16
-SPANS = [(0, 0, M), (1, 0, M - BLOCK), (1, M - BLOCK, BLOCK)]
-TAB_AT = (0, 25664)
+REPEATED = [(u, 0) for u in range(3)]
+
+TABLE_BYTES = 4 * T
 W3_AT = 0
-GAIN_AT = 8192
-W3_SC_AT = 8256
-W2_AT = (9280, 25664)
-V_AT = (42048, 46144)
-W1_CODES_AT = 50240
-TAIL = [(BLOCK * u, BLOCK) for u in range(BLOCKS)]
-REPEATED = [(0, 0), (0, 1), (1, 0)]
+GAIN_AT = W3_AT + 8 * N
+W3_SCALES_AT = GAIN_AT + 64
+W2_FIRST_AT = W3_SCALES_AT + N
+TABLE_AT = (0, W2_FIRST_AT + TABLE_BYTES)
+W2_AT = (W2_FIRST_AT, TABLE_AT[1])
+OPERANDS_AT = TABLE_AT[1] + TABLE_BYTES
 
 
 def tile_list_muni_butterfly_residual_kernel(
@@ -40,12 +42,15 @@ def tile_list_muni_butterfly_residual_kernel(
     nc = tc.nc
     with ExitStack() as ctx:
         keep = ctx.enter_context(tc.tile_pool(name="keep", bufs=1))
-        big = ctx.enter_context(tc.tile_pool(name="big", bufs=1))
+        placed = ctx.enter_context(tc.tile_pool(name="placed", bufs=1))
         ring = ctx.enter_context(tc.tile_pool(name="ring", bufs=2))
         psum = ctx.enter_context(tc.psum_pool(name="psum", bufs=1))
 
         def kept(tag, shape, dtype):
             return keep.tile(shape, dtype, name=tag, align_bytes=64)
+
+        def bank_tile(number, shape):
+            return psum.tile(shape, F32, name="bank%d" % number)
 
         offs_sb = kept("offs_sb", [P, S // PER_COLUMN], U16)
         pos_sb = [kept("pos_sb%d" % leg, [P, M // PER_COLUMN], U16) for leg in range(3)]
@@ -53,74 +58,80 @@ def tile_list_muni_butterfly_residual_kernel(
 
         tab_sc = kept("tab_sc", [P, T], U8)
         w_sc_raw = kept("w_sc_raw", [P, 2, N], U8)
-        scale_sb = [kept("scale_sb%d" % a, [P, 2, 1024], U8) for a in range(2)]
+        first_sc = [kept("first_sc%d" % a, [P, 2, S], U8) for a in range(2)]
         for rows in (slice(32, 64), slice(64, P)):
             nc.vector.memset(tab_sc[rows].bitcast(I32), 0)
             nc.gpsimd.memset(w_sc_raw[rows].bitcast(I32), 0)
-        nc.gpsimd.memset(scale_sb[1][:].bitcast(I32), 0)
+        nc.gpsimd.memset(first_sc[1][:].bitcast(I32), 0)
 
-        tab_sb = {0: big.tile([P, T], I32, name="tab_sb0", offset=TAB_AT[0])}
+        table = [tab_words[a].rearrange("p t i -> p (t i)").bitcast(I32) for a in range(2)]
+        tab_first = placed.tile([P, T], I32, name="tab_first", offset=TABLE_AT[0])
         nc.sync.dma_start(tab_sc[0:32].bitcast(I32), tab_scales.rearrange("a q t -> (a q) t").bitcast(I32))
         nc.sync.dma_start(offs_sb[:], offs)
         nc.sync.dma_start(w_sc_raw[0:32, 0].bitcast(I32), w1_scales.rearrange("a q c -> (a q) c").bitcast(I32))
-        nc.sync.dma_start(tab_sb[0][:], tab_words[0].rearrange("p t i -> p (t i)").bitcast(I32))
+        nc.sync.dma_start(tab_first[:], table[0])
         nc.sync.dma_start(w_sc_raw[0:32, 1].bitcast(I32), w3_scales.rearrange("a q c -> (a q) c").bitcast(I32))
         for leg, positions in enumerate((pos1, pos2, pos3)):
             nc.sync.dma_start(pos_sb[leg][:], positions)
         nc.sync.dma_start(w1_raw[:], w1_words.rearrange("a p c -> p a c").bitcast(I32))
 
-        def load_table(a, first, last):
-            words = slice(T // 4 * first, T // 4 * last)
-            nc.sync.dma_start(tab_sb[a][:, words], tab_words[a].rearrange("p t i -> p (t i)").bitcast(I32)[:, words])
-
-        v_sc = big.tile([P, S], U8, name="v_sc", offset=TAB_AT[1])
+        v_sc = placed.tile([P, S], U8, name="v_sc", offset=TABLE_AT[1])
         nc.vector.tensor_copy(v_sc[:], tab_sc[:].indirect(offs_sb[:]))
-        nc.vector.tensor_copy(scale_sb[0][:, 0].bitcast(I32), v_sc[:].bitcast(I32))
+        nc.vector.tensor_copy(first_sc[0][:, 0].bitcast(I32), v_sc[:].bitcast(I32))
         nc.vector.tensor_copy(
-            scale_sb[0][:, 1].bitcast(I32).rearrange("p (b t g w) -> p b g t w", b=2, t=4, w=2),
+            first_sc[0][:, 1].bitcast(I32).rearrange("p (b t g w) -> p b g t w", b=2, t=4, w=2),
             w_sc_raw[:, 0].bitcast(I32).rearrange("p (b g t w) -> p b g t w", b=2, t=4, w=2),
         )
-        moves = [(a, q) for a in range(2) for q in range(4)][1:]
-        tab_sb[1] = big.tile([P, T], I32, name="tab_sb1", offset=TAB_AT[1])
-        load_table(1, 0, 1)
-        for a, q in moves:
-            if (a, q) == moves[4]:
-                load_table(1, 1, 3)
-            row = 16 * a + 4 * q
-            nc.sync.dma_start(scale_sb[a][32 * q : 32 * q + 4].bitcast(I32), scale_sb[0][row : row + 4].bitcast(I32))
-        load_table(1, 3, 4)
 
-        w1_codes = big.tile([P, 2, H // 2], I32, name="w1_codes", offset=W1_CODES_AT, align_bytes=64)
+        moves = [(a, q) for a in range(2) for q in range(4)][1:]
+        tab_second = placed.tile([P, T], I32, name="tab_second", offset=TABLE_AT[1])
+
+        def load_quarters(first, last):
+            words = slice(T // 4 * first, T // 4 * last)
+            nc.sync.dma_start(tab_second[:, words], table[1][:, words])
+
+        def move_scales(some_moves):
+            for a, q in some_moves:
+                row = 16 * a + 4 * q
+                nc.sync.dma_start(
+                    first_sc[a][32 * q : 32 * q + 4].bitcast(I32), first_sc[0][row : row + 4].bitcast(I32)
+                )
+
+        load_quarters(0, 1)
+        move_scales(moves[:4])
+        load_quarters(1, 3)
+        move_scales(moves[4:])
+        load_quarters(3, 4)
+
+        w1_codes = placed.tile([P, 2, H // 2], I32, name="w1_codes", offset=OPERANDS_AT + 8 * S, align_bytes=64)
         nc.vector.tensor_copy(
             w1_codes[:].rearrange("p a (b t g w) -> p (a b) g t w", b=2, t=4, w=4),
             w1_raw[:].rearrange("p a (b g t w) -> p (a b) g t w", b=2, t=4, w=4),
         )
 
-        v_first = big.tile([P, S], U32, name="v_first", offset=V_AT[0], align_bytes=64)
-        nc.vector.tensor_copy(v_first[:], tab_sb[0][:].bitcast(U32).indirect(offs_sb[:]))
+        v_first = placed.tile([P, S], U32, name="v_first", offset=OPERANDS_AT, align_bytes=64)
+        nc.vector.tensor_copy(v_first[:], tab_first[:].bitcast(U32).indirect(offs_sb[:]))
         v_codes = {(0, half): v_first[:, BANK * half : BANK * (half + 1)] for half in range(2)}
         for half in range(2):
-            v_second = big.tile(
-                [P, BANK], U32, name="v_second%d" % half, offset=V_AT[1] + 4 * BANK * half, align_bytes=64
+            v_second = placed.tile(
+                [P, BANK], U32, name="v_second%d" % half, offset=OPERANDS_AT + 4 * (S + BANK * half), align_bytes=64
             )
             v_codes[1, half] = v_second[:]
-            nc.vector.tensor_copy(
-                v_second[:],
-                tab_sb[1][:].bitcast(U32).indirect(offs_sb[:, 32 * half : 32 * (half + 1)]),
-            )
+            entries = offs_sb[:, BANK // PER_COLUMN * half : BANK // PER_COLUMN * (half + 1)]
+            nc.vector.tensor_copy(v_second[:], tab_second[:].bitcast(U32).indirect(entries))
 
-        w3_raw = big.tile([P, 2, N], I32, name="w3_raw", offset=W3_AT)
+        w3_raw = placed.tile([P, 2, N], I32, name="w3_raw", offset=W3_AT)
         for a in range(2):
             nc.sync.dma_start(w3_raw[:, a], w3_words[a].rearrange("p c i -> p (c i)").bitcast(I32))
-        gain_sb = big.tile([P, 2, 4], F32, name="gain_sb", offset=GAIN_AT)
+        gain_sb = placed.tile([P, 2, 4], F32, name="gain_sb", offset=GAIN_AT)
         nc.sync.dma_start(gain_sb[:], gain.rearrange("(b p t) -> p b t", b=2, t=4))
-        w2_raw = [big.tile([P, 4, N], F32, name="w2_raw%d" % a, offset=W2_AT[a]) for a in range(2)]
+        w2_raw = [placed.tile([P, 4, N], F32, name="w2_raw%d" % a, offset=W2_AT[a]) for a in range(2)]
         for a in range(2):
             w2_rows = w2[PASS * a : PASS * (a + 1), :].rearrange("(g t i) n -> t g i n", t=4, i=8)
             for t in range(4):
                 nc.sync.dma_start(w2_raw[a][:, t, :], w2_rows[t])
 
-        w3_sc = big.tile([P, N], U8, name="w3_sc", offset=W3_SC_AT, align_bytes=64)
+        w3_sc = placed.tile([P, N], U8, name="w3_sc", offset=W3_SCALES_AT, align_bytes=64)
         nc.vector.tensor_copy(
             w3_sc[:].rearrange("p (b t g m) -> p b g t m", b=2, t=4, m=16),
             w_sc_raw[:, 1].rearrange("p (b g m t) -> p b g t m", b=2, t=4, m=16),
@@ -135,8 +146,8 @@ def tile_list_muni_butterfly_residual_kernel(
         w2_sc = [kept("w2_sc%d" % a, [P, N], U8) for a in range(2)]
         z_codes = [kept("z_codes%d" % a, [P, M], U32) for a in range(2)]
         z_sc = [kept("z_sc%d" % a, [P, M], U8) for a in range(2)]
-        belly, wings, y_bank, y_sb, tanh_y, act_codes, act_sc = {}, {}, {}, {}, {}, {}, {}
-        act_bf, out_bank, twice_abs = {}, {}, {}
+        belly, twice_abs, wings = {}, {}, {}
+        y_bank, y_sb, tanh_y, act_codes, act_sc, out_bank = {}, {}, {}, {}, {}, {}
 
         def order_w3():
             for a in range(2):
@@ -149,14 +160,14 @@ def tile_list_muni_butterfly_residual_kernel(
             for i in (2 * pair, 2 * pair + 1):
                 for half in range(2):
                     quotes = slice(BANK * half, BANK * (half + 1))
-                    bank = psum.tile([P, BANK], F32, name="bank%d" % ((2 * i + half) % 8))
+                    bank = bank_tile((2 * i + half) % BANKS, [P, BANK])
                     for a in range(2):
                         nc.tensor.matmul_mx(
                             out=bank[:],
                             lhsT=w1_codes[:, a, 64 * i : 64 * (i + 1)].bitcast(U8).bitcast(FP4X4),
-                            lhsT_scale=scale_sb[a][:, 1, P * i : P * (i + 1)],
+                            lhsT_scale=first_sc[a][:, 1, P * i : P * (i + 1)],
                             rhs=v_codes[a, half].bitcast(FP8X4),
-                            rhs_scale=scale_sb[a][:, 0, quotes],
+                            rhs_scale=first_sc[a][:, 0, quotes],
                             start=(a == 0),
                             stop=(a == 1),
                         )
@@ -171,143 +182,118 @@ def tile_list_muni_butterfly_residual_kernel(
                 nc.scalar.copy(dst[:, part], src[:, part])
             nc.vector.quantize_mx(out=w2_codes[a][:, cols].bitcast(FP8X4), scales=w2_sc[a][:, cols], in_=grouped[:])
 
-        def picked(i, leg, first, count):
-            entries = pos_sb[leg][:, first // PER_COLUMN : (first + count) // PER_COLUMN]
+        def picked(i, leg, trades):
+            entries = pos_sb[leg][:, trades.start // PER_COLUMN : trades.stop // PER_COLUMN]
             return h_sb[i][:].indirect(entries)
 
         def gather_belly(pair):
             belly[pair] = kept("belly%d" % pair, [P, 2, M], F32)
             for e in range(2):
-                nc.vector.tensor_copy(belly[pair][:, e, :], picked(2 * pair + e, 0, 0, M))
+                nc.vector.tensor_copy(belly[pair][:, e, :], picked(2 * pair + e, 0, slice(0, M)))
 
         def double_abs(pair):
-            twice_abs[pair] = big.tile([P, 2, M], F32, name="twice_abs%d" % pair, offset=V_AT[0] + 8 * M * pair)
+            twice_abs[pair] = placed.tile(
+                [P, 2, M], F32, name="twice_abs%d" % pair, offset=OPERANDS_AT + 4 * S * pair
+            )
             nc.scalar.activation(twice_abs[pair][:], belly[pair][:], ACT.Abs, scale=2.0)
 
-        def gather_wings(a, half, first, count, short):
-            trades = slice(first, first + count)
+        def gather_wings(pair, trades, short):
             for e in range(2):
-                i = 4 * a + 2 * half + e
                 nc.vector.tensor_tensor(
-                    short[:, e, :], picked(i, 1, first, count), twice_abs[i // 2][:, e, trades], ALU.subtract
+                    short[:, e, :], picked(2 * pair + e, 1, trades), twice_abs[pair][:, e, trades], ALU.subtract
                 )
             for e in range(2):
-                t = 2 * half + e
+                a, t = divmod(2 * pair + e, 4)
                 nc.vector.tensor_tensor(
-                    wings[a][:, t, trades], picked(4 * a + t, 2, first, count), short[:, e, :], ALU.add
+                    wings[a][:, t, trades], picked(2 * pair + e, 2, trades), short[:, e, :], ALU.add
                 )
 
-        def gather_all_trades(a, half):
-            if half == 0:
-                wings[a] = kept("wings%d" % a, [P, 4, M], F32)
-            gather_wings(a, half, 0, M, ring.tile([P, 2, M], F32, name="short"))
+        def gather_all_wings(pair):
+            if pair % 2 == 0:
+                wings[pair // 2] = kept("wings%d" % (pair // 2), [P, 4, M], F32)
+            gather_wings(pair, slice(0, M), ring.tile([P, 2, M], F32, name="short"))
 
-        def quantise_z(a, first, count, z_bf):
-            trades = slice(first, first + count)
-            nc.scalar.activation(
+        def z_views(a, trades, z_bf):
+            return (
                 z_bf[:].rearrange("p (g m) t -> p g t m", m=4),
                 wings[a][:, :, trades].rearrange("p t (g m) -> p g t m", m=4),
-                ACT.Copy,
-                scale=-0.5,
             )
+
+        def quantise_rounded_z(a, trades, z_bf):
             nc.vector.quantize_mx(
                 out=z_codes[a][:, trades].bitcast(FP8X4),
                 scales=z_sc[a][:, trades],
                 in_=z_bf[:].rearrange("p m t -> p (m t)"),
             )
 
+        def quantise_z(a, trades, z_bf):
+            dst, src = z_views(a, trades, z_bf)
+            nc.scalar.activation(dst, src, ACT.Copy, scale=-0.5)
+            quantise_rounded_z(a, trades, z_bf)
+
         def z_tile(count):
             return ring.tile([P, count, 4], BF16, name="z_bf", bufs=3, align_bytes=64)
 
-        def banks_of(u):
-            per_bank = BANK // TAIL[u][1]
-            return [(b, t0, per_bank) for b in range(2) for t0 in range(0, 4, per_bank)]
+        def batch(u):
+            return slice(BATCH * u, BATCH * (u + 1))
 
-        def product(bank, b, t0, w_codes, w_sc, x_codes, x_sc, start, stop):
-            count = bank.shape[1]
+        def product(bank, b, w_codes, w_sc, x_codes, x_sc, start, stop):
             for a in range(2):
-                for e in range(count):
-                    cols = slice(PASS * b + P * (t0 + e), PASS * b + P * (t0 + e + 1))
+                for t in range(4):
+                    cols = slice(PASS * b + P * t, PASS * b + P * (t + 1))
                     nc.tensor.matmul_mx(
-                        out=bank[:, e, :],
+                        out=bank[:, t, :],
                         lhsT=w_codes[a][:, cols].bitcast(FP8X4),
                         lhsT_scale=w_sc[a][:, cols],
                         rhs=x_codes[a].bitcast(FP8X4),
                         rhs_scale=x_sc[a],
-                        start=(start and a == 0 and e == 0),
-                        stop=(stop and a == 1 and e == count - 1),
+                        start=(start and a == 0 and t == 0),
+                        stop=(stop and a == 1 and t == 3),
                     )
 
-        def z_product(bank, u, b, t0, stop):
-            trades = slice(TAIL[u][0], TAIL[u][0] + TAIL[u][1])
-            z_codes_u = [z_codes[a][:, trades] for a in range(2)]
-            product(bank, b, t0, w2_codes, w2_sc, z_codes_u, [z_sc[a][:, trades] for a in range(2)], True, stop)
+        def z_product(u, b, stop):
+            bank = bank_tile(2 * u + b, [P, 4, BATCH])
+            x_codes = [z_codes[a][:, batch(u)] for a in range(2)]
+            product(bank, b, w2_codes, w2_sc, x_codes, [z_sc[a][:, batch(u)] for a in range(2)], True, stop)
+            return bank
 
         def second_product(u):
-            width = TAIL[u][1]
-            for b, t0, count in banks_of(u):
-                y_bank[u, b, t0] = psum.tile([P, count, width], F32, name="bank%d" % (2 * u + b))
-                z_product(y_bank[u, b, t0], u, b, t0, True)
-                if width == BLOCK:
-                    tanh_y[u, b] = ring.tile([P, width, 4], F32, name="tanh_y", bufs=6)
-                    nc.scalar.activation(tanh_y[u, b][:], y_bank[u, b, t0][:].rearrange("p t m -> p m t"), ACT.Tanh)
-                else:
-                    tanh_y[u, b, t0] = ring.tile([P, count, width], F32, name="tanh_y", bufs=6)
-                    nc.scalar.activation(tanh_y[u, b, t0][:], y_bank[u, b, t0][:], ACT.Tanh)
+            for b in range(2):
+                y_bank[u, b] = z_product(u, b, True)
+                tanh_y[u, b] = ring.tile([P, BATCH, 4], F32, name="tanh_y", bufs=6)
+                nc.scalar.activation(tanh_y[u, b][:], y_bank[u, b][:].rearrange("p t m -> p m t"), ACT.Tanh)
 
-        def open_out(u):
-            for b, t0, count in banks_of(u):
+        def keep_residual(u):
+            for b in range(2):
                 if (u, b) in REPEATED:
-                    out_bank[u, b, t0] = psum.tile([P, count, TAIL[u][1]], F32, name="bank%d" % (2 * u + b))
-                    z_product(out_bank[u, b, t0], u, b, t0, False)
+                    out_bank[u, b] = z_product(u, b, False)
+                else:
+                    y_sb[u, b] = ring.tile([P, 4, BATCH], F32, name="y_sb", bufs=5)
+                    nc.scalar.copy(y_sb[u, b][:], y_bank[u, b][:])
 
-        def keep_y(u):
-            for b, t0, count in banks_of(u):
-                if (u, b) not in REPEATED:
-                    y_sb[u, b, t0] = ring.tile([P, count, TAIL[u][1]], F32, name="y_sb", bufs=5)
-                    nc.scalar.copy(y_sb[u, b, t0][:], y_bank[u, b, t0][:])
-
-        def gain_on_scalar(u, b):
-            width = TAIL[u][1]
-            planes = ring.tile([P, 4, width], BF16, name="act_planes")
-            for t in range(4):
-                nc.scalar.activation(
-                    planes[:, t, :], tanh_y[u, b, t - t % 2][:, t % 2, :], ACT.Copy, scale=gain_sb[:, b, t : t + 1]
+        def quantise_act(u):
+            act_bf = [ring.tile([P, BATCH, 4], BF16, name="act_bf", bufs=4, align_bytes=64) for b in range(2)]
+            for b in range(2):
+                nc.vector.tensor_tensor(
+                    act_bf[b][:], tanh_y[u, b][:], gain_sb[:, b, :].unsqueeze(1).to_broadcast([P, BATCH, 4]), ALU.mult
                 )
-            act_bf[u, b] = ring.tile([P, width, 4], BF16, name="act_bf", bufs=4, align_bytes=64)
-            nc.scalar.copy(
-                act_bf[u, b][:].rearrange("p (g m) t -> p g t m", m=4),
-                planes[:].rearrange("p t (g m) -> p g t m", m=4),
-            )
-
-        def gain_on_vector(u, b):
-            width = TAIL[u][1]
-            act_bf[u, b] = ring.tile([P, width, 4], BF16, name="act_bf", bufs=4, align_bytes=64)
-            nc.vector.tensor_tensor(
-                act_bf[u, b][:], tanh_y[u, b][:], gain_sb[:, b, :].unsqueeze(1).to_broadcast([P, width, 4]), ALU.mult
-            )
-
-        def quantise_act(u, b):
-            width = TAIL[u][1]
-            act_codes[u, b] = ring.tile([P, width], U32, name="act_codes", bufs=4, align_bytes=64)
-            act_sc[u, b] = ring.tile([P, width], U8, name="act_sc", bufs=4, align_bytes=64)
-            nc.vector.quantize_mx(
-                out=act_codes[u, b][:].bitcast(FP8X4),
-                scales=act_sc[u, b][:],
-                in_=act_bf[u, b][:].rearrange("p m t -> p (m t)"),
-            )
+            for b in range(2):
+                act_codes[u, b] = ring.tile([P, BATCH], U32, name="act_codes", bufs=4, align_bytes=64)
+                act_sc[u, b] = ring.tile([P, BATCH], U8, name="act_sc", bufs=4, align_bytes=64)
+                nc.vector.quantize_mx(
+                    out=act_codes[u, b][:].bitcast(FP8X4),
+                    scales=act_sc[u, b][:],
+                    in_=act_bf[b][:].rearrange("p m t -> p (m t)"),
+                )
 
         def third_product(u):
-            first, width = TAIL[u]
-            for b, t0, count in banks_of(u):
+            for b in range(2):
                 repeated = (u, b) in REPEATED
                 if not repeated:
-                    out_bank[u, b, t0] = psum.tile([P, count, width], F32, name="bank%d" % (2 * u + b))
-                bank = out_bank[u, b, t0]
+                    out_bank[u, b] = bank_tile(2 * u + b, [P, 4, BATCH])
                 product(
-                    bank,
+                    out_bank[u, b],
                     b,
-                    t0,
                     [w3_codes[:, a] for a in range(2)],
                     [w3_sc[4 * a : P] for a in range(2)],
                     [act_codes[u, a][:] for a in range(2)],
@@ -316,21 +302,15 @@ def tile_list_muni_butterfly_residual_kernel(
                     True,
                 )
 
-        def finish(u, b):
-            first, width = TAIL[u]
-            result = ring.tile([P, 4, width], F32, name="result", bufs=8)
-            if (u, b) in REPEATED:
-                nc.scalar.copy(result[:], out_bank[u, b, 0][:])
-            else:
-                nc.vector.tensor_tensor(result[:], out_bank[u, b, 0][:], y_sb[u, b, 0][:], ALU.add)
-            rows = out[PASS * b : PASS * (b + 1), first : first + width].rearrange("(p t) m -> p t m", t=4)
-            nc.sync.dma_start(rows, result[:])
-
-        def act(u):
+        def finish(u):
             for b in range(2):
-                gain_on_vector(u, b)
-            for b in range(2):
-                quantise_act(u, b)
+                result = ring.tile([P, 4, BATCH], F32, name="result", bufs=2 * BATCHES)
+                if (u, b) in REPEATED:
+                    nc.scalar.copy(result[:], out_bank[u, b][:])
+                else:
+                    nc.vector.tensor_tensor(result[:], out_bank[u, b][:], y_sb[u, b][:], ALU.add)
+                rows = out[PASS * b : PASS * (b + 1), batch(u)]
+                nc.sync.dma_start(rows.rearrange("(p t) m -> p t m", t=4), result[:])
 
         order_w3()
         for pair in range(4):
@@ -338,43 +318,30 @@ def tile_list_muni_butterfly_residual_kernel(
             gather_belly(pair)
         for pair in range(4):
             double_abs(pair)
-        for half in range(2):
-            gather_all_trades(0, half)
+        for pair in range(2):
+            gather_all_wings(pair)
         for b in range(2):
             quantise_w2(0, b)
-        gather_all_trades(1, 0)
+        gather_all_wings(2)
         quantise_w2(1, 0)
         for first in (0, M // 2):
-            quantise_z(0, first, M // 2, z_tile(M // 2))
-        gather_wings(1, 1, 0, M - BLOCK, kept("wings0", [P, 2, M - BLOCK], F32))
+            quantise_z(0, slice(first, first + M // 2), z_tile(M // 2))
+        gather_wings(3, slice(0, M - BATCH), kept("wings0", [P, 2, M - BATCH], F32))
         quantise_w2(1, 1)
-        quantise_z(1, 0, BLOCK, kept("z_first", [P, BLOCK, 4], BF16))
-        for u in (1, 2):
-            quantise_z(1, BLOCK * u, BLOCK, z_tile(BLOCK))
-        gather_wings(1, 1, M - BLOCK, BLOCK, kept("z_first", [P, 2, BLOCK], F32))
+        quantise_z(1, batch(0), kept("z_first", [P, BATCH, 4], BF16))
+        for u in range(1, LAST):
+            quantise_z(1, batch(u), z_tile(BATCH))
+        gather_wings(3, batch(LAST), kept("z_first", [P, 2, BATCH], F32))
         second_product(0)
-        quantise_z(1, M - BLOCK, BLOCK, z_tile(BLOCK))
+        z_last = z_tile(BATCH)
+        dst, src = z_views(1, batch(LAST), z_last)
+        nc.vector.tensor_scalar(dst, src, -0.5, None, ALU.mult)
+        quantise_rounded_z(1, batch(LAST), z_last)
         second_product(1)
-        open_out(0)
-        act(0)
-        second_product(2)
-        open_out(1)
-        keep_y(1)
-        act(1)
-        third_product(0)
-        second_product(3)
-        finish(0, 0)
-        finish(0, 1)
-        act(2)
-        third_product(1)
-        keep_y(2)
-        finish(1, 1)
-        finish(1, 0)
-        third_product(2)
-        keep_y(3)
-        finish(2, 0)
-        act(3)
-        third_product(3)
-        finish(2, 1)
-        for b in range(2):
-            finish(3, b)
+        for u in range(BATCHES):
+            keep_residual(u)
+            if u + 2 < BATCHES:
+                second_product(u + 2)
+            quantise_act(u)
+            third_product(u)
+            finish(u)

@@ -305,12 +305,15 @@ def tile_list_muni_butterfly_residual_kernel(
         def finish(u):
             for b in range(2):
                 result = ring.tile([P, 4, BATCH], F32, name="result", bufs=2 * BATCHES)
-                if (u, b) in REPEATED:
+                if (u, b) in REPEATED and u == LAST - 1:
+                    nc.vector.tensor_copy(result[:], out_bank[u, b][:])
+                elif (u, b) in REPEATED:
                     nc.scalar.copy(result[:], out_bank[u, b][:])
                 else:
                     nc.vector.tensor_tensor(result[:], out_bank[u, b][:], y_sb[u, b][:], ALU.add)
                 rows = out[PASS * b : PASS * (b + 1), batch(u)]
-                nc.sync.dma_start(rows.rearrange("(p t) m -> p t m", t=4), result[:])
+                queue = nc.scalar if u >= LAST - 1 and b == 1 else nc.sync
+                queue.dma_start(rows.rearrange("(p t) m -> p t m", t=4), result[:])
 
         order_w3()
         for pair in range(4):
@@ -344,4 +347,7 @@ def tile_list_muni_butterfly_residual_kernel(
                 second_product(u + 2)
             quantise_act(u)
             third_product(u)
-            finish(u)
+            if u < LAST - 1:
+                finish(u)
+        finish(LAST - 1)
+        finish(LAST)

@@ -27,7 +27,8 @@ PER_COLUMN = 16
 REPEATED = [(u, 0) for u in range(3)]
 
 TABLE_BYTES = 4 * T
-W3_AT = 0
+W1_SECOND_AT = 0
+W3_AT = W1_SECOND_AT + 2 * H
 GAIN_AT = W3_AT + 8 * N
 W3_SCALES_AT = GAIN_AT + 64
 W2_FIRST_AT = W3_SCALES_AT + N
@@ -54,7 +55,6 @@ def tile_list_muni_butterfly_residual_kernel(
 
         offs_sb = kept("offs_sb", [P, S // PER_COLUMN], U16)
         pos_sb = [kept("pos_sb%d" % leg, [P, M // PER_COLUMN], U16) for leg in range(3)]
-        w1_raw = kept("w1_raw", [P, 2, H // 2], I32)
 
         tab_sc = kept("tab_sc", [P, T], U8)
         w_sc_raw = kept("w_sc_raw", [P, 2, N], U8)
@@ -73,7 +73,9 @@ def tile_list_muni_butterfly_residual_kernel(
         nc.sync.dma_start(w_sc_raw[0:32, 1].bitcast(I32), w3_scales.rearrange("a q c -> (a q) c").bitcast(I32))
         for leg, positions in enumerate((pos1, pos2, pos3)):
             nc.sync.dma_start(pos_sb[leg][:], positions)
-        nc.sync.dma_start(w1_raw[:], w1_words.rearrange("a p c -> p a c").bitcast(I32))
+        w1_groups = w1_words.rearrange("a p (b c) -> b p a c", b=2)
+        w1_raw = {0: kept("w1_first", [P, 2, H // 4], I32)}
+        nc.sync.dma_start(w1_raw[0][:], w1_groups[0].bitcast(I32))
 
         v_sc = placed.tile([P, S], U8, name="v_sc", offset=TABLE_AT[1])
         nc.vector.tensor_copy(v_sc[:], tab_sc[:].indirect(offs_sb[:]))
@@ -103,11 +105,18 @@ def tile_list_muni_butterfly_residual_kernel(
         move_scales(moves[4:])
         load_quarters(3, 4)
 
-        w1_codes = placed.tile([P, 2, H // 2], I32, name="w1_codes", offset=OPERANDS_AT + 8 * S, align_bytes=64)
-        nc.vector.tensor_copy(
-            w1_codes[:].rearrange("p a (b t g w) -> p (a b) g t w", b=2, t=4, w=4),
-            w1_raw[:].rearrange("p a (b g t w) -> p (a b) g t w", b=2, t=4, w=4),
-        )
+        w1_codes = [
+            placed.tile([P, 2, H // 4], I32, name="w1_codes%d" % b, offset=OPERANDS_AT + (8 + 2 * b) * S, align_bytes=64)
+            for b in range(2)
+        ]
+
+        def order_w1(b, engine):
+            engine.tensor_copy(
+                w1_codes[b][:].rearrange("p a (t g w) -> p a t g w", t=4, w=4),
+                w1_raw[b][:].rearrange("p a (g t w) -> p a t g w", t=4, w=4),
+            )
+
+        order_w1(0, nc.vector)
 
         v_first = placed.tile([P, S], U32, name="v_first", offset=OPERANDS_AT, align_bytes=64)
         nc.vector.tensor_copy(v_first[:], tab_first[:].bitcast(U32).indirect(offs_sb[:]))
@@ -120,6 +129,9 @@ def tile_list_muni_butterfly_residual_kernel(
             entries = offs_sb[:, BANK // PER_COLUMN * half : BANK // PER_COLUMN * (half + 1)]
             nc.vector.tensor_copy(v_second[:], tab_second[:].bitcast(U32).indirect(entries))
 
+        w1_raw[1] = placed.tile([P, 2, H // 4], I32, name="w1_second", offset=W1_SECOND_AT)
+        nc.sync.dma_start(w1_raw[1][:], w1_groups[1].bitcast(I32))
+        order_w1(1, nc.gpsimd)
         w3_raw = placed.tile([P, 2, N], I32, name="w3_raw", offset=W3_AT)
         for a in range(2):
             nc.sync.dma_start(w3_raw[:, a], w3_words[a].rearrange("p c i -> p (c i)").bitcast(I32))
@@ -164,7 +176,7 @@ def tile_list_muni_butterfly_residual_kernel(
                     for a in range(2):
                         nc.tensor.matmul_mx(
                             out=bank[:],
-                            lhsT=w1_codes[:, a, 64 * i : 64 * (i + 1)].bitcast(U8).bitcast(FP4X4),
+                            lhsT=w1_codes[i // 4][:, a, 64 * (i % 4) : 64 * (i % 4 + 1)].bitcast(U8).bitcast(FP4X4),
                             lhsT_scale=first_sc[a][:, 1, P * i : P * (i + 1)],
                             rhs=v_codes[a, half].bitcast(FP8X4),
                             rhs_scale=first_sc[a][:, 0, quotes],

@@ -69,13 +69,13 @@ def tile_list_muni_butterfly_residual_kernel(
         nc.sync.dma_start(tab_sc[0:32].bitcast(I32), tab_scales.rearrange("a q t -> (a q) t").bitcast(I32))
         nc.sync.dma_start(offs_sb[:], offs)
         nc.sync.dma_start(w_sc_raw[0:32, 0].bitcast(I32), w1_scales.rearrange("a q c -> (a q) c").bitcast(I32))
+        w1_groups = w1_words.rearrange("a p (b c) -> b p a c", b=2)
+        w1_raw = {0: kept("w1_first", [P, 2, H // 4], I32)}
+        nc.sync.dma_start(w1_raw[0][:], w1_groups[0].bitcast(I32))
         nc.sync.dma_start(tab_first[:], table[0])
         nc.sync.dma_start(w_sc_raw[0:32, 1].bitcast(I32), w3_scales.rearrange("a q c -> (a q) c").bitcast(I32))
         for leg, positions in enumerate((pos1, pos2, pos3)):
             nc.sync.dma_start(pos_sb[leg][:], positions)
-        w1_groups = w1_words.rearrange("a p (b c) -> b p a c", b=2)
-        w1_raw = {0: kept("w1_first", [P, 2, H // 4], I32)}
-        nc.sync.dma_start(w1_raw[0][:], w1_groups[0].bitcast(I32))
 
         v_sc = placed.tile([P, S], U8, name="v_sc", offset=TABLE_AT[1])
         nc.vector.tensor_copy(v_sc[:], tab_sc[:].indirect(offs_sb[:]))
@@ -99,11 +99,10 @@ def tile_list_muni_butterfly_residual_kernel(
                     first_sc[a][32 * q : 32 * q + 4].bitcast(I32), first_sc[0][row : row + 4].bitcast(I32)
                 )
 
-        load_quarters(0, 1)
-        move_scales(moves[:4])
-        load_quarters(1, 3)
-        move_scales(moves[4:])
-        load_quarters(3, 4)
+        load_quarters(0, 2)
+        move_scales(moves[:3])
+        load_quarters(2, 4)
+        move_scales(moves[3:])
 
         w1_codes = [
             placed.tile([P, 2, H // 4], I32, name="w1_codes%d" % b, offset=OPERANDS_AT + (8 + 2 * b) * S, align_bytes=64)
@@ -129,12 +128,12 @@ def tile_list_muni_butterfly_residual_kernel(
             entries = offs_sb[:, BANK // PER_COLUMN * half : BANK // PER_COLUMN * (half + 1)]
             nc.vector.tensor_copy(v_second[:], tab_second[:].bitcast(U32).indirect(entries))
 
-        w1_raw[1] = placed.tile([P, 2, H // 4], I32, name="w1_second", offset=W1_SECOND_AT)
-        nc.sync.dma_start(w1_raw[1][:], w1_groups[1].bitcast(I32))
-        order_w1(1, nc.gpsimd)
         w3_raw = placed.tile([P, 2, N], I32, name="w3_raw", offset=W3_AT)
         for a in range(2):
             nc.sync.dma_start(w3_raw[:, a], w3_words[a].rearrange("p c i -> p (c i)").bitcast(I32))
+        w1_raw[1] = placed.tile([P, 2, H // 4], I32, name="w1_second", offset=W1_SECOND_AT)
+        nc.sync.dma_start(w1_raw[1][:], w1_groups[1].bitcast(I32))
+        order_w1(1, nc.gpsimd)
         gain_sb = placed.tile([P, 2, 4], F32, name="gain_sb", offset=GAIN_AT)
         nc.sync.dma_start(gain_sb[:], gain.rearrange("(b p t) -> p b t", b=2, t=4))
         w2_raw = [placed.tile([P, 4, N], F32, name="w2_raw%d" % a, offset=W2_AT[a]) for a in range(2)]
@@ -205,7 +204,7 @@ def tile_list_muni_butterfly_residual_kernel(
 
         def double_abs(pair):
             twice_abs[pair] = placed.tile(
-                [P, 2, M], F32, name="twice_abs%d" % pair, offset=OPERANDS_AT + 4 * S * pair
+                [P, 2, M], F32, name="twice_abs%d" % pair, offset=OPERANDS_AT + 4 * S * ((pair + 3) % 4)
             )
             nc.scalar.activation(twice_abs[pair][:], belly[pair][:], ACT.Abs, scale=2.0)
 
@@ -328,15 +327,21 @@ def tile_list_muni_butterfly_residual_kernel(
                 queue.dma_start(rows.rearrange("(p t) m -> p t m", t=4), result[:])
 
         order_w3()
-        for pair in range(4):
+        for pair in range(2):
             first_product(pair)
             gather_belly(pair)
-        for pair in range(4):
+        double_abs(0)
+        for pair in range(2, 4):
+            first_product(pair)
+        gather_all_wings(0)
+        for pair in range(2, 4):
+            gather_belly(pair)
+        double_abs(1)
+        gather_all_wings(1)
+        quantise_w2(0, 0)
+        for pair in range(2, 4):
             double_abs(pair)
-        for pair in range(2):
-            gather_all_wings(pair)
-        for b in range(2):
-            quantise_w2(0, b)
+        quantise_w2(0, 1)
         gather_all_wings(2)
         quantise_w2(1, 0)
         for first in (0, M // 2):

@@ -23,6 +23,7 @@ BANKS = 8
 BATCH = 128
 BATCHES = M // BATCH
 LAST = BATCHES - 1
+ROWS_AT = 96
 PER_COLUMN = 16
 REPEATED = [(u, 0) for u in range(3)]
 
@@ -59,33 +60,32 @@ def tile_list_muni_butterfly_residual_kernel(
         tab_sc = kept("tab_sc", [P, T], U8)
         w_sc_raw = kept("w_sc_raw", [P, 2, N], U8)
         first_sc = [kept("first_sc%d" % a, [P, 2, S], U8) for a in range(2)]
-        for rows in (slice(32, 64), slice(64, P)):
-            nc.vector.memset(tab_sc[rows].bitcast(I32), 0)
-            nc.gpsimd.memset(w_sc_raw[rows].bitcast(I32), 0)
-        nc.gpsimd.memset(first_sc[1][:].bitcast(I32), 0)
+        nc.vector.memset(tab_sc[0:ROWS_AT].bitcast(I32), 0)
+        nc.vector.memset(w_sc_raw[0:ROWS_AT].bitcast(I32), 0)
+        nc.vector.memset(first_sc[0][:].bitcast(I32), 0)
 
         table = [tab_words[a].rearrange("p t i -> p (t i)").bitcast(I32) for a in range(2)]
         tab_first = placed.tile([P, T], I32, name="tab_first", offset=TABLE_AT[0])
-        nc.sync.dma_start(tab_sc[0:32].bitcast(I32), tab_scales.rearrange("a q t -> (a q) t").bitcast(I32))
+        nc.sync.dma_start(tab_sc[ROWS_AT:P].bitcast(I32), tab_scales.rearrange("a q t -> (a q) t").bitcast(I32))
         nc.sync.dma_start(offs_sb[:], offs)
-        nc.sync.dma_start(w_sc_raw[0:32, 0].bitcast(I32), w1_scales.rearrange("a q c -> (a q) c").bitcast(I32))
+        nc.sync.dma_start(w_sc_raw[ROWS_AT:P, 0].bitcast(I32), w1_scales.rearrange("a q c -> (a q) c").bitcast(I32))
         w1_groups = w1_words.rearrange("a p (b c) -> b p a c", b=2)
         w1_raw = {0: kept("w1_first", [P, 2, H // 4], I32)}
         nc.sync.dma_start(w1_raw[0][:], w1_groups[0].bitcast(I32))
         nc.sync.dma_start(tab_first[:], table[0])
-        nc.sync.dma_start(w_sc_raw[0:32, 1].bitcast(I32), w3_scales.rearrange("a q c -> (a q) c").bitcast(I32))
+        nc.sync.dma_start(w_sc_raw[ROWS_AT:P, 1].bitcast(I32), w3_scales.rearrange("a q c -> (a q) c").bitcast(I32))
         for leg, positions in enumerate((pos1, pos2, pos3)):
             nc.sync.dma_start(pos_sb[leg][:], positions)
 
         v_sc = placed.tile([P, S], U8, name="v_sc", offset=TABLE_AT[1])
         nc.vector.tensor_copy(v_sc[:], tab_sc[:].indirect(offs_sb[:]))
-        nc.vector.tensor_copy(first_sc[0][:, 0].bitcast(I32), v_sc[:].bitcast(I32))
+        nc.vector.tensor_copy(first_sc[1][:, 0].bitcast(I32), v_sc[:].bitcast(I32))
         nc.vector.tensor_copy(
-            first_sc[0][:, 1].bitcast(I32).rearrange("p (b t g w) -> p b g t w", b=2, t=4, w=2),
+            first_sc[1][:, 1].bitcast(I32).rearrange("p (b t g w) -> p b g t w", b=2, t=4, w=2),
             w_sc_raw[:, 0].bitcast(I32).rearrange("p (b g t w) -> p b g t w", b=2, t=4, w=2),
         )
 
-        moves = [(a, q) for a in range(2) for q in range(4)][1:]
+        moves = [(a, q) for a in range(2) for q in range(4)]
         tab_second = placed.tile([P, T], I32, name="tab_second", offset=TABLE_AT[1])
 
         def load_quarters(first, last):
@@ -94,15 +94,15 @@ def tile_list_muni_butterfly_residual_kernel(
 
         def move_scales(some_moves):
             for a, q in some_moves:
-                row = 16 * a + 4 * q
+                row = ROWS_AT + 16 * a + 4 * q
                 nc.sync.dma_start(
-                    first_sc[a][32 * q : 32 * q + 4].bitcast(I32), first_sc[0][row : row + 4].bitcast(I32)
+                    first_sc[a][32 * q : 32 * q + 4].bitcast(I32), first_sc[1][row : row + 4].bitcast(I32)
                 )
 
         load_quarters(0, 2)
-        move_scales(moves[:3])
+        move_scales(moves[:4])
         load_quarters(2, 4)
-        move_scales(moves[3:])
+        move_scales(moves[4:])
 
         w1_codes = [
             placed.tile([P, 2, H // 4], I32, name="w1_codes%d" % b, offset=OPERANDS_AT + (8 + 2 * b) * S, align_bytes=64)
@@ -147,8 +147,8 @@ def tile_list_muni_butterfly_residual_kernel(
             w3_sc[:].rearrange("p (b t g m) -> p b g t m", b=2, t=4, m=16),
             w_sc_raw[:, 1].rearrange("p (b g m t) -> p b g t m", b=2, t=4, m=16),
         )
-        for a, q in moves:
-            row, to = 16 * a + 4 * q, 32 * q + 4 * a
+        for q, a in sorted((q, a) for a, q in moves):
+            row, to = ROWS_AT + 16 * a + 4 * q, 32 * q + 4 * a
             nc.sync.dma_start(w3_sc[to : to + 4].bitcast(I32), w3_sc[row : row + 4].bitcast(I32))
 
         w3_codes = kept("w3_codes", [P, 2, N], I32)

@@ -301,7 +301,7 @@ def tile_list_muni_butterfly_residual_kernel(
             for b in range(2):
                 repeated = (u, b) in REPEATED
                 if not repeated:
-                    out_bank[u, b] = bank_tile(2 * u + b, [P, 4, BATCH])
+                    out_bank[u, b] = bank_tile(2 * (u % LAST) + b, [P, 4, BATCH])
                 product(
                     out_bank[u, b],
                     b,
@@ -313,12 +313,10 @@ def tile_list_muni_butterfly_residual_kernel(
                     True,
                 )
 
-        def finish(u):
-            for b in range(2):
+        def finish(u, groups=range(2)):
+            for b in groups:
                 result = ring.tile([P, 4, BATCH], F32, name="result", bufs=2 * BATCHES)
-                if (u, b) in REPEATED and u == LAST - 1:
-                    nc.vector.tensor_copy(result[:], out_bank[u, b][:])
-                elif (u, b) in REPEATED:
+                if (u, b) in REPEATED:
                     nc.scalar.copy(result[:], out_bank[u, b][:])
                 else:
                     nc.vector.tensor_tensor(result[:], out_bank[u, b][:], y_sb[u, b][:], ALU.add)
@@ -364,7 +362,7 @@ def tile_list_muni_butterfly_residual_kernel(
                 second_product(u + 2)
             quantise_act(u)
             third_product(u)
-            if u < LAST - 1:
-                finish(u)
-        finish(LAST - 1)
+            if u < LAST:
+                finish(u, range(2) if u < LAST - 1 else [0])
+        finish(LAST - 1, [1])
         finish(LAST)

@@ -341,9 +341,9 @@ def tile_list_muni_butterfly_residual_kernel(
             double_abs(pair)
         quantise_w2(0, 1)
         gather_all_wings(2)
-        quantise_w2(1, 0)
         for first in (0, M // 2):
             quantise_z(0, slice(first, first + M // 2), z_tile(M // 2))
+        quantise_w2(1, 0)
         gather_wings(3, slice(0, M - BATCH), kept("wings0", [P, 2, M - BATCH], F32))
         quantise_w2(1, 1)
         quantise_z(1, batch(0), kept("z_first", [P, BATCH, 4], BF16))

@@ -155,7 +155,7 @@ def tile_list_muni_butterfly_residual_kernel(
         h_sb = [kept("h_sb%d" % i, [P, S], F32) for i in range(8)]
         w2_codes = [kept("w2_codes%d" % a, [P, N], U32) for a in range(2)]
         w2_sc = [kept("w2_sc%d" % a, [P, N], U8) for a in range(2)]
-        z_codes = [kept("z_codes%d" % a, [P, M], U32) for a in range(2)]
+        z_codes = {(a, h): kept("z_codes%d%d" % (a, h), [P, M // 2], U32) for a, h in ((0, 0), (1, 0), (1, 1))}
         z_sc = [kept("z_sc%d" % a, [P, M], U8) for a in range(2)]
         belly, twice_abs, wings = {}, {}, {}
         y_bank, y_sb, tanh_y, act_codes, act_sc, out_bank = {}, {}, {}, {}, {}, {}
@@ -202,22 +202,31 @@ def tile_list_muni_butterfly_residual_kernel(
             for e in range(2):
                 nc.vector.tensor_copy(belly[pair][:, e, :], picked(2 * pair + e, 0, slice(0, M)))
 
-        def double_abs(pair):
-            twice_abs[pair] = placed.tile(
-                [P, 2, M], F32, name="twice_abs%d" % pair, offset=OPERANDS_AT + 4 * S * ((pair + 3) % 4)
+        def double_abs(pair, trades=slice(0, M)):
+            twice_abs[pair, trades.start] = placed.tile(
+                [P, 2, trades.stop - trades.start],
+                F32,
+                name="twice_abs%d_%d" % (pair, trades.start),
+                offset=OPERANDS_AT + 4 * S * ((pair + 3) % 4) + 8 * trades.start,
             )
-            nc.scalar.activation(twice_abs[pair][:], belly[pair][:], ACT.Abs, scale=2.0)
+            nc.scalar.activation(twice_abs[pair, trades.start][:], belly[pair][:, :, trades], ACT.Abs, scale=2.0)
 
-        def gather_wings(pair, trades, short):
+        def gather_short(pair, trades, short):
             for e in range(2):
                 nc.vector.tensor_tensor(
-                    short[:, e, :], picked(2 * pair + e, 1, trades), twice_abs[pair][:, e, trades], ALU.subtract
+                    short[:, e, :], picked(2 * pair + e, 1, trades), twice_abs[pair, trades.start][:, e, :], ALU.subtract
                 )
+
+        def gather_long(pair, trades, short):
             for e in range(2):
                 a, t = divmod(2 * pair + e, 4)
                 nc.vector.tensor_tensor(
                     wings[a][:, t, trades], picked(2 * pair + e, 2, trades), short[:, e, :], ALU.add
                 )
+
+        def gather_wings(pair, trades, short):
+            gather_short(pair, trades, short)
+            gather_long(pair, trades, short)
 
         def gather_all_wings(pair):
             if pair % 2 == 0:
@@ -230,9 +239,13 @@ def tile_list_muni_butterfly_residual_kernel(
                 wings[a][:, :, trades].rearrange("p t (g m) -> p g t m", m=4),
             )
 
+        def z_words(a, trades):
+            half, first = divmod(trades.start, M // 2)
+            return z_codes[a, half][:, first : first + trades.stop - trades.start]
+
         def quantise_rounded_z(a, trades, z_bf):
             nc.vector.quantize_mx(
-                out=z_codes[a][:, trades].bitcast(FP8X4),
+                out=z_words(a, trades).bitcast(FP8X4),
                 scales=z_sc[a][:, trades],
                 in_=z_bf[:].rearrange("p m t -> p (m t)"),
             )
@@ -264,7 +277,7 @@ def tile_list_muni_butterfly_residual_kernel(
 
         def z_product(u, b, stop):
             bank = bank_tile(2 * u + b, [P, 4, BATCH])
-            x_codes = [z_codes[a][:, batch(u)] for a in range(2)]
+            x_codes = [z_words(a, batch(u)) for a in range(2)]
             product(bank, b, w2_codes, w2_sc, x_codes, [z_sc[a][:, batch(u)] for a in range(2)], True, stop)
             return bank
 
@@ -337,14 +350,23 @@ def tile_list_muni_butterfly_residual_kernel(
         double_abs(1)
         gather_all_wings(1)
         quantise_w2(0, 0)
-        for pair in range(2, 4):
-            double_abs(pair)
+        double_abs(2)
+        double_abs(3, slice(0, M - BATCH))
+        double_abs(3, batch(LAST))
         quantise_w2(0, 1)
         gather_all_wings(2)
-        for first in (0, M // 2):
-            quantise_z(0, slice(first, first + M // 2), z_tile(M // 2))
+        quantise_z(0, slice(0, M // 2), z_tile(M // 2))
+        z_second = z_tile(M // 2)
+        dst, src = z_views(0, slice(M // 2, M), z_second)
+        nc.scalar.activation(dst, src, ACT.Copy, scale=-0.5)
         quantise_w2(1, 0)
-        gather_wings(3, slice(0, M - BATCH), kept("wings0", [P, 2, M - BATCH], F32))
+        short = kept("wings0", [P, 2, M - BATCH], F32)
+        gather_short(3, slice(0, M - BATCH), short)
+        z_codes[0, 1] = placed.tile(
+            [P, M // 2], U32, name="z_codes01", offset=OPERANDS_AT + 8 * S, align_bytes=64
+        )
+        quantise_rounded_z(0, slice(M // 2, M), z_second)
+        gather_long(3, slice(0, M - BATCH), short)
         quantise_w2(1, 1)
         quantise_z(1, batch(0), kept("z_first", [P, BATCH, 4], BF16))
         for u in range(1, LAST):

@@ -23,6 +23,8 @@ BANKS = 8
 BATCH = 128
 BATCHES = M // BATCH
 LAST = BATCHES - 1
+EARLY = slice(0, M - BATCH)
+LOWER, UPPER = slice(0, M // 2), slice(M // 2, M)
 ROWS_AT = 96
 PER_COLUMN = 16
 REPEATED = [(u, 0) for u in range(3)]
@@ -36,6 +38,7 @@ W2_FIRST_AT = W3_SCALES_AT + N
 TABLE_AT = (0, W2_FIRST_AT + TABLE_BYTES)
 W2_AT = (W2_FIRST_AT, TABLE_AT[1])
 OPERANDS_AT = TABLE_AT[1] + TABLE_BYTES
+DOUBLED_AT = [OPERANDS_AT + 4 * S * place for place in (3, 0, 1, 2)]
 
 
 def tile_list_muni_butterfly_residual_kernel(
@@ -85,27 +88,20 @@ def tile_list_muni_butterfly_residual_kernel(
             w_sc_raw[:, 0].bitcast(I32).rearrange("p (b g t w) -> p b g t w", b=2, t=4, w=2),
         )
 
-        moves = [(a, q) for a in range(2) for q in range(4)]
         tab_second = placed.tile([P, T], I32, name="tab_second", offset=TABLE_AT[1])
-
-        def load_quarters(first, last):
-            words = slice(T // 4 * first, T // 4 * last)
+        for a in range(2):
+            words = slice(T // 2 * a, T // 2 * (a + 1))
             nc.sync.dma_start(tab_second[:, words], table[1][:, words])
-
-        def move_scales(some_moves):
-            for a, q in some_moves:
+            for q in range(4):
                 row = ROWS_AT + 16 * a + 4 * q
                 nc.sync.dma_start(
                     first_sc[a][32 * q : 32 * q + 4].bitcast(I32), first_sc[1][row : row + 4].bitcast(I32)
                 )
 
-        load_quarters(0, 2)
-        move_scales(moves[:4])
-        load_quarters(2, 4)
-        move_scales(moves[4:])
-
         w1_codes = [
-            placed.tile([P, 2, H // 4], I32, name="w1_codes%d" % b, offset=OPERANDS_AT + (8 + 2 * b) * S, align_bytes=64)
+            placed.tile(
+                [P, 2, H // 4], I32, name="w1_codes%d" % b, offset=OPERANDS_AT + (8 + 2 * b) * S, align_bytes=64
+            )
             for b in range(2)
         ]
 
@@ -147,15 +143,16 @@ def tile_list_muni_butterfly_residual_kernel(
             w3_sc[:].rearrange("p (b t g m) -> p b g t m", b=2, t=4, m=16),
             w_sc_raw[:, 1].rearrange("p (b g m t) -> p b g t m", b=2, t=4, m=16),
         )
-        for q, a in sorted((q, a) for a, q in moves):
-            row, to = ROWS_AT + 16 * a + 4 * q, 32 * q + 4 * a
-            nc.sync.dma_start(w3_sc[to : to + 4].bitcast(I32), w3_sc[row : row + 4].bitcast(I32))
+        for q in range(4):
+            for a in range(2):
+                row, to = ROWS_AT + 16 * a + 4 * q, 32 * q + 4 * a
+                nc.sync.dma_start(w3_sc[to : to + 4].bitcast(I32), w3_sc[row : row + 4].bitcast(I32))
 
         w3_codes = kept("w3_codes", [P, 2, N], I32)
         h_sb = [kept("h_sb%d" % i, [P, S], F32) for i in range(8)]
         w2_codes = [kept("w2_codes%d" % a, [P, N], U32) for a in range(2)]
         w2_sc = [kept("w2_sc%d" % a, [P, N], U8) for a in range(2)]
-        z_codes = {(a, h): kept("z_codes%d%d" % (a, h), [P, M // 2], U32) for a, h in ((0, 0), (1, 0), (1, 1))}
+        z_codes = {key: kept("z_codes%d%d" % key, [P, M // 2], U32) for key in ((0, 0), (1, 0), (1, 1))}
         z_sc = [kept("z_sc%d" % a, [P, M], U8) for a in range(2)]
         belly, twice_abs, wings = {}, {}, {}
         y_bank, y_sb, tanh_y, act_codes, act_sc, out_bank = {}, {}, {}, {}, {}, {}
@@ -207,15 +204,14 @@ def tile_list_muni_butterfly_residual_kernel(
                 [P, 2, trades.stop - trades.start],
                 F32,
                 name="twice_abs%d_%d" % (pair, trades.start),
-                offset=OPERANDS_AT + 4 * S * ((pair + 3) % 4) + 8 * trades.start,
+                offset=DOUBLED_AT[pair] + 8 * trades.start,
             )
             nc.scalar.activation(twice_abs[pair, trades.start][:], belly[pair][:, :, trades], ACT.Abs, scale=2.0)
 
         def gather_short(pair, trades, short):
+            doubled = twice_abs[pair, trades.start]
             for e in range(2):
-                nc.vector.tensor_tensor(
-                    short[:, e, :], picked(2 * pair + e, 1, trades), twice_abs[pair, trades.start][:, e, :], ALU.subtract
-                )
+                nc.vector.tensor_tensor(short[:, e, :], picked(2 * pair + e, 1, trades), doubled[:, e, :], ALU.subtract)
 
         def gather_long(pair, trades, short):
             for e in range(2):
@@ -240,8 +236,8 @@ def tile_list_muni_butterfly_residual_kernel(
             )
 
         def z_words(a, trades):
-            half, first = divmod(trades.start, M // 2)
-            return z_codes[a, half][:, first : first + trades.stop - trades.start]
+            upper, first = divmod(trades.start, M // 2)
+            return z_codes[a, upper][:, first : first + trades.stop - trades.start]
 
         def quantise_rounded_z(a, trades, z_bf):
             nc.vector.quantize_mx(
@@ -250,9 +246,12 @@ def tile_list_muni_butterfly_residual_kernel(
                 in_=z_bf[:].rearrange("p m t -> p (m t)"),
             )
 
-        def quantise_z(a, trades, z_bf):
+        def round_z(a, trades, z_bf):
             dst, src = z_views(a, trades, z_bf)
             nc.scalar.activation(dst, src, ACT.Copy, scale=-0.5)
+
+        def quantise_z(a, trades, z_bf):
+            round_z(a, trades, z_bf)
             quantise_rounded_z(a, trades, z_bf)
 
         def z_tile(count):
@@ -292,7 +291,7 @@ def tile_list_muni_butterfly_residual_kernel(
                 if (u, b) in REPEATED:
                     out_bank[u, b] = z_product(u, b, False)
                 else:
-                    y_sb[u, b] = ring.tile([P, 4, BATCH], F32, name="y_sb", bufs=5)
+                    y_sb[u, b] = ring.tile([P, 4, BATCH], F32, name="y_sb", bufs=2 * BATCHES - len(REPEATED))
                     nc.scalar.copy(y_sb[u, b][:], y_bank[u, b][:])
 
         def quantise_act(u):
@@ -334,7 +333,7 @@ def tile_list_muni_butterfly_residual_kernel(
                 else:
                     nc.vector.tensor_tensor(result[:], out_bank[u, b][:], y_sb[u, b][:], ALU.add)
                 rows = out[PASS * b : PASS * (b + 1), batch(u)]
-                queue = nc.scalar if u >= LAST - 1 and b == 1 else nc.sync
+                queue = nc.scalar if (u, b) == (LAST, 1) else nc.sync
                 queue.dma_start(rows.rearrange("(p t) m -> p t m", t=4), result[:])
 
         order_w3()
@@ -351,22 +350,19 @@ def tile_list_muni_butterfly_residual_kernel(
         gather_all_wings(1)
         quantise_w2(0, 0)
         double_abs(2)
-        double_abs(3, slice(0, M - BATCH))
+        double_abs(3, EARLY)
         double_abs(3, batch(LAST))
         quantise_w2(0, 1)
         gather_all_wings(2)
-        quantise_z(0, slice(0, M // 2), z_tile(M // 2))
-        z_second = z_tile(M // 2)
-        dst, src = z_views(0, slice(M // 2, M), z_second)
-        nc.scalar.activation(dst, src, ACT.Copy, scale=-0.5)
+        quantise_z(0, LOWER, z_tile(M // 2))
+        z_upper = z_tile(M // 2)
+        round_z(0, UPPER, z_upper)
         quantise_w2(1, 0)
-        short = kept("wings0", [P, 2, M - BATCH], F32)
-        gather_short(3, slice(0, M - BATCH), short)
-        z_codes[0, 1] = placed.tile(
-            [P, M // 2], U32, name="z_codes01", offset=OPERANDS_AT + 8 * S, align_bytes=64
-        )
-        quantise_rounded_z(0, slice(M // 2, M), z_second)
-        gather_long(3, slice(0, M - BATCH), short)
+        short_early = kept("wings0", [P, 2, M - BATCH], F32)
+        gather_short(3, EARLY, short_early)
+        z_codes[0, 1] = placed.tile([P, M // 2], U32, name="z_codes01", offset=DOUBLED_AT[3], align_bytes=64)
+        quantise_rounded_z(0, UPPER, z_upper)
+        gather_long(3, EARLY, short_early)
         quantise_w2(1, 1)
         quantise_z(1, batch(0), kept("z_first", [P, BATCH, 4], BF16))
         for u in range(1, LAST):
@@ -384,7 +380,8 @@ def tile_list_muni_butterfly_residual_kernel(
                 second_product(u + 2)
             quantise_act(u)
             third_product(u)
+            if u > 0:
+                finish(u - 1, [1])
             if u < LAST:
-                finish(u, range(2) if u < LAST - 1 else [0])
-        finish(LAST - 1, [1])
+                finish(u, [0])
         finish(LAST)

@@ -23,22 +23,25 @@ BANKS = 8
 BATCH = 128
 BATCHES = M // BATCH
 LAST = BATCHES - 1
-EARLY = slice(0, M - BATCH)
-LOWER, UPPER = slice(0, M // 2), slice(M // 2, M)
+ALL = slice(0, M)
+HALVES = (slice(0, M // 2), slice(M // 2, M))
 ROWS_AT = 96
 PER_COLUMN = 16
+BELLY, SHORT, LONG = range(3)
 REPEATED = [(u, 0) for u in range(3)]
 
-TABLE_BYTES = 4 * T
+KIB = 1024
+TABLE_AT = (0, 27 * KIB)
 W1_SECOND_AT = 0
-W3_AT = W1_SECOND_AT + 2 * H
-GAIN_AT = W3_AT + 8 * N
-W3_SCALES_AT = GAIN_AT + 64
-W2_FIRST_AT = W3_SCALES_AT + N
-TABLE_AT = (0, W2_FIRST_AT + TABLE_BYTES)
-W2_AT = (W2_FIRST_AT, TABLE_AT[1])
-OPERANDS_AT = TABLE_AT[1] + TABLE_BYTES
-DOUBLED_AT = [OPERANDS_AT + 4 * S * place for place in (3, 0, 1, 2)]
+W3_SCALES_AT = 2 * KIB
+GAIN_AT = 3 * KIB
+W2_AT = {(0, 0): 4 * KIB, (0, 1): 12 * KIB, (1, 0): 20 * KIB, (1, 1): 36 * KIB}
+W3_AT = 28 * KIB
+OPERANDS_AT = 44 * KIB
+RESULT_AT = 4 * KIB
+Y_AT = 20 * KIB
+TANH_AT = 30 * KIB
+TANH_PLACES = 6
 
 
 def tile_list_muni_butterfly_residual_kernel(
@@ -54,6 +57,9 @@ def tile_list_muni_butterfly_residual_kernel(
         def kept(tag, shape, dtype):
             return keep.tile(shape, dtype, name=tag, align_bytes=64)
 
+        def place(name, shape, dtype, offset):
+            return placed.tile(shape, dtype, name=name, offset=offset, align_bytes=64)
+
         def bank_tile(number, shape):
             return psum.tile(shape, F32, name="bank%d" % number)
 
@@ -68,7 +74,7 @@ def tile_list_muni_butterfly_residual_kernel(
         nc.vector.memset(first_sc[0][:].bitcast(I32), 0)
 
         table = [tab_words[a].rearrange("p t i -> p (t i)").bitcast(I32) for a in range(2)]
-        tab_first = placed.tile([P, T], I32, name="tab_first", offset=TABLE_AT[0])
+        tab_first = place("tab_first", [P, T], I32, TABLE_AT[0])
         nc.sync.dma_start(tab_sc[ROWS_AT:P].bitcast(I32), tab_scales.rearrange("a q t -> (a q) t").bitcast(I32))
         nc.sync.dma_start(offs_sb[:], offs)
         nc.sync.dma_start(w_sc_raw[ROWS_AT:P, 0].bitcast(I32), w1_scales.rearrange("a q c -> (a q) c").bitcast(I32))
@@ -80,7 +86,7 @@ def tile_list_muni_butterfly_residual_kernel(
         for leg, positions in enumerate((pos1, pos2, pos3)):
             nc.sync.dma_start(pos_sb[leg][:], positions)
 
-        v_sc = placed.tile([P, S], U8, name="v_sc", offset=TABLE_AT[1])
+        v_sc = place("v_sc", [P, S], U8, W3_AT)
         nc.vector.tensor_copy(v_sc[:], tab_sc[:].indirect(offs_sb[:]))
         nc.vector.tensor_copy(first_sc[1][:, 0].bitcast(I32), v_sc[:].bitcast(I32))
         nc.vector.tensor_copy(
@@ -88,7 +94,7 @@ def tile_list_muni_butterfly_residual_kernel(
             w_sc_raw[:, 0].bitcast(I32).rearrange("p (b g t w) -> p b g t w", b=2, t=4, w=2),
         )
 
-        tab_second = placed.tile([P, T], I32, name="tab_second", offset=TABLE_AT[1])
+        tab_second = place("tab_second", [P, T], I32, TABLE_AT[1])
         for a in range(2):
             words = slice(T // 2 * a, T // 2 * (a + 1))
             nc.sync.dma_start(tab_second[:, words], table[1][:, words])
@@ -98,47 +104,43 @@ def tile_list_muni_butterfly_residual_kernel(
                     first_sc[a][32 * q : 32 * q + 4].bitcast(I32), first_sc[1][row : row + 4].bitcast(I32)
                 )
 
-        w1_codes = [
-            placed.tile(
-                [P, 2, H // 4], I32, name="w1_codes%d" % b, offset=OPERANDS_AT + (8 + 2 * b) * S, align_bytes=64
-            )
-            for b in range(2)
-        ]
+        w1_codes = [place("w1_codes%d" % b, [P, 2, H // 4], I32, OPERANDS_AT + (8 + 2 * b) * KIB) for b in range(2)]
 
-        def order_w1(b, engine):
-            engine.tensor_copy(
+        def order_w1(b):
+            nc.vector.tensor_copy(
                 w1_codes[b][:].rearrange("p a (t g w) -> p a t g w", t=4, w=4),
                 w1_raw[b][:].rearrange("p a (g t w) -> p a t g w", t=4, w=4),
             )
 
-        order_w1(0, nc.vector)
+        order_w1(0)
 
-        v_first = placed.tile([P, S], U32, name="v_first", offset=OPERANDS_AT, align_bytes=64)
+        v_first = place("v_first", [P, S], U32, OPERANDS_AT)
         nc.vector.tensor_copy(v_first[:], tab_first[:].bitcast(U32).indirect(offs_sb[:]))
         v_codes = {(0, half): v_first[:, BANK * half : BANK * (half + 1)] for half in range(2)}
         for half in range(2):
-            v_second = placed.tile(
-                [P, BANK], U32, name="v_second%d" % half, offset=OPERANDS_AT + 4 * (S + BANK * half), align_bytes=64
-            )
+            v_second = place("v_second%d" % half, [P, BANK], U32, OPERANDS_AT + 4 * (S + BANK * half))
             v_codes[1, half] = v_second[:]
             entries = offs_sb[:, BANK // PER_COLUMN * half : BANK // PER_COLUMN * (half + 1)]
             nc.vector.tensor_copy(v_second[:], tab_second[:].bitcast(U32).indirect(entries))
 
-        w3_raw = placed.tile([P, 2, N], I32, name="w3_raw", offset=W3_AT)
+        w1_raw[1] = place("w1_second", [P, 2, H // 4], I32, W1_SECOND_AT)
+        nc.sync.dma_start(w1_raw[1][:], w1_groups[1].bitcast(I32))
+        order_w1(1)
+        w2_raw = {}
+        for a in range(2):
+            for b in range(2):
+                w2_raw[a, b] = place("w2_raw%d%d" % (a, b), [P, 4, PASS], F32, W2_AT[a, b])
+                w2_rows = w2[PASS * a : PASS * (a + 1), PASS * b : PASS * (b + 1)]
+                w2_rows = w2_rows.rearrange("(g t i) n -> t g i n", t=4, i=8)
+                for t in range(4):
+                    nc.sync.dma_start(w2_raw[a, b][:, t, :], w2_rows[t])
+        w3_raw = place("w3_raw", [P, 2, N], I32, W3_AT)
         for a in range(2):
             nc.sync.dma_start(w3_raw[:, a], w3_words[a].rearrange("p c i -> p (c i)").bitcast(I32))
-        w1_raw[1] = placed.tile([P, 2, H // 4], I32, name="w1_second", offset=W1_SECOND_AT)
-        nc.sync.dma_start(w1_raw[1][:], w1_groups[1].bitcast(I32))
-        order_w1(1, nc.gpsimd)
-        gain_sb = placed.tile([P, 2, 4], F32, name="gain_sb", offset=GAIN_AT)
+        gain_sb = place("gain_sb", [P, 2, 4], F32, GAIN_AT)
         nc.sync.dma_start(gain_sb[:], gain.rearrange("(b p t) -> p b t", b=2, t=4))
-        w2_raw = [placed.tile([P, 4, N], F32, name="w2_raw%d" % a, offset=W2_AT[a]) for a in range(2)]
-        for a in range(2):
-            w2_rows = w2[PASS * a : PASS * (a + 1), :].rearrange("(g t i) n -> t g i n", t=4, i=8)
-            for t in range(4):
-                nc.sync.dma_start(w2_raw[a][:, t, :], w2_rows[t])
 
-        w3_sc = placed.tile([P, N], U8, name="w3_sc", offset=W3_SCALES_AT, align_bytes=64)
+        w3_sc = place("w3_sc", [P, N], U8, W3_SCALES_AT)
         nc.vector.tensor_copy(
             w3_sc[:].rearrange("p (b t g m) -> p b g t m", b=2, t=4, m=16),
             w_sc_raw[:, 1].rearrange("p (b g m t) -> p b g t m", b=2, t=4, m=16),
@@ -152,21 +154,26 @@ def tile_list_muni_butterfly_residual_kernel(
         h_sb = [kept("h_sb%d" % i, [P, S], F32) for i in range(8)]
         w2_codes = [kept("w2_codes%d" % a, [P, N], U32) for a in range(2)]
         w2_sc = [kept("w2_sc%d" % a, [P, N], U8) for a in range(2)]
-        z_codes = {key: kept("z_codes%d%d" % key, [P, M // 2], U32) for key in ((0, 0), (1, 0), (1, 1))}
+        z_codes = {(a, half): kept("z_codes%d%d" % (a, half), [P, M // 2], U32) for a in range(2) for half in range(2)}
         z_sc = [kept("z_sc%d" % a, [P, M], U8) for a in range(2)]
-        belly, twice_abs, wings = {}, {}, {}
+        wings = [kept("wings%d" % a, [P, 4, M], F32) for a in range(2)]
+        short = [kept("short%d" % a, [P, 4, M], F32) for a in range(2)]
+        belly_late = kept("belly_late", [P, 4, M], F32)
+        twice_abs = kept("twice_abs", [P, 4, M], F32)
+        belly_early = [kept("belly_early%d" % half, [P, 4, M // 2], F32) for half in range(2)]
+        abs_early = [kept("abs_early%d" % half, [P, M // 2, 4], F32) for half in range(2)]
+        w2_bf = {}
         y_bank, y_sb, tanh_y, act_codes, act_sc, out_bank = {}, {}, {}, {}, {}, {}
 
-        def order_w3():
-            for a in range(2):
-                nc.vector.tensor_copy(
-                    w3_codes[:, a].rearrange("p (b t g m) -> p b g t m", b=2, t=4, m=4),
-                    w3_raw[:, a].rearrange("p (b g m t) -> p b g t m", b=2, t=4, m=4),
-                )
+        def order_w3(a):
+            nc.vector.tensor_copy(
+                w3_codes[:, a].rearrange("p (b t g m) -> p b g t m", b=2, t=4, m=4),
+                w3_raw[:, a].rearrange("p (b g m t) -> p b g t m", b=2, t=4, m=4),
+            )
 
         def first_product(pair):
-            for i in (2 * pair, 2 * pair + 1):
-                for half in range(2):
+            for half in range(2):
+                for i in (2 * pair, 2 * pair + 1):
                     quotes = slice(BANK * half, BANK * (half + 1))
                     bank = bank_tile((2 * i + half) % BANKS, [P, BANK])
                     for a in range(2):
@@ -181,87 +188,94 @@ def tile_list_muni_butterfly_residual_kernel(
                         )
                     nc.scalar.copy(h_sb[i][:, quotes], bank[:])
 
+        def round_w2(a, b):
+            w2_bf[a, b] = ring.tile([P, 4 * PASS], BF16, name="w2_bf", align_bytes=64)
+            dst = w2_bf[a, b][:].rearrange("p (t m j) -> p m j t", t=4, j=4)
+            src = w2_raw[a, b][:].rearrange("p j (m t) -> p m j t", t=4)
+            nc.vector.tensor_copy(dst, src)
+
         def quantise_w2(a, b):
             cols = slice(PASS * b, PASS * (b + 1))
-            grouped = ring.tile([P, 4 * PASS], BF16, name="w2_grouped", bufs=3, align_bytes=64)
-            dst = grouped[:].rearrange("p (t m j) -> p m j t", t=4, j=4)
-            src = w2_raw[a][:, :, cols].rearrange("p j (m t) -> p m j t", t=4)
-            for part in (slice(0, 64), slice(64, P)):
-                nc.scalar.copy(dst[:, part], src[:, part])
-            nc.vector.quantize_mx(out=w2_codes[a][:, cols].bitcast(FP8X4), scales=w2_sc[a][:, cols], in_=grouped[:])
+            nc.vector.quantize_mx(
+                out=w2_codes[a][:, cols].bitcast(FP8X4), scales=w2_sc[a][:, cols], in_=w2_bf[a, b][:]
+            )
 
         def picked(i, leg, trades):
             entries = pos_sb[leg][:, trades.start // PER_COLUMN : trades.stop // PER_COLUMN]
             return h_sb[i][:].indirect(entries)
 
-        def gather_belly(pair):
-            belly[pair] = kept("belly%d" % pair, [P, 2, M], F32)
-            for e in range(2):
-                nc.vector.tensor_copy(belly[pair][:, e, :], picked(2 * pair + e, 0, slice(0, M)))
+        def short_on_scalar(pair):
+            for i in (2 * pair, 2 * pair + 1):
+                nc.scalar.activation(short[0][:, i, :], picked(i, SHORT, ALL), ACT.Copy)
 
-        def double_abs(pair, trades=slice(0, M)):
-            twice_abs[pair, trades.start] = placed.tile(
-                [P, 2, trades.stop - trades.start],
-                F32,
-                name="twice_abs%d_%d" % (pair, trades.start),
-                offset=DOUBLED_AT[pair] + 8 * trades.start,
-            )
-            nc.scalar.activation(twice_abs[pair, trades.start][:], belly[pair][:, :, trades], ACT.Abs, scale=2.0)
+        def long_leg(i, trades):
+            a, t = divmod(i, 4)
+            nc.vector.tensor_tensor(wings[a][:, t, trades], picked(i, LONG, trades), short[a][:, t, trades], ALU.add)
 
-        def gather_short(pair, trades, short):
-            doubled = twice_abs[pair, trades.start]
-            for e in range(2):
-                nc.vector.tensor_tensor(short[:, e, :], picked(2 * pair + e, 1, trades), doubled[:, e, :], ALU.subtract)
+        def late_bellies(pair):
+            rows = slice(2 * pair - 4, 2 * pair - 2)
+            for i in (2 * pair, 2 * pair + 1):
+                nc.scalar.activation(belly_late[:, i - 4, :], picked(i, BELLY, ALL), ACT.Copy)
+            nc.scalar.activation(twice_abs[:, rows, :], belly_late[:, rows, :], ACT.Abs, scale=2.0)
 
-        def gather_long(pair, trades, short):
-            for e in range(2):
-                a, t = divmod(2 * pair + e, 4)
+        def late_wings(pair, trades):
+            for i in (2 * pair, 2 * pair + 1):
                 nc.vector.tensor_tensor(
-                    wings[a][:, t, trades], picked(2 * pair + e, 2, trades), short[:, e, :], ALU.add
+                    short[1][:, i - 4, trades], picked(i, SHORT, trades), twice_abs[:, i - 4, trades], ALU.subtract
                 )
+            for i in (2 * pair, 2 * pair + 1):
+                long_leg(i, trades)
 
-        def gather_wings(pair, trades, short):
-            gather_short(pair, trades, short)
-            gather_long(pair, trades, short)
+        def early_bellies(half):
+            for i in range(4):
+                nc.scalar.activation(belly_early[half][:, i, :], picked(i, BELLY, HALVES[half]), ACT.Copy)
 
-        def gather_all_wings(pair):
-            if pair % 2 == 0:
-                wings[pair // 2] = kept("wings%d" % (pair // 2), [P, 4, M], F32)
-            gather_wings(pair, slice(0, M), ring.tile([P, 2, M], F32, name="short"))
-
-        def z_views(a, trades, z_bf):
-            return (
-                z_bf[:].rearrange("p (g m) t -> p g t m", m=4),
-                wings[a][:, :, trades].rearrange("p t (g m) -> p g t m", m=4),
+        def early_abs(half):
+            nc.scalar.activation(
+                abs_early[half][:].rearrange("p (g m) t -> p g t m", m=4),
+                belly_early[half][:].rearrange("p t (g m) -> p g t m", m=4),
+                ACT.Abs,
             )
 
         def z_words(a, trades):
-            upper, first = divmod(trades.start, M // 2)
-            return z_codes[a, upper][:, first : first + trades.stop - trades.start]
+            half, first = divmod(trades.start, M // 2)
+            return z_codes[a, half][:, first : first + trades.stop - trades.start]
 
-        def quantise_rounded_z(a, trades, z_bf):
+        def quantise_z(a, trades, z_bf):
             nc.vector.quantize_mx(
                 out=z_words(a, trades).bitcast(FP8X4),
                 scales=z_sc[a][:, trades],
                 in_=z_bf[:].rearrange("p m t -> p (m t)"),
             )
 
-        def round_z(a, trades, z_bf):
-            dst, src = z_views(a, trades, z_bf)
-            nc.scalar.activation(dst, src, ACT.Copy, scale=-0.5)
-
-        def quantise_z(a, trades, z_bf):
-            round_z(a, trades, z_bf)
-            quantise_rounded_z(a, trades, z_bf)
-
-        def z_tile(count):
-            return ring.tile([P, count, 4], BF16, name="z_bf", bufs=3, align_bytes=64)
-
         def batch(u):
             return slice(BATCH * u, BATCH * (u + 1))
 
-        def product(bank, b, w_codes, w_sc, x_codes, x_sc, start, stop):
-            for a in range(2):
+        def early_z(u):
+            z_bf = ring.tile([P, BATCH, 4], BF16, name="z_early", bufs=4, align_bytes=64)
+            half, first = divmod(BATCH * u, M // 2)
+            nc.vector.scalar_tensor_tensor(
+                z_bf[:],
+                wings[0][:, :, batch(u)].rearrange("p t m -> p m t"),
+                -0.5,
+                abs_early[half][:, first : first + BATCH, :],
+                ALU.mult,
+                ALU.add,
+            )
+            return z_bf
+
+        def late_z(half, on_scalar):
+            z_bf = ring.tile([P, M // 2, 4], BF16, name="z_late", align_bytes=64)
+            dst = z_bf[:].rearrange("p (g m) t -> p g t m", m=4)
+            src = wings[1][:, :, HALVES[half]].rearrange("p t (g m) -> p g t m", m=4)
+            if on_scalar:
+                nc.scalar.activation(dst, src, ACT.Copy, scale=-0.5)
+            else:
+                nc.vector.tensor_scalar(dst, src, -0.5, None, ALU.mult)
+            return z_bf
+
+        def product(bank, b, w_codes, w_sc, x_codes, x_sc, start, stop, passes):
+            for a in passes:
                 for t in range(4):
                     cols = slice(PASS * b + P * t, PASS * b + P * (t + 1))
                     nc.tensor.matmul_mx(
@@ -270,20 +284,21 @@ def tile_list_muni_butterfly_residual_kernel(
                         lhsT_scale=w_sc[a][:, cols],
                         rhs=x_codes[a].bitcast(FP8X4),
                         rhs_scale=x_sc[a],
-                        start=(start and a == 0 and t == 0),
-                        stop=(stop and a == 1 and t == 3),
+                        start=(start and a == passes[0] and t == 0),
+                        stop=(stop and a == passes[1] and t == 3),
                     )
 
         def z_product(u, b, stop):
             bank = bank_tile(2 * u + b, [P, 4, BATCH])
             x_codes = [z_words(a, batch(u)) for a in range(2)]
-            product(bank, b, w2_codes, w2_sc, x_codes, [z_sc[a][:, batch(u)] for a in range(2)], True, stop)
+            product(bank, b, w2_codes, w2_sc, x_codes, [z_sc[a][:, batch(u)] for a in range(2)], True, stop, (1, 0))
             return bank
 
         def second_product(u):
             for b in range(2):
                 y_bank[u, b] = z_product(u, b, True)
-                tanh_y[u, b] = ring.tile([P, BATCH, 4], F32, name="tanh_y", bufs=6)
+                at = TANH_AT + 2 * KIB * ((2 * u + b) % TANH_PLACES)
+                tanh_y[u, b] = place("tanh_y%d%d" % (u, b), [P, BATCH, 4], F32, at)
                 nc.scalar.activation(tanh_y[u, b][:], y_bank[u, b][:].rearrange("p t m -> p m t"), ACT.Tanh)
 
         def keep_residual(u):
@@ -291,7 +306,7 @@ def tile_list_muni_butterfly_residual_kernel(
                 if (u, b) in REPEATED:
                     out_bank[u, b] = z_product(u, b, False)
                 else:
-                    y_sb[u, b] = ring.tile([P, 4, BATCH], F32, name="y_sb", bufs=2 * BATCHES - len(REPEATED))
+                    y_sb[u, b] = place("y_sb%d%d" % (u, b), [P, 4, BATCH], F32, Y_AT + 2 * KIB * len(y_sb))
                     nc.scalar.copy(y_sb[u, b][:], y_bank[u, b][:])
 
         def quantise_act(u):
@@ -323,11 +338,12 @@ def tile_list_muni_butterfly_residual_kernel(
                     [act_sc[u, a][:] for a in range(2)],
                     not repeated,
                     True,
+                    (0, 1),
                 )
 
         def finish(u, groups=range(2)):
             for b in groups:
-                result = ring.tile([P, 4, BATCH], F32, name="result", bufs=2 * BATCHES)
+                result = place("result%d%d" % (u, b), [P, 4, BATCH], F32, RESULT_AT + 2 * KIB * (2 * u + b))
                 if (u, b) in REPEATED:
                     nc.scalar.copy(result[:], out_bank[u, b][:])
                 else:
@@ -336,52 +352,62 @@ def tile_list_muni_butterfly_residual_kernel(
                 queue = nc.scalar if (u, b) == (LAST, 1) else nc.sync
                 queue.dma_start(rows.rearrange("(p t) m -> p t m", t=4), result[:])
 
-        order_w3()
-        for pair in range(2):
-            first_product(pair)
-            gather_belly(pair)
-        double_abs(0)
-        for pair in range(2, 4):
-            first_product(pair)
-        gather_all_wings(0)
-        for pair in range(2, 4):
-            gather_belly(pair)
-        double_abs(1)
-        gather_all_wings(1)
+        first_product(0)
+        short_on_scalar(0)
+        round_w2(0, 0)
         quantise_w2(0, 0)
-        double_abs(2)
-        double_abs(3, EARLY)
-        double_abs(3, batch(LAST))
+        long_leg(0, ALL)
+        long_leg(1, ALL)
+        first_product(1)
+        short_on_scalar(1)
+        round_w2(0, 1)
+        round_w2(1, 0)
         quantise_w2(0, 1)
-        gather_all_wings(2)
-        quantise_z(0, LOWER, z_tile(M // 2))
-        z_upper = z_tile(M // 2)
-        round_z(0, UPPER, z_upper)
+        long_leg(2, ALL)
         quantise_w2(1, 0)
-        short_early = kept("wings0", [P, 2, M - BATCH], F32)
-        gather_short(3, EARLY, short_early)
-        z_codes[0, 1] = placed.tile([P, M // 2], U32, name="z_codes01", offset=DOUBLED_AT[3], align_bytes=64)
-        quantise_rounded_z(0, UPPER, z_upper)
-        gather_long(3, EARLY, short_early)
+        long_leg(3, ALL)
+        first_product(2)
+        late_bellies(2)
+        round_w2(1, 1)
+        order_w3(0)
         quantise_w2(1, 1)
-        quantise_z(1, batch(0), kept("z_first", [P, BATCH, 4], BF16))
-        for u in range(1, LAST):
-            quantise_z(1, batch(u), z_tile(BATCH))
-        gather_wings(3, batch(LAST), kept("z_first", [P, 2, BATCH], F32))
+        order_w3(1)
+        late_wings(2, ALL)
+        first_product(3)
+        late_bellies(3)
+        late_wings(3, HALVES[0])
+        early_bellies(0)
+        early_abs(0)
+        quantise_z(1, HALVES[0], late_z(0, False))
+        z_early = [early_z(u) for u in range(2)]
+        for u in range(2):
+            quantise_z(0, batch(u), z_early[u])
+        early_bellies(1)
         second_product(0)
-        z_last = z_tile(BATCH)
-        dst, src = z_views(1, batch(LAST), z_last)
-        nc.vector.tensor_scalar(dst, src, -0.5, None, ALU.mult)
-        quantise_rounded_z(1, batch(LAST), z_last)
+        late_wings(3, HALVES[1])
+        early_abs(1)
+        z_late = late_z(1, True)
         second_product(1)
-        for u in range(BATCHES):
+        keep_residual(0)
+        quantise_act(0)
+        third_product(0)
+        z_early = early_z(2)
+        quantise_z(1, HALVES[1], z_late)
+        quantise_z(0, batch(2), z_early)
+        second_product(2)
+        finish(0, [0])
+        keep_residual(1)
+        quantise_act(1)
+        third_product(1)
+        quantise_z(0, batch(3), early_z(3))
+        second_product(3)
+        finish(0, [1])
+        finish(1, [0])
+        for u in range(2, BATCHES):
             keep_residual(u)
-            if u + 2 < BATCHES:
-                second_product(u + 2)
             quantise_act(u)
             third_product(u)
-            if u > 0:
-                finish(u - 1, [1])
+            finish(u - 1, [1])
             if u < LAST:
                 finish(u, [0])
         finish(LAST)

@@ -158,10 +158,8 @@ def tile_list_muni_butterfly_residual_kernel(
         z_sc = [kept("z_sc%d" % a, [P, M], U8) for a in range(2)]
         wings = [kept("wings%d" % a, [P, 4, M], F32) for a in range(2)]
         short = [kept("short%d" % a, [P, 4, M], F32) for a in range(2)]
-        belly_late = kept("belly_late", [P, 4, M], F32)
-        twice_abs = kept("twice_abs", [P, 4, M], F32)
-        belly_early = [kept("belly_early%d" % half, [P, 4, M // 2], F32) for half in range(2)]
-        abs_early = [kept("abs_early%d" % half, [P, M // 2, 4], F32) for half in range(2)]
+        belly = [kept("belly%d" % a, [P, 4, M], F32) for a in range(2)]
+        belly_abs = [kept("belly_abs%d" % a, [P, 4, M], F32) for a in range(2)]
         w2_bf = {}
         y_bank, y_sb, tanh_y, act_codes, act_sc, out_bank = {}, {}, {}, {}, {}, {}
 
@@ -171,9 +169,9 @@ def tile_list_muni_butterfly_residual_kernel(
                 w3_raw[:, a].rearrange("p (b g m t) -> p b g t m", b=2, t=4, m=4),
             )
 
-        def first_product(pair):
+        def first_product(tiles):
             for half in range(2):
-                for i in (2 * pair, 2 * pair + 1):
+                for i in tiles:
                     quotes = slice(BANK * half, BANK * (half + 1))
                     bank = bank_tile((2 * i + half) % BANKS, [P, BANK])
                     for a in range(2):
@@ -186,7 +184,10 @@ def tile_list_muni_butterfly_residual_kernel(
                             start=(a == 0),
                             stop=(a == 1),
                         )
-                    nc.scalar.copy(h_sb[i][:, quotes], bank[:])
+                    if half == 0:
+                        nc.scalar.activation(h_sb[i][:, quotes], bank[:], ACT.Copy, scale=0.5)
+                    else:
+                        nc.vector.tensor_scalar(h_sb[i][:, quotes], bank[:], 0.5, None, ALU.mult)
 
         def round_w2(a, b):
             w2_bf[a, b] = ring.tile([P, 4 * PASS], BF16, name="w2_bf", align_bytes=64)
@@ -204,38 +205,19 @@ def tile_list_muni_butterfly_residual_kernel(
             entries = pos_sb[leg][:, trades.start // PER_COLUMN : trades.stop // PER_COLUMN]
             return h_sb[i][:].indirect(entries)
 
-        def short_on_scalar(pair):
-            for i in (2 * pair, 2 * pair + 1):
-                nc.scalar.activation(short[0][:, i, :], picked(i, SHORT, ALL), ACT.Copy)
+        def short_leg(i):
+            nc.scalar.activation(short[i // 4][:, i % 4, :], picked(i, SHORT, ALL), ACT.Copy)
 
-        def long_leg(i, trades):
+        def long_leg(i):
             a, t = divmod(i, 4)
-            nc.vector.tensor_tensor(wings[a][:, t, trades], picked(i, LONG, trades), short[a][:, t, trades], ALU.add)
+            nc.vector.tensor_tensor(wings[a][:, t, :], picked(i, LONG, ALL), short[a][:, t, :], ALU.add)
 
-        def late_bellies(pair):
-            rows = slice(2 * pair - 4, 2 * pair - 2)
-            for i in (2 * pair, 2 * pair + 1):
-                nc.scalar.activation(belly_late[:, i - 4, :], picked(i, BELLY, ALL), ACT.Copy)
-            nc.scalar.activation(twice_abs[:, rows, :], belly_late[:, rows, :], ACT.Abs, scale=2.0)
+        def bellies(a, trades):
+            for t in range(4):
+                nc.scalar.activation(belly[a][:, t, trades], picked(4 * a + t, BELLY, trades), ACT.Copy)
 
-        def late_wings(pair, trades):
-            for i in (2 * pair, 2 * pair + 1):
-                nc.vector.tensor_tensor(
-                    short[1][:, i - 4, trades], picked(i, SHORT, trades), twice_abs[:, i - 4, trades], ALU.subtract
-                )
-            for i in (2 * pair, 2 * pair + 1):
-                long_leg(i, trades)
-
-        def early_bellies(half):
-            for i in range(4):
-                nc.scalar.activation(belly_early[half][:, i, :], picked(i, BELLY, HALVES[half]), ACT.Copy)
-
-        def early_abs(half):
-            nc.scalar.activation(
-                abs_early[half][:].rearrange("p (g m) t -> p g t m", m=4),
-                belly_early[half][:].rearrange("p t (g m) -> p g t m", m=4),
-                ACT.Abs,
-            )
+        def absolute(a, trades):
+            nc.scalar.activation(belly_abs[a][:, :, trades], belly[a][:, :, trades], ACT.Abs, scale=2.0)
 
         def z_words(a, trades):
             half, first = divmod(trades.start, M // 2)
@@ -251,27 +233,15 @@ def tile_list_muni_butterfly_residual_kernel(
         def batch(u):
             return slice(BATCH * u, BATCH * (u + 1))
 
-        def early_z(u):
-            z_bf = ring.tile([P, BATCH, 4], BF16, name="z_early", bufs=4, align_bytes=64)
-            half, first = divmod(BATCH * u, M // 2)
-            nc.vector.scalar_tensor_tensor(
-                z_bf[:],
-                wings[0][:, :, batch(u)].rearrange("p t m -> p m t"),
-                -0.5,
-                abs_early[half][:, first : first + BATCH, :],
-                ALU.mult,
-                ALU.add,
+        def round_z(a, trades):
+            count = trades.stop - trades.start
+            z_bf = ring.tile([P, count, 4], BF16, name="z_bf", bufs=3, align_bytes=64)
+            nc.vector.tensor_tensor(
+                z_bf[:].rearrange("p (g m) t -> p g t m", m=2),
+                belly_abs[a][:, :, trades].rearrange("p t (g m) -> p g t m", m=2),
+                wings[a][:, :, trades].rearrange("p t (g m) -> p g t m", m=2),
+                ALU.subtract,
             )
-            return z_bf
-
-        def late_z(half, on_scalar):
-            z_bf = ring.tile([P, M // 2, 4], BF16, name="z_late", align_bytes=64)
-            dst = z_bf[:].rearrange("p (g m) t -> p g t m", m=4)
-            src = wings[1][:, :, HALVES[half]].rearrange("p t (g m) -> p g t m", m=4)
-            if on_scalar:
-                nc.scalar.activation(dst, src, ACT.Copy, scale=-0.5)
-            else:
-                nc.vector.tensor_scalar(dst, src, -0.5, None, ALU.mult)
             return z_bf
 
         def product(bank, b, w_codes, w_sc, x_codes, x_sc, start, stop, passes):
@@ -291,7 +261,7 @@ def tile_list_muni_butterfly_residual_kernel(
         def z_product(u, b, stop):
             bank = bank_tile(2 * u + b, [P, 4, BATCH])
             x_codes = [z_words(a, batch(u)) for a in range(2)]
-            product(bank, b, w2_codes, w2_sc, x_codes, [z_sc[a][:, batch(u)] for a in range(2)], True, stop, (1, 0))
+            product(bank, b, w2_codes, w2_sc, x_codes, [z_sc[a][:, batch(u)] for a in range(2)], True, stop, (0, 1))
             return bank
 
         def second_product(u):
@@ -352,54 +322,54 @@ def tile_list_muni_butterfly_residual_kernel(
                 queue = nc.scalar if (u, b) == (LAST, 1) else nc.sync
                 queue.dma_start(rows.rearrange("(p t) m -> p t m", t=4), result[:])
 
-        first_product(0)
-        short_on_scalar(0)
-        round_w2(0, 0)
-        quantise_w2(0, 0)
-        long_leg(0, ALL)
-        long_leg(1, ALL)
-        first_product(1)
-        short_on_scalar(1)
-        round_w2(0, 1)
-        round_w2(1, 0)
-        quantise_w2(0, 1)
-        long_leg(2, ALL)
-        quantise_w2(1, 0)
-        long_leg(3, ALL)
-        first_product(2)
-        late_bellies(2)
+        first_product(range(4))
+        for i in range(4):
+            short_leg(i)
+        long_leg(0)
+        first_product((4, 5))
+        long_leg(1)
+        short_leg(4)
+        short_leg(5)
+        first_product((6, 7))
+        short_leg(6)
+        short_leg(7)
+        parts = [(a, b) for a in range(2) for b in range(2)]
+        for n in range(3):
+            round_w2(*parts[n])
+            long_leg(2 + 2 * n)
+            quantise_w2(*parts[n])
+            long_leg(3 + 2 * n)
+        bellies(0, ALL)
+        absolute(0, HALVES[0])
         round_w2(1, 1)
-        order_w3(0)
+        z_bf = round_z(0, HALVES[0])
         quantise_w2(1, 1)
-        order_w3(1)
-        late_wings(2, ALL)
-        first_product(3)
-        late_bellies(3)
-        late_wings(3, HALVES[0])
-        early_bellies(0)
-        early_abs(0)
-        quantise_z(1, HALVES[0], late_z(0, False))
-        z_early = [early_z(u) for u in range(2)]
+        quantise_z(0, HALVES[0], z_bf)
+        bellies(1, HALVES[0])
+        absolute(1, HALVES[0])
+        z_first = [round_z(1, batch(u)) for u in range(2)]
         for u in range(2):
-            quantise_z(0, batch(u), z_early[u])
-        early_bellies(1)
+            quantise_z(1, batch(u), z_first[u])
+        order_w3(0)
+        order_w3(1)
+        bellies(1, HALVES[1])
         second_product(0)
-        late_wings(3, HALVES[1])
-        early_abs(1)
-        z_late = late_z(1, True)
+        absolute(0, HALVES[1])
+        absolute(1, HALVES[1])
         second_product(1)
         keep_residual(0)
         quantise_act(0)
         third_product(0)
-        z_early = early_z(2)
-        quantise_z(1, HALVES[1], z_late)
-        quantise_z(0, batch(2), z_early)
+        z_bf = round_z(0, HALVES[1])
+        z_third = round_z(1, batch(2))
+        quantise_z(0, HALVES[1], z_bf)
+        quantise_z(1, batch(2), z_third)
         second_product(2)
         finish(0, [0])
         keep_residual(1)
         quantise_act(1)
         third_product(1)
-        quantise_z(0, batch(3), early_z(3))
+        quantise_z(1, batch(3), round_z(1, batch(3)))
         second_product(3)
         finish(0, [1])
         finish(1, [0])

@@ -31,16 +31,18 @@ BELLY, SHORT, LONG = range(3)
 REPEATED = [(u, 0) for u in range(3)]
 
 KIB = 1024
-TABLE_AT = (0, 27 * KIB)
-W1_SECOND_AT = 0
-W3_SCALES_AT = 2 * KIB
-GAIN_AT = 3 * KIB
-W2_AT = {(0, 0): 4 * KIB, (0, 1): 12 * KIB, (1, 0): 20 * KIB, (1, 1): 36 * KIB}
-W3_AT = 28 * KIB
-OPERANDS_AT = 44 * KIB
-RESULT_AT = 4 * KIB
-Y_AT = 20 * KIB
-TANH_AT = 30 * KIB
+TABLE_AT = (6 * KIB, 33 * KIB)
+W3_CODES_AT = 0
+W1_SECOND_AT = 6 * KIB
+W3_SCALES_AT = 8 * KIB
+GAIN_AT = 9 * KIB
+W3_AT = 10 * KIB
+W2_AT = {(0, 0): 18 * KIB, (0, 1): 26 * KIB, (1, 0): 34 * KIB, (1, 1): 42 * KIB}
+V_SC_AT = 34 * KIB
+OPERANDS_AT = 50 * KIB
+RESULT_AT = 10 * KIB
+Y_AT = 26 * KIB
+TANH_AT = 36 * KIB
 TANH_PLACES = 6
 
 
@@ -86,7 +88,7 @@ def tile_list_muni_butterfly_residual_kernel(
         for leg, positions in enumerate((pos1, pos2, pos3)):
             nc.sync.dma_start(pos_sb[leg][:], positions)
 
-        v_sc = place("v_sc", [P, S], U8, W3_AT)
+        v_sc = place("v_sc", [P, S], U8, V_SC_AT)
         nc.vector.tensor_copy(v_sc[:], tab_sc[:].indirect(offs_sb[:]))
         nc.vector.tensor_copy(first_sc[1][:, 0].bitcast(I32), v_sc[:].bitcast(I32))
         nc.vector.tensor_copy(
@@ -126,6 +128,9 @@ def tile_list_muni_butterfly_residual_kernel(
         w1_raw[1] = place("w1_second", [P, 2, H // 4], I32, W1_SECOND_AT)
         nc.sync.dma_start(w1_raw[1][:], w1_groups[1].bitcast(I32))
         order_w1(1)
+        w3_raw = [place("w3_raw%d" % a, [P, N], I32, W3_AT + 4 * KIB * a) for a in range(2)]
+        for a in range(2):
+            nc.sync.dma_start(w3_raw[a][:], w3_words[a].rearrange("p c i -> p (c i)").bitcast(I32))
         w2_raw = {}
         for a in range(2):
             for b in range(2):
@@ -134,9 +139,6 @@ def tile_list_muni_butterfly_residual_kernel(
                 w2_rows = w2_rows.rearrange("(g t i) n -> t g i n", t=4, i=8)
                 for t in range(4):
                     nc.sync.dma_start(w2_raw[a, b][:, t, :], w2_rows[t])
-        w3_raw = place("w3_raw", [P, 2, N], I32, W3_AT)
-        for a in range(2):
-            nc.sync.dma_start(w3_raw[:, a], w3_words[a].rearrange("p c i -> p (c i)").bitcast(I32))
         gain_sb = place("gain_sb", [P, 2, 4], F32, GAIN_AT)
         nc.sync.dma_start(gain_sb[:], gain.rearrange("(b p t) -> p b t", b=2, t=4))
 
@@ -150,7 +152,7 @@ def tile_list_muni_butterfly_residual_kernel(
                 row, to = ROWS_AT + 16 * a + 4 * q, 32 * q + 4 * a
                 nc.sync.dma_start(w3_sc[to : to + 4].bitcast(I32), w3_sc[row : row + 4].bitcast(I32))
 
-        w3_codes = kept("w3_codes", [P, 2, N], I32)
+        w3_codes = place("w3_codes", [P, 2, N], I32, W3_CODES_AT)
         h_sb = [kept("h_sb%d" % i, [P, S], F32) for i in range(8)]
         w2_codes = [kept("w2_codes%d" % a, [P, N], U32) for a in range(2)]
         w2_sc = [kept("w2_sc%d" % a, [P, N], U8) for a in range(2)]
@@ -164,10 +166,12 @@ def tile_list_muni_butterfly_residual_kernel(
         y_bank, y_sb, tanh_y, act_codes, act_sc, out_bank = {}, {}, {}, {}, {}, {}
 
         def order_w3(a):
-            nc.vector.tensor_copy(
-                w3_codes[:, a].rearrange("p (b t g m) -> p b g t m", b=2, t=4, m=4),
-                w3_raw[:, a].rearrange("p (b g m t) -> p b g t m", b=2, t=4, m=4),
-            )
+            for b in range(2):
+                cols = slice(PASS * b, PASS * (b + 1))
+                nc.gpsimd.tensor_copy(
+                    w3_codes[:, a, cols].rearrange("p (t g m) -> p g t m", t=4, m=4),
+                    w3_raw[a][:, cols].rearrange("p (g m t) -> p g t m", t=4, m=4),
+                )
 
         def first_product(tiles):
             for half in range(2):
@@ -184,7 +188,7 @@ def tile_list_muni_butterfly_residual_kernel(
                             start=(a == 0),
                             stop=(a == 1),
                         )
-                    if half == 0:
+                    if half == 0 and i < 7:
                         nc.scalar.activation(h_sb[i][:, quotes], bank[:], ACT.Copy, scale=0.5)
                     else:
                         nc.vector.tensor_scalar(h_sb[i][:, quotes], bank[:], 0.5, None, ALU.mult)
@@ -208,9 +212,9 @@ def tile_list_muni_butterfly_residual_kernel(
         def short_leg(i):
             nc.scalar.activation(short[i // 4][:, i % 4, :], picked(i, SHORT, ALL), ACT.Copy)
 
-        def long_leg(i):
+        def long_leg(i, trades=ALL):
             a, t = divmod(i, 4)
-            nc.vector.tensor_tensor(wings[a][:, t, :], picked(i, LONG, ALL), short[a][:, t, :], ALU.add)
+            nc.vector.tensor_tensor(wings[a][:, t, trades], picked(i, LONG, trades), short[a][:, t, trades], ALU.add)
 
         def bellies(a, trades):
             for t in range(4):
@@ -322,23 +326,26 @@ def tile_list_muni_butterfly_residual_kernel(
                 queue = nc.scalar if (u, b) == (LAST, 1) else nc.sync
                 queue.dma_start(rows.rearrange("(p t) m -> p t m", t=4), result[:])
 
+        order_w3(0)
+        order_w3(1)
         first_product(range(4))
         for i in range(4):
             short_leg(i)
-        long_leg(0)
         first_product((4, 5))
-        long_leg(1)
         short_leg(4)
         short_leg(5)
         first_product((6, 7))
         short_leg(6)
         short_leg(7)
+        long_leg(0)
+        long_leg(1)
         parts = [(a, b) for a in range(2) for b in range(2)]
         for n in range(3):
+            trades = ALL if n < 2 else HALVES[0]
             round_w2(*parts[n])
-            long_leg(2 + 2 * n)
+            long_leg(2 + 2 * n, trades)
             quantise_w2(*parts[n])
-            long_leg(3 + 2 * n)
+            long_leg(3 + 2 * n, trades)
         bellies(0, ALL)
         absolute(0, HALVES[0])
         round_w2(1, 1)
@@ -350,8 +357,8 @@ def tile_list_muni_butterfly_residual_kernel(
         z_first = [round_z(1, batch(u)) for u in range(2)]
         for u in range(2):
             quantise_z(1, batch(u), z_first[u])
-        order_w3(0)
-        order_w3(1)
+        long_leg(6, HALVES[1])
+        long_leg(7, HALVES[1])
         bellies(1, HALVES[1])
         second_product(0)
         absolute(0, HALVES[1])

@@ -30,6 +30,8 @@ PER_COLUMN = 16
 BELLY, SHORT, LONG = range(3)
 REPEATED = [(u, 0) for u in range(3)]
 
+OUT_BANK = {(0, 1): 1, (1, 1): 3, (2, 1): 1, (3, 0): 0, (3, 1): 3}
+
 KIB = 1024
 TABLE_AT = (6 * KIB, 33 * KIB)
 W3_CODES_AT = 0
@@ -41,9 +43,9 @@ W2_AT = {(0, 0): 18 * KIB, (0, 1): 26 * KIB, (1, 0): 34 * KIB, (1, 1): 42 * KIB}
 V_SC_AT = 34 * KIB
 OPERANDS_AT = 50 * KIB
 RESULT_AT = 10 * KIB
-Y_AT = 26 * KIB
-TANH_AT = 36 * KIB
-TANH_PLACES = 6
+Y_AT = 50 * KIB
+TANH_AT = 34 * KIB
+TANH_PLACES = 8
 
 
 def tile_list_muni_butterfly_residual_kernel(
@@ -275,8 +277,8 @@ def tile_list_muni_butterfly_residual_kernel(
                 tanh_y[u, b] = place("tanh_y%d%d" % (u, b), [P, BATCH, 4], F32, at)
                 nc.scalar.activation(tanh_y[u, b][:], y_bank[u, b][:].rearrange("p t m -> p m t"), ACT.Tanh)
 
-        def keep_residual(u):
-            for b in range(2):
+        def keep_residual(u, groups=range(2)):
+            for b in groups:
                 if (u, b) in REPEATED:
                     out_bank[u, b] = z_product(u, b, False)
                 else:
@@ -302,7 +304,7 @@ def tile_list_muni_butterfly_residual_kernel(
             for b in range(2):
                 repeated = (u, b) in REPEATED
                 if not repeated:
-                    out_bank[u, b] = bank_tile(2 * (u % LAST) + b, [P, 4, BATCH])
+                    out_bank[u, b] = bank_tile(OUT_BANK[u, b], [P, 4, BATCH])
                 product(
                     out_bank[u, b],
                     b,
@@ -363,28 +365,30 @@ def tile_list_muni_butterfly_residual_kernel(
         second_product(0)
         absolute(0, HALVES[1])
         absolute(1, HALVES[1])
-        second_product(1)
-        keep_residual(0)
-        quantise_act(0)
-        third_product(0)
         z_bf = round_z(0, HALVES[1])
         z_third = round_z(1, batch(2))
         quantise_z(0, HALVES[1], z_bf)
         quantise_z(1, batch(2), z_third)
+        second_product(1)
+        keep_residual(0)
         second_product(2)
-        finish(0, [0])
+        quantise_act(0)
+        third_product(0)
+        quantise_z(1, batch(3), round_z(1, batch(3)))
         keep_residual(1)
+        second_product(3)
+        finish(0, [0])
         quantise_act(1)
         third_product(1)
-        quantise_z(1, batch(3), round_z(1, batch(3)))
-        second_product(3)
         finish(0, [1])
-        finish(1, [0])
-        for u in range(2, BATCHES):
-            keep_residual(u)
-            quantise_act(u)
-            third_product(u)
-            finish(u - 1, [1])
-            if u < LAST:
-                finish(u, [0])
+        keep_residual(2, [0])
+        quantise_act(2)
+        third_product(2)
+        finish(1)
+        keep_residual(2, [1])
+        finish(2, [0])
+        keep_residual(3)
+        quantise_act(3)
+        third_product(3)
+        finish(2, [1])
         finish(LAST)

@@ -218,12 +218,12 @@ def tile_list_muni_butterfly_residual_kernel(
             a, t = divmod(i, 4)
             nc.vector.tensor_tensor(wings[a][:, t, trades], picked(i, LONG, trades), short[a][:, t, trades], ALU.add)
 
-        def bellies(a, trades):
-            for t in range(4):
+        def bellies(a, trades, rows=range(4)):
+            for t in rows:
                 nc.scalar.activation(belly[a][:, t, trades], picked(4 * a + t, BELLY, trades), ACT.Copy)
 
-        def absolute(a, trades):
-            nc.scalar.activation(belly_abs[a][:, :, trades], belly[a][:, :, trades], ACT.Abs, scale=2.0)
+        def absolute(a, trades, rows=slice(0, 4)):
+            nc.scalar.activation(belly_abs[a][:, rows, trades], belly[a][:, rows, trades], ACT.Abs, scale=2.0)
 
         def z_words(a, trades):
             half, first = divmod(trades.start, M // 2)
@@ -343,27 +343,26 @@ def tile_list_muni_butterfly_residual_kernel(
         long_leg(1)
         parts = [(a, b) for a in range(2) for b in range(2)]
         for n in range(3):
-            trades = ALL if n < 2 else HALVES[0]
             round_w2(*parts[n])
-            long_leg(2 + 2 * n, trades)
+            long_leg(2 + 2 * n)
             quantise_w2(*parts[n])
-            long_leg(3 + 2 * n, trades)
+            long_leg(3 + 2 * n)
         bellies(0, ALL)
         absolute(0, HALVES[0])
-        round_w2(1, 1)
         z_bf = round_z(0, HALVES[0])
-        quantise_w2(1, 1)
+        round_w2(1, 1)
         quantise_z(0, HALVES[0], z_bf)
-        bellies(1, HALVES[0])
-        absolute(1, HALVES[0])
+        bellies(1, ALL, (0, 1))
+        bellies(1, HALVES[0], (2, 3))
+        absolute(1, HALVES[0], slice(0, 2))
+        absolute(1, HALVES[0], slice(2, 4))
         z_first = [round_z(1, batch(u)) for u in range(2)]
         for u in range(2):
             quantise_z(1, batch(u), z_first[u])
-        long_leg(6, HALVES[1])
-        long_leg(7, HALVES[1])
-        bellies(1, HALVES[1])
-        second_product(0)
+        quantise_w2(1, 1)
         absolute(0, HALVES[1])
+        bellies(1, HALVES[1], (2, 3))
+        second_product(0)
         absolute(1, HALVES[1])
         z_bf = round_z(0, HALVES[1])
         z_third = round_z(1, batch(2))

@@ -32,6 +32,8 @@ REPEATED = [(u, 0) for u in range(3)]
 
 OUT_BANK = {(0, 1): 1, (1, 1): 3, (2, 1): 1, (3, 0): 0, (3, 1): 3}
 
+ABS_PLACE = {(0, 0): 0, (1, 0): 1, (0, 1): 2, (1, 1): 2}
+
 KIB = 1024
 TABLE_AT = (6 * KIB, 33 * KIB)
 W3_CODES_AT = 0
@@ -163,7 +165,7 @@ def tile_list_muni_butterfly_residual_kernel(
         wings = [kept("wings%d" % a, [P, 4, M], F32) for a in range(2)]
         short = [kept("short%d" % a, [P, 4, M], F32) for a in range(2)]
         belly = [kept("belly%d" % a, [P, 4, M], F32) for a in range(2)]
-        belly_abs = [kept("belly_abs%d" % a, [P, 4, M], F32) for a in range(2)]
+        belly_abs = {}
         w2_bf = {}
         y_bank, y_sb, tanh_y, act_codes, act_sc, out_bank = {}, {}, {}, {}, {}, {}
 
@@ -175,11 +177,16 @@ def tile_list_muni_butterfly_residual_kernel(
                     w3_raw[a][:, cols].rearrange("p (g m t) -> p g t m", t=4, m=4),
                 )
 
-        def first_product(tiles):
-            for half in range(2):
+        def first_bank(i, half):
+            if i < 4:
+                return 2 * i + half
+            return 2 * (i - 4) if half == 1 else (2 * (i - 3) + 1) % BANKS
+
+        def first_product(tiles, halves=range(2)):
+            for half in halves:
                 for i in tiles:
                     quotes = slice(BANK * half, BANK * (half + 1))
-                    bank = bank_tile((2 * i + half) % BANKS, [P, BANK])
+                    bank = bank_tile(first_bank(i, half), [P, BANK])
                     for a in range(2):
                         nc.tensor.matmul_mx(
                             out=bank[:],
@@ -197,8 +204,8 @@ def tile_list_muni_butterfly_residual_kernel(
 
         def round_w2(a, b):
             w2_bf[a, b] = ring.tile([P, 4 * PASS], BF16, name="w2_bf", align_bytes=64)
-            dst = w2_bf[a, b][:].rearrange("p (t m j) -> p m j t", t=4, j=4)
-            src = w2_raw[a, b][:].rearrange("p j (m t) -> p m j t", t=4)
+            dst = w2_bf[a, b][:].rearrange("p (s t m j) -> p s m j t", s=2, t=2, j=4)
+            src = w2_raw[a, b][:].rearrange("p j (m s t) -> p s m j t", s=2, t=2)
             nc.vector.tensor_copy(dst, src)
 
         def quantise_w2(a, b):
@@ -222,8 +229,11 @@ def tile_list_muni_butterfly_residual_kernel(
             for t in rows:
                 nc.scalar.activation(belly[a][:, t, trades], picked(4 * a + t, BELLY, trades), ACT.Copy)
 
-        def absolute(a, trades, rows=slice(0, 4)):
-            nc.scalar.activation(belly_abs[a][:, rows, trades], belly[a][:, rows, trades], ACT.Abs, scale=2.0)
+        def absolute(a, half, rows=slice(0, 4)):
+            if (a, half) not in belly_abs:
+                tag = "belly_abs%d" % ABS_PLACE[a, half]
+                belly_abs[a, half] = kept(tag, [P, 4, M // 2], F32)
+            nc.scalar.activation(belly_abs[a, half][:, rows], belly[a][:, rows, HALVES[half]], ACT.Abs, scale=2.0)
 
         def z_words(a, trades):
             half, first = divmod(trades.start, M // 2)
@@ -241,10 +251,11 @@ def tile_list_muni_butterfly_residual_kernel(
 
         def round_z(a, trades):
             count = trades.stop - trades.start
+            half, first = divmod(trades.start, M // 2)
             z_bf = ring.tile([P, count, 4], BF16, name="z_bf", bufs=3, align_bytes=64)
             nc.vector.tensor_tensor(
                 z_bf[:].rearrange("p (g m) t -> p g t m", m=2),
-                belly_abs[a][:, :, trades].rearrange("p t (g m) -> p g t m", m=2),
+                belly_abs[a, half][:, :, first : first + count].rearrange("p t (g m) -> p g t m", m=2),
                 wings[a][:, :, trades].rearrange("p t (g m) -> p g t m", m=2),
                 ALU.subtract,
             )
@@ -333,46 +344,53 @@ def tile_list_muni_butterfly_residual_kernel(
         first_product(range(4))
         for i in range(4):
             short_leg(i)
-        first_product((4, 5))
+        first_product(range(4, 8), [1])
+        first_product([7], [0])
+        first_product((4, 5), [0])
         short_leg(4)
         short_leg(5)
-        first_product((6, 7))
+        first_product([6], [0])
         short_leg(6)
         short_leg(7)
         long_leg(0)
         long_leg(1)
         parts = [(a, b) for a in range(2) for b in range(2)]
-        for n in range(3):
+        for n in range(2):
             round_w2(*parts[n])
             long_leg(2 + 2 * n)
             quantise_w2(*parts[n])
             long_leg(3 + 2 * n)
+        round_w2(1, 0)
+        long_leg(6)
+        long_leg(7)
         bellies(0, ALL)
-        absolute(0, HALVES[0])
+        absolute(0, 0)
         z_bf = round_z(0, HALVES[0])
-        round_w2(1, 1)
+        quantise_w2(1, 0)
         quantise_z(0, HALVES[0], z_bf)
+        round_w2(1, 1)
         bellies(1, ALL, (0, 1))
         bellies(1, HALVES[0], (2, 3))
-        absolute(1, HALVES[0], slice(0, 2))
-        absolute(1, HALVES[0], slice(2, 4))
-        z_first = [round_z(1, batch(u)) for u in range(2)]
-        for u in range(2):
-            quantise_z(1, batch(u), z_first[u])
+        absolute(1, 0, slice(0, 2))
+        absolute(1, 0, slice(2, 4))
+        z_bf = round_z(1, batch(0))
         quantise_w2(1, 1)
-        absolute(0, HALVES[1])
+        quantise_z(1, batch(0), z_bf)
+        absolute(0, 1)
         bellies(1, HALVES[1], (2, 3))
-        second_product(0)
-        absolute(1, HALVES[1])
+        z_second = round_z(1, batch(1))
         z_bf = round_z(0, HALVES[1])
-        z_third = round_z(1, batch(2))
+        quantise_z(1, batch(1), z_second)
         quantise_z(0, HALVES[1], z_bf)
-        quantise_z(1, batch(2), z_third)
-        second_product(1)
-        keep_residual(0)
-        second_product(2)
+        second_product(0)
+        absolute(1, 1)
+        keep_residual(0, [0])
         quantise_act(0)
+        quantise_z(1, batch(2), round_z(1, batch(2)))
+        second_product(1)
+        keep_residual(0, [1])
         third_product(0)
+        second_product(2)
         quantise_z(1, batch(3), round_z(1, batch(3)))
         keep_residual(1)
         second_product(3)

@@ -180,7 +180,7 @@ def tile_list_muni_butterfly_residual_kernel(
         def first_bank(i, half):
             if i < 4:
                 return 2 * i + half
-            return 2 * (i - 4) if half == 1 else (2 * (i - 3) + 1) % BANKS
+            return 2 * (i - 4) if half == 1 else 2 * (7 - i) + 1
 
         def first_product(tiles, halves=range(2)):
             for half in halves:
@@ -197,7 +197,7 @@ def tile_list_muni_butterfly_residual_kernel(
                             start=(a == 0),
                             stop=(a == 1),
                         )
-                    if half == 0 and i < 7:
+                    if half == 0 and i < 5:
                         nc.scalar.activation(h_sb[i][:, quotes], bank[:], ACT.Copy, scale=0.5)
                     else:
                         nc.vector.tensor_scalar(h_sb[i][:, quotes], bank[:], 0.5, None, ALU.mult)
@@ -345,13 +345,9 @@ def tile_list_muni_butterfly_residual_kernel(
         for i in range(4):
             short_leg(i)
         first_product(range(4, 8), [1])
-        first_product([7], [0])
-        first_product((4, 5), [0])
-        short_leg(4)
-        short_leg(5)
-        first_product([6], [0])
-        short_leg(6)
-        short_leg(7)
+        first_product((7, 6, 5, 4), [0])
+        for i in range(4, 8):
+            short_leg(i)
         long_leg(0)
         long_leg(1)
         parts = [(a, b) for a in range(2) for b in range(2)]

@@ -180,7 +180,7 @@ def tile_list_muni_butterfly_residual_kernel(
         def first_bank(i, half):
             if i < 4:
                 return 2 * i + half
-            return 2 * (i - 4) if half == 1 else 2 * (7 - i) + 1
+            return 2 * (i - 4) if half == 1 else {7: 1, 6: 3, 4: 5, 5: 7}[i]
 
         def first_product(tiles, halves=range(2)):
             for half in halves:
@@ -197,7 +197,7 @@ def tile_list_muni_butterfly_residual_kernel(
                             start=(a == 0),
                             stop=(a == 1),
                         )
-                    if half == 0 and i < 5:
+                    if half == 0 and i < 6:
                         nc.scalar.activation(h_sb[i][:, quotes], bank[:], ACT.Copy, scale=0.5)
                     else:
                         nc.vector.tensor_scalar(h_sb[i][:, quotes], bank[:], 0.5, None, ALU.mult)
@@ -345,7 +345,7 @@ def tile_list_muni_butterfly_residual_kernel(
         for i in range(4):
             short_leg(i)
         first_product(range(4, 8), [1])
-        first_product((7, 6, 5, 4), [0])
+        first_product((7, 6, 4, 5), [0])
         for i in range(4, 8):
             short_leg(i)
         long_leg(0)

@@ -345,7 +345,9 @@ def tile_list_muni_butterfly_residual_kernel(
         for i in range(4):
             short_leg(i)
         first_product(range(4, 8), [1])
-        first_product((7, 6, 4, 5), [0])
+        first_product((7, 6), [0])
+        bellies(0, ALL, (0, 1))
+        first_product((4, 5), [0])
         for i in range(4, 8):
             short_leg(i)
         long_leg(0)
@@ -359,7 +361,7 @@ def tile_list_muni_butterfly_residual_kernel(
         round_w2(1, 0)
         long_leg(6)
         long_leg(7)
-        bellies(0, ALL)
+        bellies(0, ALL, (2, 3))
         absolute(0, 0)
         z_bf = round_z(0, HALVES[0])
         quantise_w2(1, 0)

from contextlib import ExitStack

import concourse.mybir as mybir

K, T, S, M, H, N = 1024, 4096, 1024, 512, 1024, 1024
FLOPS = 2 * K * H * S + 2 * H * N * M + 2 * N * N * M

F32 = mybir.dt.float32
BF16 = mybir.dt.bfloat16
I32 = mybir.dt.int32
U32 = mybir.dt.uint32
U16 = mybir.dt.uint16
U8 = mybir.dt.uint8
FP8X4 = mybir.dt.float8_e4m3fn_x4
FP4X4 = mybir.dt.float4_e2m1fn_x4
ALU = mybir.AluOpType
ACT = mybir.ActivationFunctionType

P = 128
PASS = 512
BANK = 512
BANKS = 8
BATCH = 128
BATCHES = M // BATCH
LAST = BATCHES - 1
ALL = slice(0, M)
HALVES = (slice(0, M // 2), slice(M // 2, M))
ROWS_AT = 96
PER_COLUMN = 16
BELLY, SHORT, LONG = range(3)
REPEATED = [(u, 0) for u in range(3)]

OUT_BANK = {(0, 1): 1, (1, 1): 3, (2, 1): 1, (3, 0): 0, (3, 1): 3}

ABS_PLACE = {(0, 0): 0, (1, 0): 1, (0, 1): 2, (1, 1): 2}

KIB = 1024
TABLE_AT = (6 * KIB, 33 * KIB)
W3_CODES_AT = 0
W1_SECOND_AT = 6 * KIB
W3_SCALES_AT = 8 * KIB
GAIN_AT = 9 * KIB
W3_AT = 10 * KIB
W2_AT = {(0, 0): 18 * KIB, (0, 1): 26 * KIB, (1, 0): 34 * KIB, (1, 1): 42 * KIB}
V_SC_AT = 34 * KIB
OPERANDS_AT = 50 * KIB
RESULT_AT = 10 * KIB
Y_AT = 50 * KIB
TANH_AT = 34 * KIB
TANH_PLACES = 8


def tile_list_muni_butterfly_residual_kernel(
    tc, tab_words, tab_scales, offs, pos1, pos2, pos3, w1_words, w1_scales, w2, w3_words, w3_scales, gain, out
):
    nc = tc.nc
    with ExitStack() as ctx:
        keep = ctx.enter_context(tc.tile_pool(name="keep", bufs=1))
        placed = ctx.enter_context(tc.tile_pool(name="placed", bufs=1))
        ring = ctx.enter_context(tc.tile_pool(name="ring", bufs=2))
        psum = ctx.enter_context(tc.psum_pool(name="psum", bufs=1))

        def kept(tag, shape, dtype):
            return keep.tile(shape, dtype, name=tag, align_bytes=64)

        def place(name, shape, dtype, offset):
            return placed.tile(shape, dtype, name=name, offset=offset, align_bytes=64)

        def bank_tile(number, shape):
            return psum.tile(shape, F32, name="bank%d" % number)

        offs_sb = kept("offs_sb", [P, S // PER_COLUMN], U16)
        pos_sb = [kept("pos_sb%d" % leg, [P, M // PER_COLUMN], U16) for leg in range(3)]

        tab_sc = kept("tab_sc", [P, T], U8)
        w_sc_raw = kept("w_sc_raw", [P, 2, N], U8)
        first_sc = [kept("first_sc%d" % a, [P, 2, S], U8) for a in range(2)]
        nc.vector.memset(tab_sc[0:ROWS_AT].bitcast(I32), 0)
        nc.vector.memset(w_sc_raw[0:ROWS_AT].bitcast(I32), 0)
        nc.vector.memset(first_sc[0][:].bitcast(I32), 0)

        table = [tab_words[a].rearrange("p t i -> p (t i)").bitcast(I32) for a in range(2)]
        tab_first = place("tab_first", [P, T], I32, TABLE_AT[0])
        nc.sync.dma_start(tab_sc[ROWS_AT:P].bitcast(I32), tab_scales.rearrange("a q t -> (a q) t").bitcast(I32))
        nc.sync.dma_start(offs_sb[:], offs)
        nc.sync.dma_start(w_sc_raw[ROWS_AT:P, 0].bitcast(I32), w1_scales.rearrange("a q c -> (a q) c").bitcast(I32))
        w1_groups = w1_words.rearrange("a p (b c) -> b p a c", b=2)
        w1_raw = {0: kept("w1_first", [P, 2, H // 4], I32)}
        nc.sync.dma_start(w1_raw[0][:], w1_groups[0].bitcast(I32))
        nc.sync.dma_start(tab_first[:], table[0])
        nc.sync.dma_start(w_sc_raw[ROWS_AT:P, 1].bitcast(I32), w3_scales.rearrange("a q c -> (a q) c").bitcast(I32))
        for leg, positions in enumerate((pos1, pos2, pos3)):
            nc.sync.dma_start(pos_sb[leg][:], positions)

        v_sc = place("v_sc", [P, S], U8, V_SC_AT)
        nc.vector.tensor_copy(v_sc[:], tab_sc[:].indirect(offs_sb[:]))
        nc.vector.tensor_copy(first_sc[1][:, 0].bitcast(I32), v_sc[:].bitcast(I32))
        nc.vector.tensor_copy(
            first_sc[1][:, 1].bitcast(I32).rearrange("p (b t g w) -> p b g t w", b=2, t=4, w=2),
            w_sc_raw[:, 0].bitcast(I32).rearrange("p (b g t w) -> p b g t w", b=2, t=4, w=2),
        )

        tab_second = place("tab_second", [P, T], I32, TABLE_AT[1])
        for a in range(2):
            words = slice(T // 2 * a, T // 2 * (a + 1))
            nc.sync.dma_start(tab_second[:, words], table[1][:, words])
            for q in range(4):
                row = ROWS_AT + 16 * a + 4 * q
                nc.sync.dma_start(
                    first_sc[a][32 * q : 32 * q + 4].bitcast(I32), first_sc[1][row : row + 4].bitcast(I32)
                )

        w1_codes = [place("w1_codes%d" % b, [P, 2, H // 4], I32, OPERANDS_AT + (8 + 2 * b) * KIB) for b in range(2)]

        def order_w1(b):
            nc.vector.tensor_copy(
                w1_codes[b][:].rearrange("p a (t g w) -> p a t g w", t=4, w=4),
                w1_raw[b][:].rearrange("p a (g t w) -> p a t g w", t=4, w=4),
            )

        order_w1(0)

        v_first = place("v_first", [P, S], U32, OPERANDS_AT)
        nc.vector.tensor_copy(v_first[:], tab_first[:].bitcast(U32).indirect(offs_sb[:]))
        v_codes = {(0, half): v_first[:, BANK * half : BANK * (half + 1)] for half in range(2)}
        for half in range(2):
            v_second = place("v_second%d" % half, [P, BANK], U32, OPERANDS_AT + 4 * (S + BANK * half))
            v_codes[1, half] = v_second[:]
            entries = offs_sb[:, BANK // PER_COLUMN * half : BANK // PER_COLUMN * (half + 1)]
            nc.vector.tensor_copy(v_second[:], tab_second[:].bitcast(U32).indirect(entries))

        w1_raw[1] = place("w1_second", [P, 2, H // 4], I32, W1_SECOND_AT)
        nc.sync.dma_start(w1_raw[1][:], w1_groups[1].bitcast(I32))
        order_w1(1)
        w3_raw = [place("w3_raw%d" % a, [P, N], I32, W3_AT + 4 * KIB * a) for a in range(2)]
        for a in range(2):
            nc.sync.dma_start(w3_raw[a][:], w3_words[a].rearrange("p c i -> p (c i)").bitcast(I32))
        w2_raw = {}
        for a in range(2):
            for b in range(2):
                w2_raw[a, b] = place("w2_raw%d%d" % (a, b), [P, 4, PASS], F32, W2_AT[a, b])
                w2_rows = w2[PASS * a : PASS * (a + 1), PASS * b : PASS * (b + 1)]
                w2_rows = w2_rows.rearrange("(g t i) n -> t g i n", t=4, i=8)
                for t in range(4):
                    nc.sync.dma_start(w2_raw[a, b][:, t, :], w2_rows[t])
        gain_sb = place("gain_sb", [P, 2, 4], F32, GAIN_AT)
        nc.sync.dma_start(gain_sb[:], gain.rearrange("(b p t) -> p b t", b=2, t=4))

        w3_sc = place("w3_sc", [P, N], U8, W3_SCALES_AT)
        nc.vector.tensor_copy(
            w3_sc[:].rearrange("p (b t g m) -> p b g t m", b=2, t=4, m=16),
            w_sc_raw[:, 1].rearrange("p (b g m t) -> p b g t m", b=2, t=4, m=16),
        )
        for q in range(4):
            for a in range(2):
                row, to = ROWS_AT + 16 * a + 4 * q, 32 * q + 4 * a
                nc.sync.dma_start(w3_sc[to : to + 4].bitcast(I32), w3_sc[row : row + 4].bitcast(I32))

        w3_codes = place("w3_codes", [P, 2, N], I32, W3_CODES_AT)
        h_sb = [kept("h_sb%d" % i, [P, S], F32) for i in range(8)]
        w2_codes = [kept("w2_codes%d" % a, [P, N], U32) for a in range(2)]
        w2_sc = [kept("w2_sc%d" % a, [P, N], U8) for a in range(2)]
        z_codes = {(a, half): kept("z_codes%d%d" % (a, half), [P, M // 2], U32) for a in range(2) for half in range(2)}
        z_sc = [kept("z_sc%d" % a, [P, M], U8) for a in range(2)]
        wings = [kept("wings%d" % a, [P, 4, M], F32) for a in range(2)]
        short = [kept("short%d" % a, [P, 4, M], F32) for a in range(2)]
        belly = [kept("belly%d" % a, [P, 4, M], F32) for a in range(2)]
        belly_abs = {}
        w2_bf = {}
        y_bank, y_sb, tanh_y, act_codes, act_sc, out_bank = {}, {}, {}, {}, {}, {}

        def order_w3(a):
            for b in range(2):
                cols = slice(PASS * b, PASS * (b + 1))
                nc.gpsimd.tensor_copy(
                    w3_codes[:, a, cols].rearrange("p (t g m) -> p g t m", t=4, m=4),
                    w3_raw[a][:, cols].rearrange("p (g m t) -> p g t m", t=4, m=4),
                )

        def first_bank(i, half):
            if i < 4:
                return 2 * i + half
            return 2 * (i - 4) if half == 1 else {7: 1, 6: 3, 4: 5, 5: 7}[i]

        def first_product(tiles, halves=range(2)):
            for half in halves:
                for i in tiles:
                    quotes = slice(BANK * half, BANK * (half + 1))
                    bank = bank_tile(first_bank(i, half), [P, BANK])
                    for a in range(2):
                        nc.tensor.matmul_mx(
                            out=bank[:],
                            lhsT=w1_codes[i // 4][:, a, 64 * (i % 4) : 64 * (i % 4 + 1)].bitcast(U8).bitcast(FP4X4),
                            lhsT_scale=first_sc[a][:, 1, P * i : P * (i + 1)],
                            rhs=v_codes[a, half].bitcast(FP8X4),
                            rhs_scale=first_sc[a][:, 0, quotes],
                            start=(a == 0),
                            stop=(a == 1),
                        )
                    if half == 0 and i < 6:
                        nc.scalar.activation(h_sb[i][:, quotes], bank[:], ACT.Copy, scale=0.5)
                    else:
                        nc.vector.tensor_scalar(h_sb[i][:, quotes], bank[:], 0.5, None, ALU.mult)

        def round_w2(a, b):
            w2_bf[a, b] = ring.tile([P, 4 * PASS], BF16, name="w2_bf", align_bytes=64)
            dst = w2_bf[a, b][:].rearrange("p (s t m j) -> p s m j t", s=2, t=2, j=4)
            src = w2_raw[a, b][:].rearrange("p j (m s t) -> p s m j t", s=2, t=2)
            nc.vector.tensor_copy(dst, src)

        def quantise_w2(a, b):
            cols = slice(PASS * b, PASS * (b + 1))
            nc.vector.quantize_mx(
                out=w2_codes[a][:, cols].bitcast(FP8X4), scales=w2_sc[a][:, cols], in_=w2_bf[a, b][:]
            )

        def picked(i, leg, trades):
            entries = pos_sb[leg][:, trades.start // PER_COLUMN : trades.stop // PER_COLUMN]
            return h_sb[i][:].indirect(entries)

        def short_leg(i):
            nc.scalar.activation(short[i // 4][:, i % 4, :], picked(i, SHORT, ALL), ACT.Copy)

        def long_leg(i, trades=ALL):
            a, t = divmod(i, 4)
            nc.vector.tensor_tensor(wings[a][:, t, trades], picked(i, LONG, trades), short[a][:, t, trades], ALU.add)

        def bellies(a, trades, rows=range(4)):
            for t in rows:
                nc.scalar.activation(belly[a][:, t, trades], picked(4 * a + t, BELLY, trades), ACT.Copy)

        def absolute(a, half, rows=slice(0, 4)):
            if (a, half) not in belly_abs:
                tag = "belly_abs%d" % ABS_PLACE[a, half]
                belly_abs[a, half] = kept(tag, [P, 4, M // 2], F32)
            nc.scalar.activation(belly_abs[a, half][:, rows], belly[a][:, rows, HALVES[half]], ACT.Abs, scale=2.0)

        def z_words(a, trades):
            half, first = divmod(trades.start, M // 2)
            return z_codes[a, half][:, first : first + trades.stop - trades.start]

        def quantise_z(a, trades, z_bf):
            nc.vector.quantize_mx(
                out=z_words(a, trades).bitcast(FP8X4),
                scales=z_sc[a][:, trades],
                in_=z_bf[:].rearrange("p m t -> p (m t)"),
            )

        def batch(u):
            return slice(BATCH * u, BATCH * (u + 1))

        def round_z(a, trades):
            count = trades.stop - trades.start
            half, first = divmod(trades.start, M // 2)
            z_bf = ring.tile([P, count, 4], BF16, name="z_bf", bufs=3, align_bytes=64)
            nc.vector.tensor_tensor(
                z_bf[:].rearrange("p (g m) t -> p g t m", m=2),
                belly_abs[a, half][:, :, first : first + count].rearrange("p t (g m) -> p g t m", m=2),
                wings[a][:, :, trades].rearrange("p t (g m) -> p g t m", m=2),
                ALU.subtract,
            )
            return z_bf

        def product(bank, b, w_codes, w_sc, x_codes, x_sc, start, stop, passes):
            for a in passes:
                for t in range(4):
                    cols = slice(PASS * b + P * t, PASS * b + P * (t + 1))
                    nc.tensor.matmul_mx(
                        out=bank[:, t, :],
                        lhsT=w_codes[a][:, cols].bitcast(FP8X4),
                        lhsT_scale=w_sc[a][:, cols],
                        rhs=x_codes[a].bitcast(FP8X4),
                        rhs_scale=x_sc[a],
                        start=(start and a == passes[0] and t == 0),
                        stop=(stop and a == passes[1] and t == 3),
                    )

        def z_product(u, b, stop):
            bank = bank_tile(2 * u + b, [P, 4, BATCH])
            x_codes = [z_words(a, batch(u)) for a in range(2)]
            product(bank, b, w2_codes, w2_sc, x_codes, [z_sc[a][:, batch(u)] for a in range(2)], True, stop, (0, 1))
            return bank

        def second_product(u):
            for b in range(2):
                y_bank[u, b] = z_product(u, b, True)
                at = TANH_AT + 2 * KIB * ((2 * u + b) % TANH_PLACES)
                tanh_y[u, b] = place("tanh_y%d%d" % (u, b), [P, BATCH, 4], F32, at)
                nc.scalar.activation(tanh_y[u, b][:], y_bank[u, b][:].rearrange("p t m -> p m t"), ACT.Tanh)

        def keep_residual(u, groups=range(2)):
            for b in groups:
                if (u, b) in REPEATED:
                    out_bank[u, b] = z_product(u, b, False)
                else:
                    y_sb[u, b] = place("y_sb%d%d" % (u, b), [P, 4, BATCH], F32, Y_AT + 2 * KIB * len(y_sb))
                    nc.scalar.copy(y_sb[u, b][:], y_bank[u, b][:])

        def quantise_act(u):
            act_bf = [ring.tile([P, BATCH, 4], BF16, name="act_bf", bufs=4, align_bytes=64) for b in range(2)]
            for b in range(2):
                nc.vector.tensor_tensor(
                    act_bf[b][:], tanh_y[u, b][:], gain_sb[:, b, :].unsqueeze(1).to_broadcast([P, BATCH, 4]), ALU.mult
                )
            for b in range(2):
                act_codes[u, b] = ring.tile([P, BATCH], U32, name="act_codes", bufs=4, align_bytes=64)
                act_sc[u, b] = ring.tile([P, BATCH], U8, name="act_sc", bufs=4, align_bytes=64)
                nc.vector.quantize_mx(
                    out=act_codes[u, b][:].bitcast(FP8X4),
                    scales=act_sc[u, b][:],
                    in_=act_bf[b][:].rearrange("p m t -> p (m t)"),
                )

        def third_product(u):
            for b in range(2):
                repeated = (u, b) in REPEATED
                if not repeated:
                    out_bank[u, b] = bank_tile(OUT_BANK[u, b], [P, 4, BATCH])
                product(
                    out_bank[u, b],
                    b,
                    [w3_codes[:, a] for a in range(2)],
                    [w3_sc[4 * a : P] for a in range(2)],
                    [act_codes[u, a][:] for a in range(2)],
                    [act_sc[u, a][:] for a in range(2)],
                    not repeated,
                    True,
                    (0, 1),
                )

        def finish(u, groups=range(2)):
            for b in groups:
                result = place("result%d%d" % (u, b), [P, 4, BATCH], F32, RESULT_AT + 2 * KIB * (2 * u + b))
                if (u, b) in REPEATED:
                    nc.scalar.copy(result[:], out_bank[u, b][:])
                else:
                    nc.vector.tensor_tensor(result[:], out_bank[u, b][:], y_sb[u, b][:], ALU.add)
                rows = out[PASS * b : PASS * (b + 1), batch(u)]
                queue = nc.scalar if (u, b) == (LAST, 1) else nc.sync
                queue.dma_start(rows.rearrange("(p t) m -> p t m", t=4), result[:])

        order_w3(0)
        order_w3(1)
        first_product(range(4))
        for i in range(4):
            short_leg(i)
        first_product(range(4, 8), [1])
        first_product((7, 6), [0])
        bellies(0, ALL, (0, 1))
        first_product((4, 5), [0])
        for i in range(4, 8):
            short_leg(i)
        long_leg(0)
        long_leg(1)
        parts = [(a, b) for a in range(2) for b in range(2)]
        for n in range(2):
            round_w2(*parts[n])
            long_leg(2 + 2 * n)
            quantise_w2(*parts[n])
            long_leg(3 + 2 * n)
        round_w2(1, 0)
        long_leg(6)
        long_leg(7)
        bellies(0, ALL, (2, 3))
        absolute(0, 0)
        z_bf = round_z(0, HALVES[0])
        quantise_w2(1, 0)
        quantise_z(0, HALVES[0], z_bf)
        round_w2(1, 1)
        bellies(1, ALL, (0, 1))
        bellies(1, HALVES[0], (2, 3))
        absolute(1, 0, slice(0, 2))
        absolute(1, 0, slice(2, 4))
        z_bf = round_z(1, batch(0))
        quantise_w2(1, 1)
        quantise_z(1, batch(0), z_bf)
        absolute(0, 1)
        bellies(1, HALVES[1], (2, 3))
        z_second = round_z(1, batch(1))
        z_bf = round_z(0, HALVES[1])
        quantise_z(1, batch(1), z_second)
        quantise_z(0, HALVES[1], z_bf)
        second_product(0)
        absolute(1, 1)
        keep_residual(0, [0])
        quantise_act(0)
        quantise_z(1, batch(2), round_z(1, batch(2)))
        second_product(1)
        keep_residual(0, [1])
        third_product(0)
        second_product(2)
        quantise_z(1, batch(3), round_z(1, batch(3)))
        keep_residual(1)
        second_product(3)
        finish(0, [0])
        quantise_act(1)
        third_product(1)
        finish(0, [1])
        keep_residual(2, [0])
        quantise_act(2)
        third_product(2)
        finish(1)
        keep_residual(2, [1])
        finish(2, [0])
        keep_residual(3)
        quantise_act(3)
        third_product(3)
        finish(2, [1])
        finish(LAST)
